import numpy as np
import ml_dtypes


def mxq(x, axis, fmt="e4m3"):
    dtype, down = {"e4m3": (ml_dtypes.float8_e4m3fn, 7), "e5m2": (ml_dtypes.float8_e5m2, 14)}[fmt]
    v = np.moveaxis(np.asarray(x, np.float32).astype(ml_dtypes.bfloat16).astype(np.float64), axis, -1)
    blocks = v.reshape(v.shape[:-1] + (-1, 32))
    amax = np.abs(blocks).max(-1, keepdims=True)
    byte = np.maximum(np.where(amax > 0, np.frexp(amax)[1] - 1 + 127, 0) - down, 1)
    scale = np.exp2(byte - 127.0)
    codes = (blocks / scale).astype(np.float32).astype(dtype).astype(np.float64)
    return np.moveaxis((codes * scale).reshape(v.shape), -1, axis)


WIDE = False


def mx_kscale(k):
    if not WIDE:
        return np.ones(k)
    levels = np.array([18, -18])
    if k % 512:
        return np.exp2(np.random.permutation(np.resize(levels, k // 32))).repeat(32)
    a = np.empty((k // 512, 16))
    for p in range(k // 512):
        a[p, :8] = np.random.permutation(np.resize(levels, 8))
        for g in range(8):
            far = levels[np.abs(levels - a[p, g]) >= 10]
            a[p, g + 8] = far[np.random.randint(len(far))]
    return np.exp2(a.ravel()).repeat(32)


def f64(x):
    return np.asarray(x).astype(np.float64)


def striped(idx):
    return np.tile(np.asarray(idx).reshape(-1, 16).T, (8, 1)).astype(np.uint16)


def unstriped(offs):
    return offs[:16].T.reshape(-1).astype(np.int64)


E2M1 = np.array([0.0, 0.5, 1.0, 1.5, 2.0, 3.0, 4.0, 6.0, -0.0, -0.5, -1.0, -1.5, -2.0, -3.0, -4.0, -6.0])


def pack_weight(w, fmt):
    k, n = w.shape
    w = f64(np.asarray(w, np.float32).astype(ml_dtypes.bfloat16)).reshape(k // 32, 32, n)
    amax = np.abs(w).max(1)
    if fmt == "e4m3":
        byte = np.frexp(amax)[1] - 1 + 127 - 7
    else:
        mant, ex = np.frexp(amax / 6.0)
        byte = np.where(mant > 0.5, ex, ex - 1) + 127
    byte = np.clip(np.where(amax > 0, byte, 1), 1, 254)
    scaled = (w * np.exp2(127.0 - byte)[:, None, :]).reshape(k, n).astype(np.float32)
    by_word = np.ascontiguousarray(scaled.reshape(k // 512, 128, 4, n).transpose(0, 1, 3, 2))
    if fmt == "e4m3":
        words = by_word.astype(ml_dtypes.float8_e4m3fn).view(np.uint8)
    else:
        c = by_word.astype(ml_dtypes.float4_e2m1fn).view(np.uint8) & 0xF
        words = (c[..., 0::2] | (c[..., 1::2] << 4)).reshape(k // 512, 128, 2 * n)
    return np.ascontiguousarray(words), np.ascontiguousarray(byte.astype(np.uint8).reshape(k // 512, 16, n))


def unpack_weight(words, scales, fmt):
    g, _, n = scales.shape
    words = np.ascontiguousarray(words).reshape(g, 128, n, -1)
    if fmt == "e4m3":
        vals = words.view(ml_dtypes.float8_e4m3fn).astype(np.float64)
    else:
        nib = np.empty((g, 128, n, 4), np.uint8)
        nib[..., 0::2] = words & 0xF
        nib[..., 1::2] = words >> 4
        vals = E2M1[nib]
    vals = vals * np.repeat(np.exp2(scales.astype(np.float64) - 127.0), 8, axis=1)[..., None]
    return vals.transpose(0, 1, 3, 2).reshape(g * 512, n)


def planes(y):
    n, m = y.shape
    v = y.astype(np.float32).astype(ml_dtypes.bfloat16).astype(np.float64).reshape(n // 32, 32, m)
    top = np.abs(v).max(1)
    byte = np.clip(np.where(top > 0, np.frexp(top)[1] - 1 + 127 - 7, 1), 1, 254)
    codes = (v * np.exp2(127.0 - byte)[:, None, :]).reshape(n, m).astype(np.float32).astype(ml_dtypes.float8_e4m3fn).view(np.uint8)
    words = codes.reshape(n // 512, 128, 4, m).transpose(0, 1, 3, 2)
    return np.ascontiguousarray(words), np.ascontiguousarray(byte.astype(np.uint8).reshape(n // 512, 16, m))


N, T, D, V = 512, 1024, 512, 1024


def setup_inputs():
    n = np.random.standard_normal
    idx = np.random.permutation(T)[:N]
    s = mx_kscale(D)[:, None]
    z = mx_kscale(V)[:, None]
    w = n((D, V)) / np.sqrt(D)
    wd, wv = pack_weight(w * s, "e2m1"), pack_weight(w.T / z, "e2m1")
    return {
        "xT": (n((D, T)) / s).astype(np.float32),
        "wd_words": wd[0],
        "wd_scales": wd[1],
        "wv_words": wv[0],
        "wv_scales": wv[1],
        "y": (2 * np.random.randint(0, 2, (V, N)) - 1).astype(np.float32),
        "cw": (np.random.uniform(0.5, 1.5, (V, 1)) / np.sqrt(V) * z).astype(np.float32),
        "rw": np.tile(np.random.uniform(0.5, 1.5, N), (128, 1)).astype(np.float32),
        "offs": striped(idx),
    }


def reference(xT, wd_words, wd_scales, wv_words, wv_scales, y, cw, rw, offs):
    idx = unstriped(offs)
    a = unpack_weight(wd_words, wd_scales, "e2m1").T @ mxq(f64(xT)[:, idx], 0, "e4m3")
    g = -f64(cw) * f64(rw)[:1] * f64(y) / (1.0 + np.exp(f64(y) * a))
    dx = unpack_weight(wv_words, wv_scales, "e2m1").T @ mxq(g, 0, "e5m2")
    gx = np.zeros((D, T))
    gx[:, idx] = dx
    out_0 = gx
    return (out_0,) + planes(out_0)

@@ -1,0 +1,221 @@
+from contextlib import ExitStack
+
+import concourse.mybir as mybir
+
+N, T, D, V = 512, 1024, 512, 1024
+FLOPS = 2 * D * V * N * 2
+
+F32 = mybir.dt.float32
+BF16 = mybir.dt.bfloat16
+I32 = mybir.dt.int32
+U32 = mybir.dt.uint32
+U16 = mybir.dt.uint16
+U8 = mybir.dt.uint8
+E4M3 = mybir.dt.float8_e4m3fn_x4
+E5M2 = mybir.dt.float8_e5m2_x4
+E2M1 = mybir.dt.float4_e2m1fn_x4
+MULT = mybir.AluOpType.mult
+ACT = mybir.ActivationFunctionType
+
+P = 128
+LANES = 4
+K_PASS = P * LANES
+V_PASSES = V // K_PASS
+RUN = 4
+
+
+def deal(nc, out, in_):
+    nc.vector.tensor_copy(
+        out=out.rearrange("p (g t m) -> p g t m", t=LANES, m=P),
+        in_=in_.rearrange("p (g m t) -> p g t m", t=LANES, m=P),
+    )
+
+
+def tile_attend_gml_pl_sig_kernel(
+    tc, xT, wd_words, wd_scales, wv_words, wv_scales, y, cw, rw, offs, out_0, out_1, out_2
+):
+    nc = tc.nc
+    with ExitStack() as ctx:
+        sb = ctx.enter_context(tc.tile_pool(name="sb", bufs=1))
+        psum = ctx.enter_context(tc.psum_pool(name="psum", bufs=1))
+
+        offsets = sb.tile([P, N // 16], U16, name="offsets")
+        nc.sync.dma_start(offsets[:], offs)
+
+        wd_scale_raw = sb.tile([P, V], U8, name="wd_scale_raw")
+        wv_scale_raw = sb.tile([P, V_PASSES * D], U8, name="wv_scale_raw")
+        nc.gpsimd.memset(wd_scale_raw[:].bitcast(U32), 0)
+        nc.gpsimd.memset(wv_scale_raw[:].bitcast(U32), 0)
+
+        wd_raw = sb.tile([P, V], U16, name="wd_raw")
+        nc.sync.dma_start(out=wd_raw[:].bitcast(I32), in_=wd_words[0].bitcast(I32))
+        for q in range(4):
+            nc.sync.dma_start(
+                out=wd_scale_raw[32 * q : 32 * q + 4, :].bitcast(I32),
+                in_=wd_scales[0, 4 * q : 4 * q + 4, :].bitcast(I32),
+            )
+        cw_sb = sb.tile([P, V_PASSES, LANES], F32, name="cw_sb")
+        nc.scalar.dma_start(out=cw_sb[:], in_=cw.rearrange("(o p r) one -> p o (r one)", p=P, r=LANES))
+        warm = sb.tile([P, V_PASSES, LANES], F32, name="warm")
+        nc.scalar.activation(warm[:], cw_sb[:], ACT.Sigmoid)
+        rw_sb = sb.tile([P, N], F32, name="rw_sb")
+        nc.sync.dma_start(out=rw_sb[:], in_=rw)
+
+        x_rows = xT.rearrange("(p t) c -> p t c", t=LANES)
+        x_planes = []
+        for t in range(LANES):
+            plane = sb.tile([P, T], F32, name=f"x_plane{t}")
+            nc.sync.dma_start(out=plane[:], in_=x_rows[:, t, :])
+            x_planes.append(plane)
+
+        y_rows = y.rearrange("(o p r) i -> o p r i", p=P, r=LANES)
+        y_tiles = {}
+        for o in range(V_PASSES):
+            for h in range(2):
+                pair = sb.tile([P, 2, N], F32, name=f"y{o}{h}")
+                nc.sync.dma_start(out=pair[:], in_=y_rows[o, :, 2 * h : 2 * h + 2, :])
+                for e in range(2):
+                    y_tiles[o, 2 * h + e] = pair[:, e, :]
+
+        wv_raw = sb.tile([P, V_PASSES, D], U16, name="wv_raw")
+        nc.sync.dma_start(out=wv_raw[:].bitcast(I32), in_=wv_words.bitcast(I32).rearrange("o p w -> p o w"))
+        for q in range(4):
+            nc.sync.dma_start(
+                out=wv_scale_raw[32 * q : 32 * q + 4, :].bitcast(I32).rearrange("f (o w) -> f o w", o=V_PASSES),
+                in_=wv_scales[:, 4 * q : 4 * q + 4, :].bitcast(I32).rearrange("o f w -> f o w"),
+            )
+
+        windows = []
+        for j in range(LANES):
+            window = sb.tile([P, T], F32, name=f"window{j}")
+            nc.vector.memset(window[:], 0.0)
+            windows.append(window)
+
+        wd_dealt = sb.tile([P, V], U16, name="wd_dealt", align_bytes=64)
+        wd_scale = sb.tile([P, V], U8, name="wd_scale", align_bytes=64)
+        deal(nc, wd_dealt[:], wd_raw[:])
+        deal(nc, wd_scale[:], wd_scale_raw[:])
+        neg_cw = sb.tile([P, V_PASSES, LANES], F32, name="neg_cw")
+        nc.vector.tensor_scalar_mul(neg_cw[:], cw_sb[:], -1.0)
+
+        x_woven = sb.tile([P, N, LANES], BF16, name="x_woven", align_bytes=64)
+        for h in range(2):
+            gathered = sb.tile([P, 2, N], BF16, name=f"gathered{h}")
+            for e in range(2):
+                nc.vector.tensor_copy(gathered[:, e, :], x_planes[2 * h + e][:].indirect(offsets[:]))
+            nc.scalar.copy(x_woven[:, :, 2 * h : 2 * h + 2], gathered[:].rearrange("p e i -> p i e"))
+
+        x_codes = sb.tile([P, N], U32, name="x_codes", align_bytes=64)
+        x_scale = sb.tile([P, N], U8, name="x_scale", align_bytes=64)
+        nc.vector.quantize_mx(
+            out=x_codes[:].bitcast(E4M3), scales=x_scale[:], in_=x_woven[:].rearrange("p i t -> p (i t)")
+        )
+
+        wv_dealt = sb.tile([P, V_PASSES * D], U16, name="wv_dealt", align_bytes=64)
+        wv_scale = sb.tile([P, V_PASSES * D], U8, name="wv_scale", align_bytes=64)
+
+        weights, sigmoids = [], []
+        for o in range(V_PASSES):
+            weight = sb.tile([P, LANES, N], F32, name=f"weight{o}")
+            sigmoid = sb.tile([P, LANES, N], F32, name=f"sigmoid{o}")
+            for r in range(LANES):
+                cols = slice(K_PASS * o + P * r, K_PASS * o + P * (r + 1))
+                score = psum.tile([P, N], F32, name="score", tag=f"bank{LANES * o + r}")
+                nc.tensor.matmul_mx(
+                    out=score[:],
+                    lhsT=wd_dealt[:, cols].bitcast(E2M1),
+                    lhsT_scale=wd_scale[:, cols],
+                    rhs=x_codes[:].bitcast(E4M3),
+                    rhs_scale=x_scale[:],
+                    start=True,
+                    stop=True,
+                )
+                nc.vector.scalar_tensor_tensor(
+                    weight[:, r, :], y_tiles[o, r], neg_cw[:, o, r : r + 1], rw_sb[:], MULT, MULT
+                )
+                margin = sb.tile([P, N], F32, name=f"margin{o}{r}")
+                nc.vector.tensor_tensor(margin[:], score[:], y_tiles[o, r], MULT)
+                nc.scalar.activation(sigmoid[:, r, :], margin[:], ACT.Sigmoid, scale=-1.0)
+            weights.append(weight)
+            sigmoids.append(sigmoid)
+
+        deal(nc, wv_dealt[:], wv_raw[:].rearrange("p o w -> p (o w)"))
+        deal(nc, wv_scale[:], wv_scale_raw[:])
+
+        sums = [psum.tile([P, N], F32, name=f"dx{j}", tag=f"bank{j}") for j in range(LANES)]
+        half = N // 2
+        for o in range(V_PASSES):
+            g_codes = sb.tile([P, N], U32, name=f"g_codes{o}", align_bytes=64)
+            g_scale = sb.tile([P, N], U8, name=f"g_scale{o}", align_bytes=64)
+            halves = []
+            for h in range(2):
+                slots = slice(half * h, half * (h + 1))
+                g_woven = sb.tile([P, half, LANES], BF16, name=f"g_woven{o}{h}", align_bytes=64)
+                nc.vector.tensor_tensor(
+                    g_woven[:].rearrange("p (c i) r -> p c r i", i=RUN),
+                    sigmoids[o][:, :, slots].rearrange("p r (c i) -> p c r i", i=RUN),
+                    weights[o][:, :, slots].rearrange("p r (c i) -> p c r i", i=RUN),
+                    MULT,
+                )
+                halves.append((slots, g_woven))
+            for slots, g_woven in halves:
+                nc.vector.quantize_mx(
+                    out=g_codes[:, slots].bitcast(E5M2),
+                    scales=g_scale[:, slots],
+                    in_=g_woven[:].rearrange("p i r -> p (i r)"),
+                )
+            for j in (2, 0, 1, 3):
+                cols = slice(D * o + P * j, D * o + P * (j + 1))
+                nc.tensor.matmul_mx(
+                    out=sums[j][:],
+                    lhsT=wv_dealt[:, cols].bitcast(E2M1),
+                    lhsT_scale=wv_scale[:, cols],
+                    rhs=g_codes[:].bitcast(E5M2),
+                    rhs_scale=g_scale[:],
+                    start=(o == 0),
+                    stop=(o == V_PASSES - 1),
+                )
+
+        out_rows = out_0.rearrange("(p j) c -> p j c", j=LANES)
+        out_woven = sb.tile([P, T, LANES], BF16, name="out_woven", align_bytes=64)
+        dx_tiles = {}
+
+        def drain(j, slot):
+            dx_tiles[j] = sb.tile([P, N], F32, name="dx_sb", tag=f"dx_sb{slot}")
+            nc.scalar.copy(dx_tiles[j][:], sums[j][:])
+
+        def scatter(j):
+            nc.vector.tensor_copy(windows[j][:].indirect(offsets[:]), dx_tiles[j][:])
+            nc.sync.dma_start(out=out_rows[:, j, :], in_=windows[j][:])
+
+        for j in (2, 0, 1):
+            drain(j, j)
+        scatter(2)
+        nc.scalar.copy(out_woven[:, :, 2], windows[2][:])
+        drain(3, 2)
+        for j in (0, 1):
+            scatter(j)
+            nc.scalar.copy(out_woven[:, :, j], windows[j][:])
+        scatter(3)
+        last = LANES - 1
+        nc.vector.tensor_copy(out_woven[:, 0:512, last], windows[last][:, 0:512])
+        nc.scalar.copy(out_woven[:, 512:768, last], windows[last][:, 512:768])
+        nc.vector.tensor_copy(out_woven[:, 768:1024, last], windows[last][:, 768:1024])
+
+        out_scale = sb.tile([P, T], U8, name="out_scale", align_bytes=64)
+        out_words = out_1[0].rearrange("p c t -> p (c t)").bitcast(I32)
+        for h in range(2):
+            cols = slice(512 * h, 512 * (h + 1))
+            out_codes = sb.tile([P, 512], U32, name=f"out_codes{h}", align_bytes=64)
+            nc.vector.quantize_mx(
+                out=out_codes[:].bitcast(E4M3),
+                scales=out_scale[:, cols],
+                in_=out_woven[:, cols, :].rearrange("p c j -> p (c j)"),
+            )
+            nc.sync.dma_start(out=out_words[:, cols], in_=out_codes[:].bitcast(I32))
+        for q in range(4):
+            queue = nc.scalar if q % 2 == 0 else nc.sync
+            queue.dma_start(
+                out=out_2[0, 4 * q : 4 * q + 4, :].bitcast(I32),
+                in_=out_scale[32 * q : 32 * q + 4, :].bitcast(I32),
+            )

@@ -45,29 +45,30 @@ def tile_attend_gml_pl_sig_kernel(
         wd_scale_raw = sb.tile([P, V], U8, name="wd_scale_raw")
         wv_scale_raw = sb.tile([P, V_PASSES * D], U8, name="wv_scale_raw")
         nc.gpsimd.memset(wd_scale_raw[:].bitcast(U32), 0)
-        nc.gpsimd.memset(wv_scale_raw[:].bitcast(U32), 0)
+        warm = sb.tile([P, 8], F32, name="warm")
+        nc.vector.memset(warm[:], 0.0)
+        nc.scalar.activation(warm[:], warm[:], ACT.Sigmoid)
 
         wd_raw = sb.tile([P, V], U16, name="wd_raw")
         nc.sync.dma_start(out=wd_raw[:].bitcast(I32), in_=wd_words[0].bitcast(I32))
-        for q in range(4):
-            nc.sync.dma_start(
-                out=wd_scale_raw[32 * q : 32 * q + 4, :].bitcast(I32),
-                in_=wd_scales[0, 4 * q : 4 * q + 4, :].bitcast(I32),
-            )
         cw_sb = sb.tile([P, V_PASSES, LANES], F32, name="cw_sb")
         nc.scalar.dma_start(out=cw_sb[:], in_=cw.rearrange("(o p r) one -> p o (r one)", p=P, r=LANES))
-        warm = sb.tile([P, V_PASSES, LANES], F32, name="warm")
-        nc.scalar.activation(warm[:], cw_sb[:], ACT.Sigmoid)
-        rw_sb = sb.tile([P, N], F32, name="rw_sb")
-        nc.sync.dma_start(out=rw_sb[:], in_=rw)
 
         x_rows = xT.rearrange("(p t) c -> p t c", t=LANES)
         x_planes = []
         for t in range(LANES):
-            plane = sb.tile([P, T], F32, name=f"x_plane{t}")
+            plane = sb.tile([P, T], F32, name=f"x_plane{t}", tag=f"x_plane{t}", align_bytes=64)
             nc.sync.dma_start(out=plane[:], in_=x_rows[:, t, :])
             x_planes.append(plane)
+            if t == 1:
+                for q in range(4):
+                    nc.sync.dma_start(
+                        out=wd_scale_raw[32 * q : 32 * q + 4, :].bitcast(I32),
+                        in_=wd_scales[0, 4 * q : 4 * q + 4, :].bitcast(I32),
+                    )
 
+        rw_sb = sb.tile([P, N], F32, name="rw_sb")
+        nc.sync.dma_start(out=rw_sb[:], in_=rw)
         y_rows = y.rearrange("(o p r) i -> o p r i", p=P, r=LANES)
         y_tiles = {}
         for o in range(V_PASSES):
@@ -79,6 +80,7 @@ def tile_attend_gml_pl_sig_kernel(
 
         wv_raw = sb.tile([P, V_PASSES, D], U16, name="wv_raw")
         nc.sync.dma_start(out=wv_raw[:].bitcast(I32), in_=wv_words.bitcast(I32).rearrange("o p w -> p o w"))
+        nc.gpsimd.memset(wv_scale_raw[:].bitcast(U32), 0)
         for q in range(4):
             nc.sync.dma_start(
                 out=wv_scale_raw[32 * q : 32 * q + 4, :].bitcast(I32).rearrange("f (o w) -> f o w", o=V_PASSES),
@@ -88,65 +90,99 @@ def tile_attend_gml_pl_sig_kernel(
         windows = []
         for j in range(LANES):
             window = sb.tile([P, T], F32, name=f"window{j}")
-            nc.vector.memset(window[:], 0.0)
+            nc.vector.memset(window[:].bitcast(U32), 0)
             windows.append(window)
 
         wd_dealt = sb.tile([P, V], U16, name="wd_dealt", align_bytes=64)
-        wd_scale = sb.tile([P, V], U8, name="wd_scale", align_bytes=64)
         deal(nc, wd_dealt[:], wd_raw[:])
-        deal(nc, wd_scale[:], wd_scale_raw[:])
         neg_cw = sb.tile([P, V_PASSES, LANES], F32, name="neg_cw")
         nc.vector.tensor_scalar_mul(neg_cw[:], cw_sb[:], -1.0)
 
         x_woven = sb.tile([P, N, LANES], BF16, name="x_woven", align_bytes=64)
         for h in range(2):
-            gathered = sb.tile([P, 2, N], BF16, name=f"gathered{h}")
+            gathered = sb.tile([P, 2, N], BF16, name=f"gathered{h}", tag=f"gathered{h}")
             for e in range(2):
                 nc.vector.tensor_copy(gathered[:, e, :], x_planes[2 * h + e][:].indirect(offsets[:]))
             nc.scalar.copy(x_woven[:, :, 2 * h : 2 * h + 2], gathered[:].rearrange("p e i -> p i e"))
 
+        wd_scale = sb.tile([P, V], U8, name="wd_scale", tag="x_plane3", align_bytes=64)
+        deal(nc, wd_scale[:], wd_scale_raw[:])
         x_codes = sb.tile([P, N], U32, name="x_codes", align_bytes=64)
         x_scale = sb.tile([P, N], U8, name="x_scale", align_bytes=64)
         nc.vector.quantize_mx(
             out=x_codes[:].bitcast(E4M3), scales=x_scale[:], in_=x_woven[:].rearrange("p i t -> p (i t)")
         )
 
-        wv_dealt = sb.tile([P, V_PASSES * D], U16, name="wv_dealt", align_bytes=64)
-        wv_scale = sb.tile([P, V_PASSES * D], U8, name="wv_scale", align_bytes=64)
+        weights = [sb.tile([P, LANES, N], F32, name=f"weight{o}") for o in range(V_PASSES)]
+        sigmoids = [sb.tile([P, LANES, N], F32, name=f"sigmoid{o}") for o in range(V_PASSES)]
+        tiles = [(o, r) for o in range(V_PASSES) for r in range(LANES)]
 
-        weights, sigmoids = [], []
-        for o in range(V_PASSES):
-            weight = sb.tile([P, LANES, N], F32, name=f"weight{o}")
-            sigmoid = sb.tile([P, LANES, N], F32, name=f"sigmoid{o}")
-            for r in range(LANES):
-                cols = slice(K_PASS * o + P * r, K_PASS * o + P * (r + 1))
-                score = psum.tile([P, N], F32, name="score", tag=f"bank{LANES * o + r}")
-                nc.tensor.matmul_mx(
-                    out=score[:],
-                    lhsT=wd_dealt[:, cols].bitcast(E2M1),
-                    lhsT_scale=wd_scale[:, cols],
-                    rhs=x_codes[:].bitcast(E4M3),
-                    rhs_scale=x_scale[:],
-                    start=True,
-                    stop=True,
-                )
-                nc.vector.scalar_tensor_tensor(
-                    weight[:, r, :], y_tiles[o, r], neg_cw[:, o, r : r + 1], rw_sb[:], MULT, MULT
-                )
-                margin = sb.tile([P, N], F32, name=f"margin{o}{r}")
-                nc.vector.tensor_tensor(margin[:], score[:], y_tiles[o, r], MULT)
-                nc.scalar.activation(sigmoid[:, r, :], margin[:], ACT.Sigmoid, scale=-1.0)
-            weights.append(weight)
-            sigmoids.append(sigmoid)
+        def weigh_on_vector(o, r):
+            nc.vector.scalar_tensor_tensor(
+                weights[o][:, r, :], y_tiles[o, r], neg_cw[:, o, r : r + 1], rw_sb[:], MULT, MULT
+            )
 
-        deal(nc, wv_dealt[:], wv_raw[:].rearrange("p o w -> p (o w)"))
-        deal(nc, wv_scale[:], wv_scale_raw[:])
+        for o, r in tiles[:2]:
+            weigh_on_vector(o, r)
+        shared = tiles[2:6]
+        outer = sb.tile([P, len(shared), N], F32, name="outer", tag="gathered1")
+        for k, (o, r) in enumerate(shared):
+            nc.scalar.activation(outer[:, k, :], rw_sb[:], ACT.Copy, scale=neg_cw[:, o, r : r + 1])
+            nc.gpsimd.tensor_tensor(weights[o][:, r, :], y_tiles[o, r], outer[:, k, :], MULT)
+
+        for o, r in tiles:
+            cols = slice(K_PASS * o + P * r, K_PASS * o + P * (r + 1))
+            score = psum.tile([P, N], F32, name="score", tag=f"bank{LANES * o + r}")
+            nc.tensor.matmul_mx(
+                out=score[:],
+                lhsT=wd_dealt[:, cols].bitcast(E2M1),
+                lhsT_scale=wd_scale[:, cols],
+                rhs=x_codes[:].bitcast(E4M3),
+                rhs_scale=x_scale[:],
+                start=True,
+                stop=True,
+            )
+            margin = sb.tile([P, N], F32, name=f"margin{o}{r}")
+            nc.vector.tensor_tensor(margin[:], score[:], y_tiles[o, r], MULT)
+            nc.scalar.activation(sigmoids[o][:, r, :], margin[:], ACT.Sigmoid, scale=-1.0)
+        for o, r in tiles[6:]:
+            weigh_on_vector(o, r)
+
+        wv_tiles = {}
+
+        def deal_wv(js, name):
+            words = sb.tile([P, V_PASSES, len(js), P], U16, name=f"wv_words_{name}", align_bytes=64)
+            scales = sb.tile([P, V_PASSES, len(js), P], U8, name=f"wv_scales_{name}", align_bytes=64)
+            pick = slice(js[0], js[-1] + 1)
+            nc.vector.tensor_copy(words[:], wv_raw[:].rearrange("p o (m t) -> p o t m", t=LANES)[:, :, pick, :])
+            nc.vector.tensor_copy(
+                scales[:], wv_scale_raw[:].rearrange("p (o m t) -> p o t m", o=V_PASSES, t=LANES)[:, :, pick, :]
+            )
+            for k, j in enumerate(js):
+                wv_tiles[j] = (words, scales, k)
 
         sums = [psum.tile([P, N], F32, name=f"dx{j}", tag=f"bank{j}") for j in range(LANES)]
+        g_tiles = []
+
+        def back(j, o):
+            words, scales, k = wv_tiles[j]
+            g_codes, g_scale = g_tiles[o]
+            nc.tensor.matmul_mx(
+                out=sums[j][:],
+                lhsT=words[:, o, k, :].bitcast(E2M1),
+                lhsT_scale=scales[:, o, k, :],
+                rhs=g_codes[:].bitcast(E5M2),
+                rhs_scale=g_scale[:],
+                start=(o == 0),
+                stop=(o == V_PASSES - 1),
+            )
+
+        deal_wv([0], "first")
         half = N // 2
         for o in range(V_PASSES):
             g_codes = sb.tile([P, N], U32, name=f"g_codes{o}", align_bytes=64)
             g_scale = sb.tile([P, N], U8, name=f"g_scale{o}", align_bytes=64)
+            g_tiles.append((g_codes, g_scale))
             halves = []
             for h in range(2):
                 slots = slice(half * h, half * (h + 1))
@@ -164,17 +200,11 @@ def tile_attend_gml_pl_sig_kernel(
                     scales=g_scale[:, slots],
                     in_=g_woven[:].rearrange("p i r -> p (i r)"),
                 )
-            for j in (2, 0, 1, 3):
-                cols = slice(D * o + P * j, D * o + P * (j + 1))
-                nc.tensor.matmul_mx(
-                    out=sums[j][:],
-                    lhsT=wv_dealt[:, cols].bitcast(E2M1),
-                    lhsT_scale=wv_scale[:, cols],
-                    rhs=g_codes[:].bitcast(E5M2),
-                    rhs_scale=g_scale[:],
-                    start=(o == 0),
-                    stop=(o == V_PASSES - 1),
-                )
+            back(0, o)
+        deal_wv([1, 2, 3], "rest")
+        for j in (2, 3, 1):
+            for o in range(V_PASSES):
+                back(j, o)
 
         out_rows = out_0.rearrange("(p j) c -> p j c", j=LANES)
         out_woven = sb.tile([P, T, LANES], BF16, name="out_woven", align_bytes=64)
@@ -188,19 +218,19 @@ def tile_attend_gml_pl_sig_kernel(
             nc.vector.tensor_copy(windows[j][:].indirect(offsets[:]), dx_tiles[j][:])
             nc.sync.dma_start(out=out_rows[:, j, :], in_=windows[j][:])
 
-        for j in (2, 0, 1):
+        for j in (0, 2, 3):
             drain(j, j)
-        scatter(2)
-        nc.scalar.copy(out_woven[:, :, 2], windows[2][:])
-        drain(3, 2)
-        for j in (0, 1):
+        scatter(0)
+        nc.scalar.copy(out_woven[:, :, 0], windows[0][:])
+        drain(1, 0)
+        for j in (2, 3):
             scatter(j)
             nc.scalar.copy(out_woven[:, :, j], windows[j][:])
-        scatter(3)
-        last = LANES - 1
+        scatter(1)
+        last = 1
         nc.vector.tensor_copy(out_woven[:, 0:512, last], windows[last][:, 0:512])
-        nc.scalar.copy(out_woven[:, 512:768, last], windows[last][:, 512:768])
-        nc.vector.tensor_copy(out_woven[:, 768:1024, last], windows[last][:, 768:1024])
+        nc.scalar.copy(out_woven[:, 512:704, last], windows[last][:, 512:704])
+        nc.vector.tensor_copy(out_woven[:, 704:1024, last], windows[last][:, 704:1024])
 
         out_scale = sb.tile([P, T], U8, name="out_scale", align_bytes=64)
         out_words = out_1[0].rearrange("p c t -> p (c t)").bitcast(I32)

@@ -49,8 +49,6 @@ def tile_attend_gml_pl_sig_kernel(
         nc.vector.memset(warm[:], 0.0)
         nc.scalar.activation(warm[:], warm[:], ACT.Sigmoid)
 
-        wd_raw = sb.tile([P, V], U16, name="wd_raw")
-        nc.sync.dma_start(out=wd_raw[:].bitcast(I32), in_=wd_words[0].bitcast(I32))
         cw_sb = sb.tile([P, V_PASSES, LANES], F32, name="cw_sb")
         nc.scalar.dma_start(out=cw_sb[:], in_=cw.rearrange("(o p r) one -> p o (r one)", p=P, r=LANES))
 
@@ -67,19 +65,22 @@ def tile_attend_gml_pl_sig_kernel(
                         in_=wd_scales[0, 4 * q : 4 * q + 4, :].bitcast(I32),
                     )
 
+        wd_raw = sb.tile([P, V], U16, name="wd_raw")
+        nc.sync.dma_start(out=wd_raw[:].bitcast(I32), in_=wd_words[0].bitcast(I32))
         rw_sb = sb.tile([P, N], F32, name="rw_sb")
         nc.sync.dma_start(out=rw_sb[:], in_=rw)
         y_rows = y.rearrange("(o p r) i -> o p r i", p=P, r=LANES)
         y_tiles = {}
+        wv_raw = sb.tile([P, V_PASSES, D], U16, name="wv_raw")
         for o in range(V_PASSES):
+            if o == 1:
+                nc.sync.dma_start(out=wv_raw[:].bitcast(I32), in_=wv_words.bitcast(I32).rearrange("o p w -> p o w"))
             for h in range(2):
                 pair = sb.tile([P, 2, N], F32, name=f"y{o}{h}")
                 nc.sync.dma_start(out=pair[:], in_=y_rows[o, :, 2 * h : 2 * h + 2, :])
                 for e in range(2):
                     y_tiles[o, 2 * h + e] = pair[:, e, :]
 
-        wv_raw = sb.tile([P, V_PASSES, D], U16, name="wv_raw")
-        nc.sync.dma_start(out=wv_raw[:].bitcast(I32), in_=wv_words.bitcast(I32).rearrange("o p w -> p o w"))
         nc.gpsimd.memset(wv_scale_raw[:].bitcast(U32), 0)
         for q in range(4):
             nc.sync.dma_start(
@@ -90,11 +91,11 @@ def tile_attend_gml_pl_sig_kernel(
         windows = []
         for j in range(LANES):
             window = sb.tile([P, T], F32, name=f"window{j}")
-            nc.vector.memset(window[:].bitcast(U32), 0)
+            engine = nc.gpsimd if j == 1 else nc.vector
+            engine.memset(window[:].bitcast(U32), 0)
             windows.append(window)
 
         wd_dealt = sb.tile([P, V], U16, name="wd_dealt", align_bytes=64)
-        deal(nc, wd_dealt[:], wd_raw[:])
         neg_cw = sb.tile([P, V_PASSES, LANES], F32, name="neg_cw")
         nc.vector.tensor_scalar_mul(neg_cw[:], cw_sb[:], -1.0)
 
@@ -105,6 +106,7 @@ def tile_attend_gml_pl_sig_kernel(
                 nc.vector.tensor_copy(gathered[:, e, :], x_planes[2 * h + e][:].indirect(offsets[:]))
             nc.scalar.copy(x_woven[:, :, 2 * h : 2 * h + 2], gathered[:].rearrange("p e i -> p i e"))
 
+        deal(nc, wd_dealt[:], wd_raw[:])
         wd_scale = sb.tile([P, V], U8, name="wd_scale", tag="x_plane3", align_bytes=64)
         deal(nc, wd_scale[:], wd_scale_raw[:])
         x_codes = sb.tile([P, N], U32, name="x_codes", align_bytes=64)
@@ -124,7 +126,7 @@ def tile_attend_gml_pl_sig_kernel(
 
         for o, r in tiles[:2]:
             weigh_on_vector(o, r)
-        shared = tiles[2:6]
+        shared = tiles[4:]
         outer = sb.tile([P, len(shared), N], F32, name="outer", tag="gathered1")
         for k, (o, r) in enumerate(shared):
             nc.scalar.activation(outer[:, k, :], rw_sb[:], ACT.Copy, scale=neg_cw[:, o, r : r + 1])
@@ -145,14 +147,14 @@ def tile_attend_gml_pl_sig_kernel(
             margin = sb.tile([P, N], F32, name=f"margin{o}{r}")
             nc.vector.tensor_tensor(margin[:], score[:], y_tiles[o, r], MULT)
             nc.scalar.activation(sigmoids[o][:, r, :], margin[:], ACT.Sigmoid, scale=-1.0)
-        for o, r in tiles[6:]:
+        for o, r in tiles[2:4]:
             weigh_on_vector(o, r)
 
         wv_tiles = {}
 
-        def deal_wv(js, name):
-            words = sb.tile([P, V_PASSES, len(js), P], U16, name=f"wv_words_{name}", align_bytes=64)
-            scales = sb.tile([P, V_PASSES, len(js), P], U8, name=f"wv_scales_{name}", align_bytes=64)
+        def deal_wv(js, words_tag, scales_tag):
+            words = sb.tile([P, V_PASSES, len(js), P], U16, name="wv_words", tag=words_tag, align_bytes=64)
+            scales = sb.tile([P, V_PASSES, len(js), P], U8, name="wv_scales", tag=scales_tag, align_bytes=64)
             pick = slice(js[0], js[-1] + 1)
             nc.vector.tensor_copy(words[:], wv_raw[:].rearrange("p o (m t) -> p o t m", t=LANES)[:, :, pick, :])
             nc.vector.tensor_copy(
@@ -177,16 +179,17 @@ def tile_attend_gml_pl_sig_kernel(
                 stop=(o == V_PASSES - 1),
             )
 
-        deal_wv([0], "first")
+        deal_wv([0], "wv_words0", "wv_scales0")
         half = N // 2
         for o in range(V_PASSES):
-            g_codes = sb.tile([P, N], U32, name=f"g_codes{o}", align_bytes=64)
+            g_codes = sb.tile([P, N], U32, name="g_codes", tag=f"g_codes{o}", align_bytes=64)
             g_scale = sb.tile([P, N], U8, name=f"g_scale{o}", align_bytes=64)
             g_tiles.append((g_codes, g_scale))
             halves = []
-            for h in range(2):
-                slots = slice(half * h, half * (h + 1))
-                g_woven = sb.tile([P, half, LANES], BF16, name=f"g_woven{o}{h}", align_bytes=64)
+            width = N if o == 0 else half
+            for h in range(N // width):
+                slots = slice(width * h, width * (h + 1))
+                g_woven = sb.tile([P, width, LANES], BF16, name="g_woven", tag=f"g_woven{o}{h}", align_bytes=64)
                 nc.vector.tensor_tensor(
                     g_woven[:].rearrange("p (c i) r -> p c r i", i=RUN),
                     sigmoids[o][:, :, slots].rearrange("p r (c i) -> p c r i", i=RUN),
@@ -201,13 +204,13 @@ def tile_attend_gml_pl_sig_kernel(
                     in_=g_woven[:].rearrange("p i r -> p (i r)"),
                 )
             back(0, o)
-        deal_wv([1, 2, 3], "rest")
+        deal_wv([1, 2, 3], "g_woven11", "g_woven10")
         for j in (2, 3, 1):
             for o in range(V_PASSES):
                 back(j, o)
 
         out_rows = out_0.rearrange("(p j) c -> p j c", j=LANES)
-        out_woven = sb.tile([P, T, LANES], BF16, name="out_woven", align_bytes=64)
+        out_woven = sb.tile([P, T, LANES], BF16, name="out_woven", tag="g_codes1", align_bytes=64)
         dx_tiles = {}
 
         def drain(j, slot):
@@ -229,14 +232,14 @@ def tile_attend_gml_pl_sig_kernel(
         scatter(1)
         last = 1
         nc.vector.tensor_copy(out_woven[:, 0:512, last], windows[last][:, 0:512])
-        nc.scalar.copy(out_woven[:, 512:704, last], windows[last][:, 512:704])
-        nc.vector.tensor_copy(out_woven[:, 704:1024, last], windows[last][:, 704:1024])
+        nc.scalar.copy(out_woven[:, 512:768, last], windows[last][:, 512:768])
+        nc.vector.tensor_copy(out_woven[:, 768:1024, last], windows[last][:, 768:1024])
 
         out_scale = sb.tile([P, T], U8, name="out_scale", align_bytes=64)
         out_words = out_1[0].rearrange("p c t -> p (c t)").bitcast(I32)
-        for h in range(2):
-            cols = slice(512 * h, 512 * (h + 1))
-            out_codes = sb.tile([P, 512], U32, name=f"out_codes{h}", align_bytes=64)
+        for first, width in ((0, 512), (768, 256), (512, 256)):
+            cols = slice(first, first + width)
+            out_codes = sb.tile([P, width], U32, name=f"out_codes{first}", align_bytes=64)
             nc.vector.quantize_mx(
                 out=out_codes[:].bitcast(E4M3),
                 scales=out_scale[:, cols],

@@ -1,6 +1,7 @@
 from contextlib import ExitStack
 
 import concourse.mybir as mybir
+from concourse.masks import make_identity
 
 N, T, D, V = 512, 1024, 512, 1024
 FLOPS = 2 * D * V * N * 2
@@ -15,6 +16,7 @@ E4M3 = mybir.dt.float8_e4m3fn_x4
 E5M2 = mybir.dt.float8_e5m2_x4
 E2M1 = mybir.dt.float4_e2m1fn_x4
 MULT = mybir.AluOpType.mult
+ADD = mybir.AluOpType.add
 ACT = mybir.ActivationFunctionType
 
 P = 128
@@ -22,6 +24,7 @@ LANES = 4
 K_PASS = P * LANES
 V_PASSES = V // K_PASS
 RUN = 4
+HALF = N // 2
 
 
 def deal(nc, out, in_):
@@ -39,211 +42,324 @@ def tile_attend_gml_pl_sig_kernel(
         sb = ctx.enter_context(tc.tile_pool(name="sb", bufs=1))
         psum = ctx.enter_context(tc.psum_pool(name="psum", bufs=1))
 
-        offsets = sb.tile([P, N // 16], U16, name="offsets")
-        nc.sync.dma_start(offsets[:], offs)
+        def listed(first, count):
+            return offsets[:, first // 16 : (first + count) // 16]
 
-        wd_scale_raw = sb.tile([P, V], U8, name="wd_scale_raw")
-        wv_scale_raw = sb.tile([P, V_PASSES * D], U8, name="wv_scale_raw")
+        offsets = sb.tile([P, N // 16], U16, name="offsets")
+        x_rows = xT.rearrange("(p t) c -> p t c", t=LANES)
+        x_planes = [sb.tile([P, T], F32, name="x_plane", tag=f"x_plane{t}", align_bytes=64) for t in range(LANES)]
+        nc.sync.dma_start(out=x_planes[0][:], in_=x_rows[:, 0, :])
+        nc.sync.dma_start(offsets[:], offs)
+        wd_scale_raw = sb.tile([P, V], U8, name="wd_scale_raw", tag="wd_scale_raw", align_bytes=64)
+        wv_scale = sb.tile([P, V_PASSES, D], U8, name="wv_scale", align_bytes=64)
         nc.gpsimd.memset(wd_scale_raw[:].bitcast(U32), 0)
+        rw_cols = sb.tile([P, LANES], F32, name="rw_cols")
+        nc.sync.dma_start(out=rw_cols[:], in_=rw[0].rearrange("(p k) -> p k", k=LANES))
+        cw_sb = sb.tile([P, V_PASSES, LANES], F32, name="cw_sb", tag="x_woven1", align_bytes=64)
+        nc.sync.dma_start(out=cw_sb[:], in_=cw.rearrange("(o p r) one -> p o (r one)", p=P, r=LANES))
         warm = sb.tile([P, 8], F32, name="warm")
         nc.vector.memset(warm[:], 0.0)
         nc.scalar.activation(warm[:], warm[:], ACT.Sigmoid)
+        identity = sb.tile([P, P], F32, name="identity")
+        make_identity(nc, identity[:])
+        nc.gpsimd.memset(wv_scale[:].bitcast(U32), 0)
 
-        cw_sb = sb.tile([P, V_PASSES, LANES], F32, name="cw_sb")
-        nc.scalar.dma_start(out=cw_sb[:], in_=cw.rearrange("(o p r) one -> p o (r one)", p=P, r=LANES))
-
-        x_rows = xT.rearrange("(p t) c -> p t c", t=LANES)
-        x_planes = []
-        for t in range(LANES):
-            plane = sb.tile([P, T], F32, name=f"x_plane{t}", tag=f"x_plane{t}", align_bytes=64)
-            nc.sync.dma_start(out=plane[:], in_=x_rows[:, t, :])
-            x_planes.append(plane)
+        for t in range(1, LANES):
+            nc.sync.dma_start(out=x_planes[t][:], in_=x_rows[:, t, :])
             if t == 1:
                 for q in range(4):
                     nc.sync.dma_start(
                         out=wd_scale_raw[32 * q : 32 * q + 4, :].bitcast(I32),
                         in_=wd_scales[0, 4 * q : 4 * q + 4, :].bitcast(I32),
                     )
-
-        wd_raw = sb.tile([P, V], U16, name="wd_raw")
+        wd_raw = sb.tile([P, V], U16, name="wd_raw", tag="wd_raw", align_bytes=64)
         nc.sync.dma_start(out=wd_raw[:].bitcast(I32), in_=wd_words[0].bitcast(I32))
-        rw_sb = sb.tile([P, N], F32, name="rw_sb")
-        nc.sync.dma_start(out=rw_sb[:], in_=rw)
         y_rows = y.rearrange("(o p r) i -> o p r i", p=P, r=LANES)
         y_tiles = {}
-        wv_raw = sb.tile([P, V_PASSES, D], U16, name="wv_raw")
-        for o in range(V_PASSES):
-            if o == 1:
-                nc.sync.dma_start(out=wv_raw[:].bitcast(I32), in_=wv_words.bitcast(I32).rearrange("o p w -> p o w"))
-            for h in range(2):
-                pair = sb.tile([P, 2, N], F32, name=f"y{o}{h}")
-                nc.sync.dma_start(out=pair[:], in_=y_rows[o, :, 2 * h : 2 * h + 2, :])
-                for e in range(2):
-                    y_tiles[o, 2 * h + e] = pair[:, e, :]
+        wv_sb = sb.tile([P, V_PASSES, D], U16, name="wv_sb", align_bytes=64)
+        for h in range(2):
+            for o in range(V_PASSES):
+                if (h, o) == (1, 0):
+                    nc.sync.dma_start(out=wv_sb[:].bitcast(I32), in_=wv_words.bitcast(I32).rearrange("o p w -> p o w"))
+                    for q in range(4):
+                        nc.sync.dma_start(
+                            out=wv_scale[32 * q : 32 * q + 4, :, :].bitcast(I32),
+                            in_=wv_scales[:, 4 * q : 4 * q + 4, :].bitcast(I32).rearrange("o f w -> f o w"),
+                        )
+                y_tiles[h, o] = sb.tile([P, LANES, HALF], F32, name=f"y{h}{o}")
+                nc.sync.dma_start(out=y_tiles[h, o][:], in_=y_rows[o, :, :, HALF * h : HALF * (h + 1)])
 
-        nc.gpsimd.memset(wv_scale_raw[:].bitcast(U32), 0)
-        for q in range(4):
-            nc.sync.dma_start(
-                out=wv_scale_raw[32 * q : 32 * q + 4, :].bitcast(I32).rearrange("f (o w) -> f o w", o=V_PASSES),
-                in_=wv_scales[:, 4 * q : 4 * q + 4, :].bitcast(I32).rearrange("o f w -> f o w"),
-            )
+        neg_cw = sb.tile([P, V_PASSES * LANES], F32, name="neg_cw")
+        nc.scalar.activation(neg_cw[:], cw_sb[:].rearrange("p o r -> p (o r)"), ACT.Copy, scale=-1.0)
+
+        rw_bank = psum.tile([P, LANES, P], F32, name="rw_bank", tag="bank7")
+        for k in range(LANES):
+            nc.tensor.transpose(rw_bank[:, k, :], rw_cols[:, k : k + 1].to_broadcast([P, P]), identity[:])
+        outer = {}
+
+        def spread(h, factors, tag):
+            outer[h] = sb.tile([P, V_PASSES * LANES, HALF], F32, name="outer", tag=tag, align_bytes=64)
+            rows = slice(h * HALF // LANES, (h + 1) * HALF // LANES)
+            for k in range(V_PASSES * LANES):
+                nc.scalar.activation(
+                    outer[h][:, k, :].rearrange("p (n k) -> p n k", k=LANES),
+                    rw_bank[:].rearrange("p k n -> p n k")[:, rows, :],
+                    ACT.Copy,
+                    scale=factors[:, k : k + 1],
+                )
+
+        neg_cw_early = sb.tile([P, V_PASSES * LANES], F32, name="neg_cw_early", tag="x_woven0", align_bytes=64)
+        nc.scalar.activation(neg_cw_early[:], cw_sb[:].rearrange("p o r -> p (o r)"), ACT.Copy, scale=-1.0)
+        spread(0, neg_cw_early, "outer0")
 
         windows = []
         for j in range(LANES):
-            window = sb.tile([P, T], F32, name=f"window{j}")
-            engine = nc.gpsimd if j == 1 else nc.vector
-            engine.memset(window[:].bitcast(U32), 0)
+            window = sb.tile([P, T], F32, name="window", tag=f"window{j}")
+            nc.gpsimd.memset(window[:].bitcast(U32), 0)
             windows.append(window)
 
-        wd_dealt = sb.tile([P, V], U16, name="wd_dealt", align_bytes=64)
-        neg_cw = sb.tile([P, V_PASSES, LANES], F32, name="neg_cw")
-        nc.vector.tensor_scalar_mul(neg_cw[:], cw_sb[:], -1.0)
+        g_codes = [sb.tile([P, N], U32, name=f"g_codes{o}", align_bytes=64) for o in range(V_PASSES)]
+        g_scale = [sb.tile([P, N], U8, name=f"g_scale{o}", align_bytes=64) for o in range(V_PASSES)]
 
-        x_woven = sb.tile([P, N, LANES], BF16, name="x_woven", align_bytes=64)
-        for h in range(2):
-            gathered = sb.tile([P, 2, N], BF16, name=f"gathered{h}", tag=f"gathered{h}")
-            for e in range(2):
-                nc.vector.tensor_copy(gathered[:, e, :], x_planes[2 * h + e][:].indirect(offsets[:]))
-            nc.scalar.copy(x_woven[:, :, 2 * h : 2 * h + 2], gathered[:].rearrange("p e i -> p i e"))
+        def tile(shape, dtype, tag):
+            return sb.tile(shape, dtype, name="shared", tag=tag, align_bytes=64)
 
-        deal(nc, wd_dealt[:], wd_raw[:])
-        wd_scale = sb.tile([P, V], U8, name="wd_scale", tag="x_plane3", align_bytes=64)
+        def gather(out, t, h):
+            nc.vector.tensor_copy(out, x_planes[t][:].indirect(listed(HALF * h, HALF)))
+
+        def walk_woven(woven):
+            return woven.rearrange("p (c i) r -> p c r i", i=RUN)
+
+        def walk_lanes(lanes):
+            return lanes.rearrange("p r (c i) -> p c r i", i=RUN)
+
+        x_scale = {}
+        x_codes = {}
+
+        def quantise_x(h, first, count, woven):
+            nc.vector.quantize_mx(
+                out=x_codes[h][:, first : first + count].bitcast(E4M3),
+                scales=x_scale[h][:, first : first + count],
+                in_=woven[:].rearrange("p i t -> p (i t)"),
+            )
+
+        early_x = tile([P, LANES, HALF], BF16, "early_x")
+        late_x = [tile([P, 2, HALF], BF16, "late_x0")[:]]
+        for t in range(LANES - 1):
+            gather(early_x[:, t, :], t, 0)
+            if t < 2:
+                gather(late_x[0][:, t, :], t, 1)
+        wd_scale = tile([P, V], U8, "x_plane1")
         deal(nc, wd_scale[:], wd_scale_raw[:])
-        x_codes = sb.tile([P, N], U32, name="x_codes", align_bytes=64)
-        x_scale = sb.tile([P, N], U8, name="x_scale", align_bytes=64)
-        nc.vector.quantize_mx(
-            out=x_codes[:].bitcast(E4M3), scales=x_scale[:], in_=x_woven[:].rearrange("p i t -> p (i t)")
-        )
+        gather(early_x[:, LANES - 1, :], LANES - 1, 0)
+        wd_dealt = sb.tile([P, V], U16, name="wd_dealt", align_bytes=64)
+        deal(nc, wd_dealt[:], wd_raw[:])
+        x_codes[0] = tile([P, HALF], U32, "wd_raw")
+        x_scale[0] = tile([P, HALF], U8, "wd_scale_raw")
+        for b in range(2):
+            woven = tile([P, P, LANES], BF16, f"x_woven{b}")
+            nc.scalar.copy(walk_woven(woven[:]), walk_lanes(early_x[:, :, P * b : P * (b + 1)]))
+            quantise_x(0, P * b, P, woven)
+        late_x.append(tile([P, 2, HALF], BF16, "x_woven0")[:])
+        for t in range(2, LANES):
+            gather(late_x[1][:, t - 2, :], t, 1)
 
-        weights = [sb.tile([P, LANES, N], F32, name=f"weight{o}") for o in range(V_PASSES)]
-        sigmoids = [sb.tile([P, LANES, N], F32, name=f"sigmoid{o}") for o in range(V_PASSES)]
-        tiles = [(o, r) for o in range(V_PASSES) for r in range(LANES)]
+        def lanes_of(flat):
+            return flat.rearrange("p (r i) -> p r i", i=HALF)
 
-        def weigh_on_vector(o, r):
-            nc.vector.scalar_tensor_tensor(
-                weights[o][:, r, :], y_tiles[o, r], neg_cw[:, o, r : r + 1], rw_sb[:], MULT, MULT
+        def score(h, o, pair, margin, sigmoid):
+            bank = psum.tile([P, 2, HALF], F32, name="score", tag=f"bank{4 * h + 2 * o + pair}")
+            for e in range(2):
+                first = K_PASS * o + P * (2 * pair + e)
+                nc.tensor.matmul_mx(
+                    out=bank[:, e, :],
+                    lhsT=wd_dealt[:, first : first + P].bitcast(E2M1),
+                    lhsT_scale=wd_scale[:, first : first + P],
+                    rhs=x_codes[h][:].bitcast(E4M3),
+                    rhs_scale=x_scale[h][:],
+                    start=True,
+                    stop=True,
+                )
+            rows = slice(2 * pair, 2 * pair + 2)
+            nc.vector.tensor_tensor(margin, bank[:], y_tiles[h, o][:, rows, :], MULT)
+            nc.scalar.activation(sigmoid[:, rows, :], margin, ACT.Sigmoid, scale=-1.0)
+
+        def weigh(engine, h, o, rows, weight):
+            engine.tensor_tensor(
+                weight[:, rows, :], y_tiles[h, o][:, rows, :], outer[h][:, LANES * o + rows.start : LANES * o + rows.stop, :], MULT
             )
 
-        for o, r in tiles[:2]:
-            weigh_on_vector(o, r)
-        shared = tiles[4:]
-        outer = sb.tile([P, len(shared), N], F32, name="outer", tag="gathered1")
-        for k, (o, r) in enumerate(shared):
-            nc.scalar.activation(outer[:, k, :], rw_sb[:], ACT.Copy, scale=neg_cw[:, o, r : r + 1])
-            nc.gpsimd.tensor_tensor(weights[o][:, r, :], y_tiles[o, r], outer[:, k, :], MULT)
+        def product(woven, sigmoid, weight):
+            nc.vector.tensor_tensor(walk_woven(woven), walk_lanes(sigmoid), walk_lanes(weight), MULT)
 
-        for o, r in tiles:
-            cols = slice(K_PASS * o + P * r, K_PASS * o + P * (r + 1))
-            score = psum.tile([P, N], F32, name="score", tag=f"bank{LANES * o + r}")
-            nc.tensor.matmul_mx(
-                out=score[:],
-                lhsT=wd_dealt[:, cols].bitcast(E2M1),
-                lhsT_scale=wd_scale[:, cols],
-                rhs=x_codes[:].bitcast(E4M3),
-                rhs_scale=x_scale[:],
-                start=True,
-                stop=True,
+        def quantise_g(o, first, count, woven):
+            nc.vector.quantize_mx(
+                out=g_codes[o][:, first : first + count].bitcast(E5M2),
+                scales=g_scale[o][:, first : first + count],
+                in_=woven[:].rearrange("p i r -> p (i r)"),
             )
-            margin = sb.tile([P, N], F32, name=f"margin{o}{r}")
-            nc.vector.tensor_tensor(margin[:], score[:], y_tiles[o, r], MULT)
-            nc.scalar.activation(sigmoids[o][:, r, :], margin[:], ACT.Sigmoid, scale=-1.0)
-        for o, r in tiles[2:4]:
-            weigh_on_vector(o, r)
+
+        def back_early(block):
+            cols = slice(P * block, P * (block + 1))
+            sums = psum.tile([P, D], F32, name="sums", tag=f"bank{2 * block}")
+            for o in range(V_PASSES):
+                nc.tensor.matmul_mx(
+                    out=sums[:],
+                    lhsT=g_codes[o][:, cols].bitcast(E5M2),
+                    lhsT_scale=g_scale[o][:, cols],
+                    rhs=wv_sb[:, o, :].bitcast(E2M1),
+                    rhs_scale=wv_scale[:, o, :],
+                    start=(o == 0),
+                    stop=(o == V_PASSES - 1),
+                )
+            by_lane = sb.tile([P, LANES, P], F32, name=f"by_lane{block}")
+            for pair in range(2):
+                lanes = slice(2 * pair, 2 * pair + 2)
+                nc.scalar.copy(by_lane[:, lanes, :], sums[:].rearrange("p (m j) -> p j m", j=LANES)[:, lanes, :])
+            turned = psum.tile([P, LANES, P], F32, name="turned", tag=f"bank{2 * block + 1}")
+            for j in range(LANES):
+                nc.tensor.transpose(turned[:, j, :], by_lane[:, j, :], identity[:])
+            return turned
 
         wv_tiles = {}
 
-        def deal_wv(js, words_tag, scales_tag):
-            words = sb.tile([P, V_PASSES, len(js), P], U16, name="wv_words", tag=words_tag, align_bytes=64)
-            scales = sb.tile([P, V_PASSES, len(js), P], U8, name="wv_scales", tag=scales_tag, align_bytes=64)
-            pick = slice(js[0], js[-1] + 1)
-            nc.vector.tensor_copy(words[:], wv_raw[:].rearrange("p o (m t) -> p o t m", t=LANES)[:, :, pick, :])
-            nc.vector.tensor_copy(
-                scales[:], wv_scale_raw[:].rearrange("p (o m t) -> p o t m", o=V_PASSES, t=LANES)[:, :, pick, :]
-            )
-            for k, j in enumerate(js):
-                wv_tiles[j] = (words, scales, k)
+        def deal_wv(parity, words_tag, scales_tag):
+            words = tile([P, V_PASSES, 2, P], U16, words_tag)
+            scales = tile([P, V_PASSES, 2, P], U8, scales_tag)
+            for dealt, raw in ((words, wv_sb), (scales, wv_scale)):
+                nc.vector.tensor_copy(
+                    dealt[:], raw[:].rearrange("p o (m k e) -> p o k m e", k=2, e=2)[:, :, :, :, parity]
+                )
+            for k in range(2):
+                wv_tiles[2 * k + parity] = (words, scales, k)
 
-        sums = [psum.tile([P, N], F32, name=f"dx{j}", tag=f"bank{j}") for j in range(LANES)]
-        g_tiles = []
-
-        def back(j, o):
+        def back(j, bank):
             words, scales, k = wv_tiles[j]
-            g_codes, g_scale = g_tiles[o]
-            nc.tensor.matmul_mx(
-                out=sums[j][:],
-                lhsT=words[:, o, k, :].bitcast(E2M1),
-                lhsT_scale=scales[:, o, k, :],
-                rhs=g_codes[:].bitcast(E5M2),
-                rhs_scale=g_scale[:],
-                start=(o == 0),
-                stop=(o == V_PASSES - 1),
-            )
-
-        deal_wv([0], "wv_words0", "wv_scales0")
-        half = N // 2
-        for o in range(V_PASSES):
-            g_codes = sb.tile([P, N], U32, name="g_codes", tag=f"g_codes{o}", align_bytes=64)
-            g_scale = sb.tile([P, N], U8, name=f"g_scale{o}", align_bytes=64)
-            g_tiles.append((g_codes, g_scale))
-            halves = []
-            width = N if o == 0 else half
-            for h in range(N // width):
-                slots = slice(width * h, width * (h + 1))
-                g_woven = sb.tile([P, width, LANES], BF16, name="g_woven", tag=f"g_woven{o}{h}", align_bytes=64)
-                nc.vector.tensor_tensor(
-                    g_woven[:].rearrange("p (c i) r -> p c r i", i=RUN),
-                    sigmoids[o][:, :, slots].rearrange("p r (c i) -> p c r i", i=RUN),
-                    weights[o][:, :, slots].rearrange("p r (c i) -> p c r i", i=RUN),
-                    MULT,
-                )
-                halves.append((slots, g_woven))
-            for slots, g_woven in halves:
-                nc.vector.quantize_mx(
-                    out=g_codes[:, slots].bitcast(E5M2),
-                    scales=g_scale[:, slots],
-                    in_=g_woven[:].rearrange("p i r -> p (i r)"),
-                )
-            back(0, o)
-        deal_wv([1, 2, 3], "g_woven11", "g_woven10")
-        for j in (2, 3, 1):
+            sums = psum.tile([P, N], F32, name="sums", tag=f"bank{bank}")
             for o in range(V_PASSES):
-                back(j, o)
+                nc.tensor.matmul_mx(
+                    out=sums[:],
+                    lhsT=words[:, o, k, :].bitcast(E2M1),
+                    lhsT_scale=scales[:, o, k, :],
+                    rhs=g_codes[o][:].bitcast(E5M2),
+                    rhs_scale=g_scale[o][:],
+                    start=(o == 0),
+                    stop=(o == V_PASSES - 1),
+                )
+            return sums
+
+        def drain(sums, first, count, tag):
+            dx = tile([P, count], F32, tag)
+            nc.scalar.copy(dx[:], sums[:, first : first + count])
+            return dx
+
+        def scatter(j, dx, first, count):
+            nc.vector.tensor_copy(windows[j][:].indirect(listed(first, count)), dx)
+
+        first_pair, second_pair, all_lanes = slice(0, 2), slice(2, LANES), slice(0, LANES)
+
+        weights = [tile([P, LANES, HALF], F32, "x_woven1")[:]]
+        weigh(nc.gpsimd, 0, 0, first_pair, weights[0])
+        weigh(nc.gpsimd, 0, 0, second_pair, weights[0])
+        sigmoids = [tile([P, LANES, HALF], F32, tag) for tag in ("sigmoid00", "sigmoid01")]
+        for o in range(V_PASSES):
+            for pair in range(2):
+                score(0, o, pair, tile([P, 2, HALF], F32, f"margin{o}{pair}")[:], sigmoids[o])
+        late_woven = tile([P, HALF, LANES], BF16, "early_x")
+        for pair in range(2):
+            nc.scalar.copy(walk_woven(late_woven[:, :, 2 * pair : 2 * pair + 2]), walk_lanes(late_x[pair]))
+        weights.append(tile([P, LANES, HALF], F32, "margin00")[:])
+        weigh(nc.vector, 0, 1, all_lanes, weights[1])
+        x_codes[1] = tile([P, HALF], U32, "margin01")
+        x_scale[1] = tile([P, HALF], U8, "x_scale1")
+        quantise_x(1, 0, HALF, late_woven)
+        deal_wv(0, "margin10", "wd_raw")
+        spread(1, neg_cw, "margin11")
+        turned = []
+        for block, tags in enumerate((("early_x", "g_woven01"), ("g_woven10", "g_woven11"))):
+            cols = slice(P * block, P * (block + 1))
+            woven = [tile([P, P, LANES], BF16, tag) for tag in tags]
+            for o in range(V_PASSES):
+                product(woven[o][:], sigmoids[o][:, :, cols], weights[o][:, :, cols])
+            for o in range(V_PASSES):
+                quantise_g(o, P * block, P, woven[o])
+            turned.append(back_early(block))
+        early_dx = [sb.tile([P, LANES, P], F32, name=f"early_dx{block}") for block in range(2)]
+        nc.scalar.copy(early_dx[0][:], turned[0][:])
+
+        unit = 2 * HALF
+        stage = tile([P, 8 * unit], F32, "g_woven11")
+        weights = [lanes_of(stage[:, 2 * unit * o : 2 * unit * (o + 1)]) for o in range(V_PASSES)]
+        weigh(nc.gpsimd, 1, 0, first_pair, weights[0])
+        weigh(nc.gpsimd, 1, 0, second_pair, weights[0])
+        weigh(nc.gpsimd, 1, 1, first_pair, weights[1])
+        weigh(nc.gpsimd, 1, 1, second_pair, weights[1])
+        sigmoids = [tile([P, LANES, HALF], F32, f"sigmoid1{o}") for o in range(V_PASSES)]
+        for o in range(V_PASSES):
+            for pair in range(2):
+                k = 4 + 2 * o + pair
+                score(1, o, pair, lanes_of(stage[:, unit * k : unit * (k + 1)]), sigmoids[o])
+        held = LANES - 1
+        nc.scalar.copy(early_dx[1][:, 0:held, :], turned[1][:, 0:held, :])
+        for j in range(LANES):
+            scatter(j, early_dx[0][:, j, :], 0, P)
+        for j in range(held):
+            scatter(j, early_dx[1][:, j, :], P, P)
+        woven = [tile([P, HALF, LANES], BF16, f"late_woven{o}") for o in range(V_PASSES)]
+        for o, b in ((0, 0), (0, 1), (1, 0)):
+            cols = slice(P * b, P * (b + 1))
+            lanes = sb.tile([P, LANES, P], BF16, name=f"lanes{o}{b}")
+            nc.gpsimd.tensor_tensor(lanes[:], sigmoids[o][:, :, cols], weights[o][:, :, cols], MULT)
+            nc.scalar.copy(walk_woven(woven[o][:, cols, :]), walk_lanes(lanes[:]))
+        product(woven[1][:, P:HALF, :], sigmoids[1][:, :, P:HALF], weights[1][:, :, P:HALF])
+        for o in range(V_PASSES):
+            quantise_g(o, HALF, HALF, woven[o])
+        held_dx = tile([P, P], F32, "late_woven1")
+        nc.scalar.copy(held_dx[:], turned[1][:, held, :])
+        deal_wv(1, "late_woven0", "sigmoid11")
+        sums = {j: back(j, bank) for j, bank in ((0, 4), (2, 5), (3, 6), (1, 7))}
+        scatter(held, held_dx[:], P, P)
 
         out_rows = out_0.rearrange("(p j) c -> p j c", j=LANES)
-        out_woven = sb.tile([P, T, LANES], BF16, name="out_woven", tag="g_codes1", align_bytes=64)
-        dx_tiles = {}
+        pieces = ((0, 512), (512, 256), (768, 256))
+        pairs = [sb.tile([P, 2, width, 2], BF16, name=f"pairs{first}") for first, width in pieces]
 
-        def drain(j, slot):
-            dx_tiles[j] = sb.tile([P, N], F32, name="dx_sb", tag=f"dx_sb{slot}")
-            nc.scalar.copy(dx_tiles[j][:], sums[j][:])
+        def round_lane(engine_copy, j, k):
+            first, width = pieces[k]
+            engine_copy(pairs[k][:, j // 2, :, j % 2], windows[j][:, first : first + width])
 
-        def scatter(j):
-            nc.vector.tensor_copy(windows[j][:].indirect(offsets[:]), dx_tiles[j][:])
-            nc.sync.dma_start(out=out_rows[:, j, :], in_=windows[j][:])
-
-        for j in (0, 2, 3):
-            drain(j, j)
-        scatter(0)
-        nc.scalar.copy(out_woven[:, :, 0], windows[0][:])
-        drain(1, 0)
-        for j in (2, 3):
-            scatter(j)
-            nc.scalar.copy(out_woven[:, :, j], windows[j][:])
-        scatter(1)
+        spans = {j: (HALF, HALF) for j in range(LANES)}
         last = 1
-        nc.vector.tensor_copy(out_woven[:, 0:512, last], windows[last][:, 0:512])
-        nc.scalar.copy(out_woven[:, 512:768, last], windows[last][:, 512:768])
-        nc.vector.tensor_copy(out_woven[:, 768:1024, last], windows[last][:, 768:1024])
+        late_dx = {j: drain(sums[j], *spans[j], f"dx{j}") for j in (0, 2, 3)}
+        for j in (0, 2, 3):
+            scatter(j, late_dx[j][:], *spans[j])
+            nc.sync.dma_start(out=out_rows[:, j, :], in_=windows[j][:])
+            for k in range(len(pieces)):
+                round_lane(nc.scalar.copy, j, k)
+            if j == 0:
+                late_dx[last] = drain(sums[last], *spans[last], "dx0")
+        scatter(last, late_dx[last][:], *spans[last])
+        nc.sync.dma_start(out=out_rows[:, last, :], in_=windows[last][:])
 
         out_scale = sb.tile([P, T], U8, name="out_scale", align_bytes=64)
         out_words = out_1[0].rearrange("p c t -> p (c t)").bitcast(I32)
-        for first, width in ((0, 512), (768, 256), (512, 256)):
+        woven_out = {}
+        for k, engine_copy, word in ((0, nc.vector.tensor_copy, I32), (1, nc.scalar.copy, U32), (2, nc.scalar.copy, U32)):
+            first, width = pieces[k]
+            round_lane(engine_copy, last, k)
+            woven_out[k] = sb.tile([P, width, LANES], BF16, name=f"out_woven{first}", align_bytes=64)
+            engine_copy(
+                woven_out[k][:].bitcast(word),
+                pairs[k][:].rearrange("p h c e -> p h (c e)").bitcast(word).rearrange("p h c -> p c h"),
+            )
+        for k in range(len(pieces)):
+            first, width = pieces[k]
             cols = slice(first, first + width)
             out_codes = sb.tile([P, width], U32, name=f"out_codes{first}", align_bytes=64)
             nc.vector.quantize_mx(
                 out=out_codes[:].bitcast(E4M3),
                 scales=out_scale[:, cols],
-                in_=out_woven[:, cols, :].rearrange("p c j -> p (c j)"),
+                in_=woven_out[k][:].rearrange("p c j -> p (c j)"),
             )
             nc.sync.dma_start(out=out_words[:, cols], in_=out_codes[:].bitcast(I32))
         for q in range(4):

@@ -169,17 +169,20 @@ def tile_attend_gml_pl_sig_kernel(
 
         def score(h, o, pair, margin, sigmoid):
             bank = psum.tile([P, 2, HALF], F32, name="score", tag=f"bank{4 * h + 2 * o + pair}")
-            for e in range(2):
-                first = K_PASS * o + P * (2 * pair + e)
-                nc.tensor.matmul_mx(
-                    out=bank[:, e, :],
-                    lhsT=wd_dealt[:, first : first + P].bitcast(E2M1),
-                    lhsT_scale=wd_scale[:, first : first + P],
-                    rhs=x_codes[h][:].bitcast(E4M3),
-                    rhs_scale=x_scale[h][:],
-                    start=True,
-                    stop=True,
-                )
+            width = P if (h, o, pair) == (0, 0, 0) else HALF
+            for col in range(0, HALF, width):
+                cols = slice(col, col + width)
+                for e in range(2):
+                    first = K_PASS * o + P * (2 * pair + e)
+                    nc.tensor.matmul_mx(
+                        out=bank[:, e, cols],
+                        lhsT=wd_dealt[:, first : first + P].bitcast(E2M1),
+                        lhsT_scale=wd_scale[:, first : first + P],
+                        rhs=x_codes[h][:, cols].bitcast(E4M3),
+                        rhs_scale=x_scale[h][:, cols],
+                        start=True,
+                        stop=True,
+                    )
             rows = slice(2 * pair, 2 * pair + 2)
             nc.vector.tensor_tensor(margin, bank[:], y_tiles[h, o][:, rows, :], MULT)
             nc.scalar.activation(sigmoid[:, rows, :], margin, ACT.Sigmoid, scale=-1.0)
@@ -261,13 +264,13 @@ def tile_attend_gml_pl_sig_kernel(
         weights = [tile([P, LANES, HALF], F32, "x_woven1")[:]]
         weigh(nc.gpsimd, 0, 0, first_pair, weights[0])
         weigh(nc.gpsimd, 0, 0, second_pair, weights[0])
-        sigmoids = [tile([P, LANES, HALF], F32, tag) for tag in ("sigmoid00", "sigmoid01")]
-        for o in range(V_PASSES):
-            for pair in range(2):
-                score(0, o, pair, tile([P, 2, HALF], F32, f"margin{o}{pair}")[:], sigmoids[o])
         late_woven = tile([P, HALF, LANES], BF16, "early_x")
         for pair in range(2):
             nc.scalar.copy(walk_woven(late_woven[:, :, 2 * pair : 2 * pair + 2]), walk_lanes(late_x[pair]))
+        sigmoids = [tile([P, LANES, HALF], F32, tag) for tag in ("late_x0", "x_woven0")]
+        for o in range(V_PASSES):
+            for pair in range(2):
+                score(0, o, pair, tile([P, 2, HALF], F32, f"margin{o}{pair}")[:], sigmoids[o])
         weights.append(tile([P, LANES, HALF], F32, "margin00")[:])
         weigh(nc.vector, 0, 1, all_lanes, weights[1])
         x_codes[1] = tile([P, HALF], U32, "margin01")
@@ -299,29 +302,30 @@ def tile_attend_gml_pl_sig_kernel(
             for pair in range(2):
                 k = 4 + 2 * o + pair
                 score(1, o, pair, lanes_of(stage[:, unit * k : unit * (k + 1)]), sigmoids[o])
-        held = LANES - 1
+        held = LANES - 2
         nc.scalar.copy(early_dx[1][:, 0:held, :], turned[1][:, 0:held, :])
         for j in range(LANES):
             scatter(j, early_dx[0][:, j, :], 0, P)
         for j in range(held):
             scatter(j, early_dx[1][:, j, :], P, P)
         woven = [tile([P, HALF, LANES], BF16, f"late_woven{o}") for o in range(V_PASSES)]
-        for o, b in ((0, 0), (0, 1), (1, 0)):
+        for o, b in ((0, 0), (0, 1)):
             cols = slice(P * b, P * (b + 1))
             lanes = sb.tile([P, LANES, P], BF16, name=f"lanes{o}{b}")
             nc.gpsimd.tensor_tensor(lanes[:], sigmoids[o][:, :, cols], weights[o][:, :, cols], MULT)
             nc.scalar.copy(walk_woven(woven[o][:, cols, :]), walk_lanes(lanes[:]))
-        product(woven[1][:, P:HALF, :], sigmoids[1][:, :, P:HALF], weights[1][:, :, P:HALF])
+        product(woven[1][:], sigmoids[1][:], weights[1])
         for o in range(V_PASSES):
             quantise_g(o, HALF, HALF, woven[o])
-        held_dx = tile([P, P], F32, "late_woven1")
-        nc.scalar.copy(held_dx[:], turned[1][:, held, :])
+        held_dx = tile([P, LANES - held, P], F32, "late_woven1")
+        nc.scalar.copy(held_dx[:], turned[1][:, held:, :])
         deal_wv(1, "late_woven0", "sigmoid11")
         sums = {j: back(j, bank) for j, bank in ((0, 4), (2, 5), (3, 6), (1, 7))}
-        scatter(held, held_dx[:], P, P)
+        for j in range(held, LANES):
+            scatter(j, held_dx[:, j - held, :], P, P)
 
         out_rows = out_0.rearrange("(p j) c -> p j c", j=LANES)
-        pieces = ((0, 512), (512, 256), (768, 256))
+        pieces = tuple((first, 256) for first in range(0, T, 256))
         pairs = [sb.tile([P, 2, width, 2], BF16, name=f"pairs{first}") for first, width in pieces]
 
         def round_lane(engine_copy, j, k):
@@ -344,14 +348,22 @@ def tile_attend_gml_pl_sig_kernel(
         out_scale = sb.tile([P, T], U8, name="out_scale", align_bytes=64)
         out_words = out_1[0].rearrange("p c t -> p (c t)").bitcast(I32)
         woven_out = {}
-        for k, engine_copy, word in ((0, nc.vector.tensor_copy, I32), (1, nc.scalar.copy, U32), (2, nc.scalar.copy, U32)):
+
+        def join_pairs(engine_copy, word, k):
             first, width = pieces[k]
-            round_lane(engine_copy, last, k)
             woven_out[k] = sb.tile([P, width, LANES], BF16, name=f"out_woven{first}", align_bytes=64)
             engine_copy(
                 woven_out[k][:].bitcast(word),
                 pairs[k][:].rearrange("p h c e -> p h (c e)").bitcast(word).rearrange("p h c -> p c h"),
             )
+
+        for k in (0, 1, 2):
+            round_lane(nc.vector.tensor_copy, last, k)
+        round_lane(nc.scalar.copy, last, 3)
+        for k in (0, 1):
+            join_pairs(nc.vector.tensor_copy, I32, k)
+        for k in (2, 3):
+            join_pairs(nc.scalar.copy, U32, k)
         for k in range(len(pieces)):
             first, width = pieces[k]
             cols = slice(first, first + width)

@@ -115,7 +115,8 @@ def tile_attend_gml_pl_sig_kernel(
         windows = []
         for j in range(LANES):
             window = sb.tile([P, T], F32, name="window", tag=f"window{j}")
-            nc.gpsimd.memset(window[:].bitcast(U32), 0)
+            engine = nc.gpsimd if j == LANES - 1 else nc.vector
+            engine.memset(window[:].bitcast(U32), 0)
             windows.append(window)
 
         g_codes = [sb.tile([P, N], U32, name=f"g_codes{o}", align_bytes=64) for o in range(V_PASSES)]

@@ -25,6 +25,7 @@ K_PASS = P * LANES
 V_PASSES = V // K_PASS
 RUN = 4
 HALF = N // 2
+V_CLEARS = 2
 
 
 def deal(nc, out, in_):
@@ -45,88 +46,79 @@ def tile_attend_gml_pl_sig_kernel(
         def listed(first, count):
             return offsets[:, first // 16 : (first + count) // 16]
 
-        offsets = sb.tile([P, N // 16], U16, name="offsets")
-        x_rows = xT.rearrange("(p t) c -> p t c", t=LANES)
-        x_planes = [sb.tile([P, T], F32, name="x_plane", tag=f"x_plane{t}", align_bytes=64) for t in range(LANES)]
-        nc.sync.dma_start(out=x_planes[0][:], in_=x_rows[:, 0, :])
-        nc.sync.dma_start(offsets[:], offs)
-        wd_scale_raw = sb.tile([P, V], U8, name="wd_scale_raw", tag="wd_scale_raw", align_bytes=64)
-        wv_scale = sb.tile([P, V_PASSES, D], U8, name="wv_scale", align_bytes=64)
+        def tile(shape, dtype, tag):
+            return sb.tile(shape, dtype, name="shared", tag=tag, align_bytes=64)
+
+        def bank(shape, number):
+            return psum.tile(shape, F32, name="bank", tag=f"bank{number}")
+
+        wd_scale_raw = tile([P, V], U8, "wd_scale_raw")
+        wv_scale = tile([P, V_PASSES, D], U8, "wv_scale")
         nc.gpsimd.memset(wd_scale_raw[:].bitcast(U32), 0)
-        rw_cols = sb.tile([P, LANES], F32, name="rw_cols")
+        for q in range(4):
+            nc.sync.dma_start(
+                out=wd_scale_raw[32 * q : 32 * q + 4, :].bitcast(I32),
+                in_=wd_scales[0, 4 * q : 4 * q + 4, :].bitcast(I32),
+            )
+        wd_raw = tile([P, V], U16, "wd_raw")
+        nc.sync.dma_start(out=wd_raw[:].bitcast(I32), in_=wd_words[0].bitcast(I32))
+        offsets = sb.tile([P, N // 16], U16, name="offsets")
+        nc.sync.dma_start(offsets[:], offs)
+        rw_cols = tile([P, LANES], F32, "rw_cols")
         nc.sync.dma_start(out=rw_cols[:], in_=rw[0].rearrange("(p k) -> p k", k=LANES))
-        cw_sb = sb.tile([P, V_PASSES, LANES], F32, name="cw_sb", tag="x_woven1", align_bytes=64)
+        x_rows = xT.rearrange("(p t) c -> p t c", t=LANES)
+        x_planes = [tile([P, T], F32, f"x_plane{t}") for t in range(LANES)]
+        nc.sync.dma_start(out=x_planes[0][:], in_=x_rows[:, 0, :])
+        cw_sb = tile([P, V_PASSES, LANES], F32, "cw_sb")
         nc.sync.dma_start(out=cw_sb[:], in_=cw.rearrange("(o p r) one -> p o (r one)", p=P, r=LANES))
-        warm = sb.tile([P, 8], F32, name="warm")
+        for t in range(1, LANES):
+            nc.sync.dma_start(out=x_planes[t][:], in_=x_rows[:, t, :])
+        warm = tile([P, 8], F32, "warm")
         nc.vector.memset(warm[:], 0.0)
         nc.scalar.activation(warm[:], warm[:], ACT.Sigmoid)
-        identity = sb.tile([P, P], F32, name="identity")
+        identity = tile([P, P], F32, "identity")
         make_identity(nc, identity[:])
         nc.gpsimd.memset(wv_scale[:].bitcast(U32), 0)
 
-        for t in range(1, LANES):
-            nc.sync.dma_start(out=x_planes[t][:], in_=x_rows[:, t, :])
-            if t == 1:
-                for q in range(4):
-                    nc.sync.dma_start(
-                        out=wd_scale_raw[32 * q : 32 * q + 4, :].bitcast(I32),
-                        in_=wd_scales[0, 4 * q : 4 * q + 4, :].bitcast(I32),
-                    )
-        wd_raw = sb.tile([P, V], U16, name="wd_raw", tag="wd_raw", align_bytes=64)
-        nc.sync.dma_start(out=wd_raw[:].bitcast(I32), in_=wd_words[0].bitcast(I32))
         y_rows = y.rearrange("(o p r) i -> o p r i", p=P, r=LANES)
         y_tiles = {}
-        wv_sb = sb.tile([P, V_PASSES, D], U16, name="wv_sb", align_bytes=64)
         for h in range(2):
-            for o in range(V_PASSES):
-                if (h, o) == (1, 0):
-                    nc.sync.dma_start(out=wv_sb[:].bitcast(I32), in_=wv_words.bitcast(I32).rearrange("o p w -> p o w"))
-                    for q in range(4):
-                        nc.sync.dma_start(
-                            out=wv_scale[32 * q : 32 * q + 4, :, :].bitcast(I32),
-                            in_=wv_scales[:, 4 * q : 4 * q + 4, :].bitcast(I32).rearrange("o f w -> f o w"),
-                        )
-                y_tiles[h, o] = sb.tile([P, LANES, HALF], F32, name=f"y{h}{o}")
+            for o in (1, 0):
+                y_tiles[h, o] = tile([P, LANES, HALF], F32, f"y{h}{o}")
                 nc.sync.dma_start(out=y_tiles[h, o][:], in_=y_rows[o, :, :, HALF * h : HALF * (h + 1)])
-
-        neg_cw = sb.tile([P, V_PASSES * LANES], F32, name="neg_cw")
-        nc.scalar.activation(neg_cw[:], cw_sb[:].rearrange("p o r -> p (o r)"), ACT.Copy, scale=-1.0)
-
-        rw_bank = psum.tile([P, LANES, P], F32, name="rw_bank", tag="bank7")
-        for k in range(LANES):
-            nc.tensor.transpose(rw_bank[:, k, :], rw_cols[:, k : k + 1].to_broadcast([P, P]), identity[:])
-        outer = {}
-
-        def spread(h, factors, tag):
-            outer[h] = sb.tile([P, V_PASSES * LANES, HALF], F32, name="outer", tag=tag, align_bytes=64)
-            rows = slice(h * HALF // LANES, (h + 1) * HALF // LANES)
-            for k in range(V_PASSES * LANES):
-                nc.scalar.activation(
-                    outer[h][:, k, :].rearrange("p (n k) -> p n k", k=LANES),
-                    rw_bank[:].rearrange("p k n -> p n k")[:, rows, :],
-                    ACT.Copy,
-                    scale=factors[:, k : k + 1],
-                )
-
-        neg_cw_early = sb.tile([P, V_PASSES * LANES], F32, name="neg_cw_early", tag="x_woven0", align_bytes=64)
-        nc.scalar.activation(neg_cw_early[:], cw_sb[:].rearrange("p o r -> p (o r)"), ACT.Copy, scale=-1.0)
-        spread(0, neg_cw_early, "outer0")
+        wv_sb = tile([P, V_PASSES, D], U16, "wv_sb")
+        nc.sync.dma_start(out=wv_sb[:].bitcast(I32), in_=wv_words.bitcast(I32).rearrange("o p w -> p o w"))
+        for q in range(4):
+            nc.sync.dma_start(
+                out=wv_scale[32 * q : 32 * q + 4, :, :].bitcast(I32),
+                in_=wv_scales[:, 4 * q : 4 * q + 4, :].bitcast(I32).rearrange("o f w -> f o w"),
+            )
 
         windows = []
         for j in range(LANES):
             window = sb.tile([P, T], F32, name="window", tag=f"window{j}")
-            engine = nc.gpsimd if j == LANES - 1 else nc.vector
+            engine = nc.vector if j < V_CLEARS else nc.gpsimd
             engine.memset(window[:].bitcast(U32), 0)
             windows.append(window)
 
-        g_codes = [sb.tile([P, N], U32, name=f"g_codes{o}", align_bytes=64) for o in range(V_PASSES)]
-        g_scale = [sb.tile([P, N], U8, name=f"g_scale{o}", align_bytes=64) for o in range(V_PASSES)]
+        neg_cw = tile([P, V_PASSES * LANES], F32, "neg_cw")
+        nc.scalar.activation(neg_cw[:], cw_sb[:].rearrange("p o r -> p (o r)"), ACT.Copy, scale=-1.0)
+        rw_bank = bank([P, LANES, P], 7)
+        for k in range(LANES):
+            nc.tensor.transpose(rw_bank[:, k, :], rw_cols[:, k : k + 1].to_broadcast([P, P]), identity[:])
+        rw_rows = rw_bank[:].rearrange("p k n -> p n k")
 
-        def tile(shape, dtype, tag):
-            return sb.tile(shape, dtype, name="shared", tag=tag, align_bytes=64)
+        def by_four(run):
+            return run.rearrange("p (n k) -> p n k", k=LANES)
 
-        def gather(out, t, h):
-            nc.vector.tensor_copy(out, x_planes[t][:].indirect(listed(HALF * h, HALF)))
+        outer = tile([P, LANES, N], F32, "outer")
+        for r in range(LANES):
+            nc.scalar.activation(by_four(outer[:, r, :]), rw_rows, ACT.Copy, scale=neg_cw[:, r : r + 1])
+
+        wd_dealt = tile([P, V], U16, "wd_dealt")
+        deal(nc, wd_dealt[:], wd_raw[:])
+        wd_scale = tile([P, V], U8, "wd_scale")
+        deal(nc, wd_scale[:], wd_scale_raw[:])
 
         def walk_woven(woven):
             return woven.rearrange("p (c i) r -> p c r i", i=RUN)
@@ -134,196 +126,166 @@ def tile_attend_gml_pl_sig_kernel(
         def walk_lanes(lanes):
             return lanes.rearrange("p r (c i) -> p c r i", i=RUN)
 
-        x_scale = {}
-        x_codes = {}
+        def gather(out, t, first, count):
+            nc.vector.tensor_copy(out, x_planes[t][:].indirect(listed(first, count)))
 
-        def quantise_x(h, first, count, woven):
+        picked = tile([P, LANES, N], BF16, "picked")
+        for t in range(LANES - 1):
+            gather(picked[:, t, :], t, 0, N)
+        spans = ((0, P), (P, P), (HALF, HALF))
+        for first, count in spans:
+            gather(picked[:, LANES - 1, first : first + count], LANES - 1, first, count)
+
+        x_codes = tile([P, N], U32, "x_codes")
+        x_scale = tile([P, N], U8, "x_scale")
+        for k, (first, count) in enumerate(spans):
+            cols = slice(first, first + count)
+            woven = tile([P, count, LANES], BF16, f"x_woven{k}")
+            nc.scalar.copy(walk_woven(woven[:]), walk_lanes(picked[:, :, cols]))
             nc.vector.quantize_mx(
-                out=x_codes[h][:, first : first + count].bitcast(E4M3),
-                scales=x_scale[h][:, first : first + count],
+                out=x_codes[:, cols].bitcast(E4M3),
+                scales=x_scale[:, cols],
                 in_=woven[:].rearrange("p i t -> p (i t)"),
             )
 
-        early_x = tile([P, LANES, HALF], BF16, "early_x")
-        late_x = [tile([P, 2, HALF], BF16, "late_x0")[:]]
-        for t in range(LANES - 1):
-            gather(early_x[:, t, :], t, 0)
-            if t < 2:
-                gather(late_x[0][:, t, :], t, 1)
-        wd_scale = tile([P, V], U8, "x_plane1")
-        deal(nc, wd_scale[:], wd_scale_raw[:])
-        gather(early_x[:, LANES - 1, :], LANES - 1, 0)
-        wd_dealt = sb.tile([P, V], U16, name="wd_dealt", align_bytes=64)
-        deal(nc, wd_dealt[:], wd_raw[:])
-        x_codes[0] = tile([P, HALF], U32, "wd_raw")
-        x_scale[0] = tile([P, HALF], U8, "wd_scale_raw")
-        for b in range(2):
-            woven = tile([P, P, LANES], BF16, f"x_woven{b}")
-            nc.scalar.copy(walk_woven(woven[:]), walk_lanes(early_x[:, :, P * b : P * (b + 1)]))
-            quantise_x(0, P * b, P, woven)
-        late_x.append(tile([P, 2, HALF], BF16, "x_woven0")[:])
-        for t in range(2, LANES):
-            gather(late_x[1][:, t - 2, :], t, 1)
+        def block_cols(b):
+            return slice(P * (b % 2), P * (b % 2 + 1))
 
-        def lanes_of(flat):
-            return flat.rearrange("p (r i) -> p r i", i=HALF)
+        def scores(out, o, r, cols):
+            first = K_PASS * o + P * r
+            nc.tensor.matmul_mx(
+                out=out,
+                lhsT=wd_dealt[:, first : first + P].bitcast(E2M1),
+                lhsT_scale=wd_scale[:, first : first + P],
+                rhs=x_codes[:, cols].bitcast(E4M3),
+                rhs_scale=x_scale[:, cols],
+                start=True,
+                stop=True,
+            )
 
-        def score(h, o, pair, margin, sigmoid):
-            bank = psum.tile([P, 2, HALF], F32, name="score", tag=f"bank{4 * h + 2 * o + pair}")
-            width = P if (h, o, pair) == (0, 0, 0) else HALF
-            for col in range(0, HALF, width):
-                cols = slice(col, col + width)
+        def by_position(lanes):
+            return lanes.rearrange("p r i -> p i r")
+
+        sigmoids = {}
+        weights = {}
+
+        def weigh_pass0(b, tag):
+            weights[b, 0] = tile([P, LANES, P], F32, tag)[:]
+            nc.gpsimd.tensor_tensor(
+                weights[b, 0], y_tiles[b // 2, 0][:, :, block_cols(b)], outer[:, :, P * b : P * (b + 1)], MULT
+            )
+
+        def weigh_pass1(h):
+            weight = tile([P, LANES, HALF], F32, f"weight1{h}")
+            rows = slice(h * HALF // LANES, (h + 1) * HALF // LANES)
+            for r in range(LANES):
+                nc.vector.scalar_tensor_tensor(
+                    by_four(weight[:, r, :]),
+                    by_four(y_tiles[h, 1][:, r, :]),
+                    neg_cw[:, LANES + r : LANES + r + 1],
+                    rw_rows[:, rows, :],
+                    MULT,
+                    MULT,
+                )
+            for b in (2 * h, 2 * h + 1):
+                weights[b, 1] = weight[:, :, block_cols(b)]
+
+        def squash(b, o, margin):
+            if b == 0:
+                sigmoids[b, o] = tile([P, LANES, P], F32, f"sigmoid{b}{o}")[:]
+            else:
+                sigmoids[b, o] = tile([P, P, LANES], F32, f"sigmoid{b}{o}")[:]
+                margin = by_position(margin)
+            nc.scalar.activation(sigmoids[b, o], margin, ACT.Sigmoid, scale=-1.0)
+
+        def early_scores(b, o):
+            sums = bank([P, LANES, P], 2 * b + o)
+            for r in range(LANES):
+                scores(sums[:, r, :], o, r, slice(P * b, P * (b + 1)))
+            margin = tile([P, LANES, P], F32, f"margin{b}{o}")
+            nc.vector.tensor_tensor(margin[:], sums[:], y_tiles[0, o][:, :, block_cols(b)], MULT)
+            squash(b, o, margin[:])
+
+        def late_scores(o, banks):
+            margin = tile([P, LANES, HALF], F32, f"late_margin{o}")
+            for pair in range(2):
+                sums = bank([P, 2, HALF], banks[pair])
                 for e in range(2):
-                    first = K_PASS * o + P * (2 * pair + e)
-                    nc.tensor.matmul_mx(
-                        out=bank[:, e, cols],
-                        lhsT=wd_dealt[:, first : first + P].bitcast(E2M1),
-                        lhsT_scale=wd_scale[:, first : first + P],
-                        rhs=x_codes[h][:, cols].bitcast(E4M3),
-                        rhs_scale=x_scale[h][:, cols],
-                        start=True,
-                        stop=True,
+                    scores(sums[:, e, :], o, 2 * pair + e, slice(HALF, N))
+                rows = slice(2 * pair, 2 * pair + 2)
+                nc.vector.tensor_tensor(margin[:, rows, :], sums[:], y_tiles[1, o][:, rows, :], MULT)
+            for b in (2, 3):
+                squash(b, o, margin[:, :, block_cols(b)])
+
+        def products(b, tag):
+            woven = tile([P, V_PASSES, P, LANES], BF16, tag)
+            for o in range(V_PASSES):
+                if b == 0:
+                    nc.vector.tensor_tensor(
+                        walk_woven(woven[:, o]), walk_lanes(sigmoids[b, o]), walk_lanes(weights[b, o]), MULT
                     )
-            rows = slice(2 * pair, 2 * pair + 2)
-            nc.vector.tensor_tensor(margin, bank[:], y_tiles[h, o][:, rows, :], MULT)
-            nc.scalar.activation(sigmoid[:, rows, :], margin, ACT.Sigmoid, scale=-1.0)
+                else:
+                    nc.gpsimd.tensor_tensor(woven[:, o], sigmoids[b, o], by_position(weights[b, o]), MULT)
+                if (b, o) == (2, 0):
+                    weigh_pass0(3, "sigmoid20")
+            return woven
 
-        def weigh(engine, h, o, rows, weight):
-            engine.tensor_tensor(
-                weight[:, rows, :], y_tiles[h, o][:, rows, :], outer[h][:, LANES * o + rows.start : LANES * o + rows.stop, :], MULT
-            )
+        turned = {}
 
-        def product(woven, sigmoid, weight):
-            nc.vector.tensor_tensor(walk_woven(woven), walk_lanes(sigmoid), walk_lanes(weight), MULT)
-
-        def quantise_g(o, first, count, woven):
+        def back(b, woven, codes_tag, sums_bank, turned_banks):
+            codes = tile([P, V_PASSES * P], U32, codes_tag)
+            scale = tile([P, V_PASSES * P], U8, f"g_scale{b}")
             nc.vector.quantize_mx(
-                out=g_codes[o][:, first : first + count].bitcast(E5M2),
-                scales=g_scale[o][:, first : first + count],
-                in_=woven[:].rearrange("p i r -> p (i r)"),
+                out=codes[:].bitcast(E5M2), scales=scale[:], in_=woven[:].rearrange("p o i r -> p (o i r)")
             )
-
-        def back_early(block):
-            cols = slice(P * block, P * (block + 1))
-            sums = psum.tile([P, D], F32, name="sums", tag=f"bank{2 * block}")
+            sums = bank([P, D], sums_bank)
             for o in range(V_PASSES):
                 nc.tensor.matmul_mx(
                     out=sums[:],
-                    lhsT=g_codes[o][:, cols].bitcast(E5M2),
-                    lhsT_scale=g_scale[o][:, cols],
+                    lhsT=codes[:, P * o : P * (o + 1)].bitcast(E5M2),
+                    lhsT_scale=scale[:, P * o : P * (o + 1)],
                     rhs=wv_sb[:, o, :].bitcast(E2M1),
                     rhs_scale=wv_scale[:, o, :],
                     start=(o == 0),
                     stop=(o == V_PASSES - 1),
                 )
-            by_lane = sb.tile([P, LANES, P], F32, name=f"by_lane{block}")
-            for pair in range(2):
-                lanes = slice(2 * pair, 2 * pair + 2)
-                nc.scalar.copy(by_lane[:, lanes, :], sums[:].rearrange("p (m j) -> p j m", j=LANES)[:, lanes, :])
-            turned = psum.tile([P, LANES, P], F32, name="turned", tag=f"bank{2 * block + 1}")
-            for j in range(LANES):
-                nc.tensor.transpose(turned[:, j, :], by_lane[:, j, :], identity[:])
-            return turned
-
-        wv_tiles = {}
-
-        def deal_wv(parity, words_tag, scales_tag):
-            words = tile([P, V_PASSES, 2, P], U16, words_tag)
-            scales = tile([P, V_PASSES, 2, P], U8, scales_tag)
-            for dealt, raw in ((words, wv_sb), (scales, wv_scale)):
-                nc.vector.tensor_copy(
-                    dealt[:], raw[:].rearrange("p o (m k e) -> p o k m e", k=2, e=2)[:, :, :, :, parity]
-                )
-            for k in range(2):
-                wv_tiles[2 * k + parity] = (words, scales, k)
-
-        def back(j, bank):
-            words, scales, k = wv_tiles[j]
-            sums = psum.tile([P, N], F32, name="sums", tag=f"bank{bank}")
-            for o in range(V_PASSES):
-                nc.tensor.matmul_mx(
-                    out=sums[:],
-                    lhsT=words[:, o, k, :].bitcast(E2M1),
-                    lhsT_scale=scales[:, o, k, :],
-                    rhs=g_codes[o][:].bitcast(E5M2),
-                    rhs_scale=g_scale[o][:],
-                    start=(o == 0),
-                    stop=(o == V_PASSES - 1),
-                )
-            return sums
-
-        def drain(sums, first, count, tag):
-            dx = tile([P, count], F32, tag)
-            nc.scalar.copy(dx[:], sums[:, first : first + count])
-            return dx
+            by_lane = tile([P, 2, 2, P], F32, f"by_lane{b}")
+            for odd in range(2):
+                nc.scalar.copy(by_lane[:, odd], sums[:].rearrange("p (m k e) -> p e k m", k=2, e=2)[:, odd])
+            banks = [bank([P, LANES, P], number) for number in turned_banks]
+            for odd in range(2):
+                for k in range(2):
+                    j = 2 * k + odd
+                    turned[b, j] = banks[odd % len(banks)][:, j, :]
+                    nc.tensor.transpose(turned[b, j], by_lane[:, odd, k, :], identity[:])
 
         def scatter(j, dx, first, count):
             nc.vector.tensor_copy(windows[j][:].indirect(listed(first, count)), dx)
 
-        first_pair, second_pair, all_lanes = slice(0, 2), slice(2, LANES), slice(0, LANES)
+        def release(parts, tag):
+            dx = tile([P, len(parts), P], F32, tag)
+            for k, (b, j) in enumerate(parts):
+                nc.scalar.copy(dx[:, k, :], turned[b, j])
+            for k, (b, j) in enumerate(parts):
+                scatter(j, dx[:, k, :], P * b, P)
 
-        weights = [tile([P, LANES, HALF], F32, "x_woven1")[:]]
-        weigh(nc.gpsimd, 0, 0, first_pair, weights[0])
-        weigh(nc.gpsimd, 0, 0, second_pair, weights[0])
-        late_woven = tile([P, HALF, LANES], BF16, "early_x")
-        for pair in range(2):
-            nc.scalar.copy(walk_woven(late_woven[:, :, 2 * pair : 2 * pair + 2]), walk_lanes(late_x[pair]))
-        sigmoids = [tile([P, LANES, HALF], F32, tag) for tag in ("late_x0", "x_woven0")]
-        for o in range(V_PASSES):
-            for pair in range(2):
-                score(0, o, pair, tile([P, 2, HALF], F32, f"margin{o}{pair}")[:], sigmoids[o])
-        weights.append(tile([P, LANES, HALF], F32, "margin00")[:])
-        weigh(nc.vector, 0, 1, all_lanes, weights[1])
-        x_codes[1] = tile([P, HALF], U32, "margin01")
-        x_scale[1] = tile([P, HALF], U8, "x_scale1")
-        quantise_x(1, 0, HALF, late_woven)
-        deal_wv(0, "margin10", "wd_raw")
-        spread(1, neg_cw, "margin11")
-        turned = []
-        for block, tags in enumerate((("early_x", "g_woven01"), ("g_woven10", "g_woven11"))):
-            cols = slice(P * block, P * (block + 1))
-            woven = [tile([P, P, LANES], BF16, tag) for tag in tags]
-            for o in range(V_PASSES):
-                product(woven[o][:], sigmoids[o][:, :, cols], weights[o][:, :, cols])
-            for o in range(V_PASSES):
-                quantise_g(o, P * block, P, woven[o])
-            turned.append(back_early(block))
-        early_dx = [sb.tile([P, LANES, P], F32, name=f"early_dx{block}") for block in range(2)]
-        nc.scalar.copy(early_dx[0][:], turned[0][:])
-
-        unit = 2 * HALF
-        stage = tile([P, 8 * unit], F32, "g_woven11")
-        weights = [lanes_of(stage[:, 2 * unit * o : 2 * unit * (o + 1)]) for o in range(V_PASSES)]
-        weigh(nc.gpsimd, 1, 0, first_pair, weights[0])
-        weigh(nc.gpsimd, 1, 0, second_pair, weights[0])
-        weigh(nc.gpsimd, 1, 1, first_pair, weights[1])
-        weigh(nc.gpsimd, 1, 1, second_pair, weights[1])
-        sigmoids = [tile([P, LANES, HALF], F32, f"sigmoid1{o}") for o in range(V_PASSES)]
-        for o in range(V_PASSES):
-            for pair in range(2):
-                k = 4 + 2 * o + pair
-                score(1, o, pair, lanes_of(stage[:, unit * k : unit * (k + 1)]), sigmoids[o])
-        held = LANES - 2
-        nc.scalar.copy(early_dx[1][:, 0:held, :], turned[1][:, 0:held, :])
-        for j in range(LANES):
-            scatter(j, early_dx[0][:, j, :], 0, P)
-        for j in range(held):
-            scatter(j, early_dx[1][:, j, :], P, P)
-        woven = [tile([P, HALF, LANES], BF16, f"late_woven{o}") for o in range(V_PASSES)]
-        for o, b in ((0, 0), (0, 1)):
-            cols = slice(P * b, P * (b + 1))
-            lanes = sb.tile([P, LANES, P], BF16, name=f"lanes{o}{b}")
-            nc.gpsimd.tensor_tensor(lanes[:], sigmoids[o][:, :, cols], weights[o][:, :, cols], MULT)
-            nc.scalar.copy(walk_woven(woven[o][:, cols, :]), walk_lanes(lanes[:]))
-        product(woven[1][:], sigmoids[1][:], weights[1])
-        for o in range(V_PASSES):
-            quantise_g(o, HALF, HALF, woven[o])
-        held_dx = tile([P, LANES - held, P], F32, "late_woven1")
-        nc.scalar.copy(held_dx[:], turned[1][:, held:, :])
-        deal_wv(1, "late_woven0", "sigmoid11")
-        sums = {j: back(j, bank) for j, bank in ((0, 4), (2, 5), (3, 6), (1, 7))}
-        for j in range(held, LANES):
-            scatter(j, held_dx[:, j - held, :], P, P)
+        weigh_pass0(0, "x_woven1")
+        weigh_pass0(1, "weight01")
+        weigh_pass0(2, "weight02")
+        weigh_pass1(0)
+        for b in range(2):
+            for o in (1, 0):
+                early_scores(b, o)
+        late_scores(1, (4, 5))
+        back(0, products(0, "g_woven0"), "g_codes0", 1, (2,))
+        late_scores(0, (6, 0))
+        weigh_pass1(1)
+        back(1, products(1, "g_woven0"), "g_codes1", 3, (4,))
+        release(((0, 0), (0, 1), (0, 2), (0, 3)), "sigmoid11")
+        back(2, products(2, "g_woven2"), "sigmoid11", 1, (5,))
+        release(((1, 0), (1, 1), (1, 2), (1, 3)), "sigmoid21")
+        back(3, products(3, "g_woven3"), "sigmoid21", 3, (6, 0))
+        release(((2, 2), (2, 0), (2, 3), (2, 1)), "sigmoid31")
 
         out_rows = out_0.rearrange("(p j) c -> p j c", j=LANES)
         pieces = tuple((first, 256) for first in range(0, T, 256))
@@ -333,18 +295,19 @@ def tile_attend_gml_pl_sig_kernel(
             first, width = pieces[k]
             engine_copy(pairs[k][:, j // 2, :, j % 2], windows[j][:, first : first + width])
 
-        spans = {j: (HALF, HALF) for j in range(LANES)}
-        last = 1
-        late_dx = {j: drain(sums[j], *spans[j], f"dx{j}") for j in (0, 2, 3)}
-        for j in (0, 2, 3):
-            scatter(j, late_dx[j][:], *spans[j])
+        def finish(j):
             nc.sync.dma_start(out=out_rows[:, j, :], in_=windows[j][:])
-            for k in range(len(pieces)):
+
+        def round_on_gpsimd(out, in_):
+            nc.gpsimd.tensor_scalar(out, in_, 1.0, 0.0, MULT, ADD)
+
+        release(((3, 2), (3, 0), (3, 3), (3, 1)), "dx3")
+        for j in (2, 0, 3, 1):
+            finish(j)
+            for k in (2, 3):
                 round_lane(nc.scalar.copy, j, k)
-            if j == 0:
-                late_dx[last] = drain(sums[last], *spans[last], "dx0")
-        scatter(last, late_dx[last][:], *spans[last])
-        nc.sync.dma_start(out=out_rows[:, last, :], in_=windows[last][:])
+            for k in (0, 1):
+                round_lane(round_on_gpsimd if j >= 2 else nc.vector.tensor_copy, j, k)
 
         out_scale = sb.tile([P, T], U8, name="out_scale", align_bytes=64)
         out_words = out_1[0].rearrange("p c t -> p (c t)").bitcast(I32)
@@ -358,9 +321,6 @@ def tile_attend_gml_pl_sig_kernel(
                 pairs[k][:].rearrange("p h c e -> p h (c e)").bitcast(word).rearrange("p h c -> p c h"),
             )
 
-        for k in (0, 1, 2):
-            round_lane(nc.vector.tensor_copy, last, k)
-        round_lane(nc.scalar.copy, last, 3)
         for k in (0, 1):
             join_pairs(nc.vector.tensor_copy, I32, k)
         for k in (2, 3):

@@ -41,12 +41,20 @@ def tile_attend_gml_pl_sig_kernel(
     nc = tc.nc
     with ExitStack() as ctx:
         sb = ctx.enter_context(tc.tile_pool(name="sb", bufs=1))
+        laid = ctx.enter_context(tc.tile_pool(name="laid", bufs=1))
         psum = ctx.enter_context(tc.psum_pool(name="psum", bufs=1))
 
         def listed(first, count):
             return offsets[:, first // 16 : (first + count) // 16]
 
+        places = {
+            "g_woven3": 0, "g_woven2_after": 1024, "g_woven2": 2048, "g_woven0": 4032, "g_woven1": 4032,
+            "dx0": 6016, "g_codes2": 5056, "g_codes3": 6528,
+        }
+
         def tile(shape, dtype, tag):
+            if tag in places:
+                return laid.tile(shape, dtype, name="laid", tag=tag, align_bytes=64, offset=places[tag])
             return sb.tile(shape, dtype, name="shared", tag=tag, align_bytes=64)
 
         def bank(shape, number):
@@ -65,7 +73,8 @@ def tile_attend_gml_pl_sig_kernel(
         offsets = sb.tile([P, N // 16], U16, name="offsets")
         nc.sync.dma_start(offsets[:], offs)
         rw_cols = tile([P, LANES], F32, "rw_cols")
-        nc.sync.dma_start(out=rw_cols[:], in_=rw[0].rearrange("(p k) -> p k", k=LANES))
+        with nc.allow_non_contiguous_dma(reason="one weight a partition"):
+            nc.sync.dma_start(out=rw_cols[:], in_=rw[0].rearrange("(k p) -> p k", p=P))
         x_rows = xT.rearrange("(p t) c -> p t c", t=LANES)
         x_planes = [tile([P, T], F32, f"x_plane{t}") for t in range(LANES)]
         nc.sync.dma_start(out=x_planes[0][:], in_=x_rows[:, 0, :])
@@ -82,10 +91,9 @@ def tile_attend_gml_pl_sig_kernel(
 
         y_rows = y.rearrange("(o p r) i -> o p r i", p=P, r=LANES)
         y_tiles = {}
-        for h in range(2):
-            for o in (1, 0):
-                y_tiles[h, o] = tile([P, LANES, HALF], F32, f"y{h}{o}")
-                nc.sync.dma_start(out=y_tiles[h, o][:], in_=y_rows[o, :, :, HALF * h : HALF * (h + 1)])
+        for h, o in ((0, 1), (0, 0), (1, 1), (1, 0)):
+            y_tiles[h, o] = tile([P, LANES, HALF], F32, f"y{h}{o}")
+            nc.sync.dma_start(out=y_tiles[h, o][:], in_=y_rows[o, :, :, HALF * h : HALF * (h + 1)])
         wv_sb = tile([P, V_PASSES, D], U16, "wv_sb")
         nc.sync.dma_start(out=wv_sb[:].bitcast(I32), in_=wv_words.bitcast(I32).rearrange("o p w -> p o w"))
         for q in range(4):
@@ -106,14 +114,14 @@ def tile_attend_gml_pl_sig_kernel(
         rw_bank = bank([P, LANES, P], 7)
         for k in range(LANES):
             nc.tensor.transpose(rw_bank[:, k, :], rw_cols[:, k : k + 1].to_broadcast([P, P]), identity[:])
-        rw_rows = rw_bank[:].rearrange("p k n -> p n k")
-
-        def by_four(run):
-            return run.rearrange("p (n k) -> p n k", k=LANES)
-
-        outer = tile([P, LANES, N], F32, "outer")
-        for r in range(LANES):
-            nc.scalar.activation(by_four(outer[:, r, :]), rw_rows, ACT.Copy, scale=neg_cw[:, r : r + 1])
+        rw_rows = rw_bank[:].rearrange("p k n -> p (k n)")
+        outer = {}
+        for first, count in ((0, P), (P, HALF)):
+            part = tile([P, LANES, count], F32, f"outer{first}")
+            for r in range(LANES):
+                nc.scalar.activation(part[:, r, :], rw_rows[:, first : first + count], ACT.Copy, scale=neg_cw[:, r : r + 1])
+            for b in range(first // P, (first + count) // P):
+                outer[b] = part[:, :, P * b - first : P * (b + 1) - first]
 
         wd_dealt = tile([P, V], U16, "wd_dealt")
         deal(nc, wd_dealt[:], wd_raw[:])
@@ -129,6 +137,8 @@ def tile_attend_gml_pl_sig_kernel(
         def gather(out, t, first, count):
             nc.vector.tensor_copy(out, x_planes[t][:].indirect(listed(first, count)))
 
+        sigmoids = {}
+        weights = {}
         picked = tile([P, LANES, N], BF16, "picked")
         for t in range(LANES - 1):
             gather(picked[:, t, :], t, 0, N)
@@ -136,14 +146,17 @@ def tile_attend_gml_pl_sig_kernel(
         for first, count in spans:
             gather(picked[:, LANES - 1, first : first + count], LANES - 1, first, count)
 
-        x_codes = tile([P, N], U32, "x_codes")
+        x_codes = {}
         x_scale = tile([P, N], U8, "x_scale")
-        for k, (first, count) in enumerate(spans):
+
+        def quantise_x(k, tag):
+            first, count = spans[k]
             cols = slice(first, first + count)
             woven = tile([P, count, LANES], BF16, f"x_woven{k}")
             nc.scalar.copy(walk_woven(woven[:]), walk_lanes(picked[:, :, cols]))
+            x_codes[first] = tile([P, count], U32, tag)[:]
             nc.vector.quantize_mx(
-                out=x_codes[:, cols].bitcast(E4M3),
+                out=x_codes[first].bitcast(E4M3),
                 scales=x_scale[:, cols],
                 in_=woven[:].rearrange("p i t -> p (i t)"),
             )
@@ -157,7 +170,7 @@ def tile_attend_gml_pl_sig_kernel(
                 out=out,
                 lhsT=wd_dealt[:, first : first + P].bitcast(E2M1),
                 lhsT_scale=wd_scale[:, first : first + P],
-                rhs=x_codes[:, cols].bitcast(E4M3),
+                rhs=x_codes[cols.start].bitcast(E4M3),
                 rhs_scale=x_scale[:, cols],
                 start=True,
                 stop=True,
@@ -166,32 +179,49 @@ def tile_attend_gml_pl_sig_kernel(
         def by_position(lanes):
             return lanes.rearrange("p r i -> p i r")
 
-        sigmoids = {}
-        weights = {}
-
         def weigh_pass0(b, tag):
             weights[b, 0] = tile([P, LANES, P], F32, tag)[:]
             nc.gpsimd.tensor_tensor(
-                weights[b, 0], y_tiles[b // 2, 0][:, :, block_cols(b)], outer[:, :, P * b : P * (b + 1)], MULT
+                weights[b, 0], y_tiles[b // 2, 0][:, :, block_cols(b)], outer[b], MULT
             )
 
-        def weigh_pass1(h):
-            weight = tile([P, LANES, HALF], F32, f"weight1{h}")
-            rows = slice(h * HALF // LANES, (h + 1) * HALF // LANES)
+        def weigh_pass1(first, count):
+            h, start = divmod(first, HALF)
+            weight = tile([P, LANES, count], F32, f"weight1{h}")
             for r in range(LANES):
                 nc.vector.scalar_tensor_tensor(
-                    by_four(weight[:, r, :]),
-                    by_four(y_tiles[h, 1][:, r, :]),
+                    weight[:, r, :],
+                    y_tiles[h, 1][:, r, start : start + count],
                     neg_cw[:, LANES + r : LANES + r + 1],
-                    rw_rows[:, rows, :],
+                    rw_rows[:, first : first + count],
                     MULT,
                     MULT,
                 )
-            for b in (2 * h, 2 * h + 1):
-                weights[b, 1] = weight[:, :, block_cols(b)]
+            for k in range(count // P):
+                weights[first // P + k, 1] = weight[:, :, P * k : P * (k + 1)]
+
+        def weigh_through_psum(b, o, stage_bank, weight_bank):
+            scaled = tile([P, LANES, P], F32, f"scaled_labels{o}")
+            for r in range(LANES):
+                k = LANES * o + r
+                nc.scalar.activation(
+                    scaled[:, r, :], y_tiles[b // 2, o][:, r, block_cols(b)], ACT.Copy, scale=neg_cw[:, k : k + 1]
+                )
+            stage = bank([P, LANES, P], stage_bank)
+            for r in range(LANES):
+                nc.tensor.transpose(stage[:, r, :], scaled[:, r, :], identity[:])
+            rows = tile([P, LANES, P], F32, f"weight_rows{o}")
+            nc.scalar.activation(rows[:], stage[:], ACT.Copy, scale=rw_cols[:, b : b + 1])
+            weight = bank([P, LANES, P], weight_bank)
+            for r in range(LANES):
+                nc.tensor.transpose(weight[:, r, :], rows[:, r, :], identity[:])
+            weights[b, o] = weight[:]
+
+        def on_vector(b, o):
+            return b in (0, 3)
 
         def squash(b, o, margin):
-            if b == 0:
+            if on_vector(b, o):
                 sigmoids[b, o] = tile([P, LANES, P], F32, f"sigmoid{b}{o}")[:]
             else:
                 sigmoids[b, o] = tile([P, P, LANES], F32, f"sigmoid{b}{o}")[:]
@@ -214,26 +244,23 @@ def tile_attend_gml_pl_sig_kernel(
                     scores(sums[:, e, :], o, 2 * pair + e, slice(HALF, N))
                 rows = slice(2 * pair, 2 * pair + 2)
                 nc.vector.tensor_tensor(margin[:, rows, :], sums[:], y_tiles[1, o][:, rows, :], MULT)
-            for b in (2, 3):
-                squash(b, o, margin[:, :, block_cols(b)])
+            return margin
 
         def products(b, tag):
             woven = tile([P, V_PASSES, P, LANES], BF16, tag)
-            for o in range(V_PASSES):
-                if b == 0:
+            for o in (0, 1) if b == 2 else (1, 0):
+                if on_vector(b, o):
                     nc.vector.tensor_tensor(
                         walk_woven(woven[:, o]), walk_lanes(sigmoids[b, o]), walk_lanes(weights[b, o]), MULT
                     )
                 else:
                     nc.gpsimd.tensor_tensor(woven[:, o], sigmoids[b, o], by_position(weights[b, o]), MULT)
-                if (b, o) == (2, 0):
-                    weigh_pass0(3, "sigmoid20")
             return woven
 
         turned = {}
 
-        def back(b, woven, codes_tag, sums_bank, turned_banks):
-            codes = tile([P, V_PASSES * P], U32, codes_tag)
+        def back(b, woven, sums_bank, turned_banks):
+            codes = tile([P, V_PASSES * P], U32, f"g_codes{b}")
             scale = tile([P, V_PASSES * P], U8, f"g_scale{b}")
             nc.vector.quantize_mx(
                 out=codes[:].bitcast(E5M2), scales=scale[:], in_=woven[:].rearrange("p o i r -> p (o i r)")
@@ -269,23 +296,35 @@ def tile_attend_gml_pl_sig_kernel(
             for k, (b, j) in enumerate(parts):
                 scatter(j, dx[:, k, :], P * b, P)
 
+        quantise_x(0, "x_codes0")
+        quantise_x(1, "x_codes1")
         weigh_pass0(0, "x_woven1")
-        weigh_pass0(1, "weight01")
-        weigh_pass0(2, "weight02")
-        weigh_pass1(0)
-        for b in range(2):
-            for o in (1, 0):
-                early_scores(b, o)
-        late_scores(1, (4, 5))
-        back(0, products(0, "g_woven0"), "g_codes0", 1, (2,))
-        late_scores(0, (6, 0))
-        weigh_pass1(1)
-        back(1, products(1, "g_woven0"), "g_codes1", 3, (4,))
-        release(((0, 0), (0, 1), (0, 2), (0, 3)), "sigmoid11")
-        back(2, products(2, "g_woven2"), "sigmoid11", 1, (5,))
-        release(((1, 0), (1, 1), (1, 2), (1, 3)), "sigmoid21")
-        back(3, products(3, "g_woven3"), "sigmoid21", 3, (6, 0))
-        release(((2, 2), (2, 0), (2, 3), (2, 1)), "sigmoid31")
+        weigh_pass1(0, HALF)
+        for o in (1, 0):
+            early_scores(0, o)
+        quantise_x(2, "outer0")
+        weigh_pass0(1, "x_woven2")
+        weigh_pass0(2, "weight20")
+        for o in (1, 0):
+            early_scores(1, o)
+        margins = {1: late_scores(1, (4, 5))}
+        woven = products(0, "g_woven0")
+        back(0, woven, 1, (2,))
+        margins[0] = late_scores(0, (6, 0))
+        weigh_pass1(HALF, P)
+        for o in (0, 1):
+            squash(2, o, margins[o][:, :, block_cols(2)])
+        release(((0, 0),), "dx00")
+        for o, banks in ((1, (3, 5)), (0, (4, 6))):
+            weigh_through_psum(3, o, *banks)
+        for o in (1, 0):
+            squash(3, o, margins[o][:, :, block_cols(3)])
+        back(1, products(1, "g_woven1"), 3, (4,))
+        release(((0, 1), (0, 2), (0, 3)), "dx0")
+        woven = products(2, "g_woven2")
+        back(3, products(3, "g_woven3"), 1, (0,))
+        back(2, woven, 3, (2,))
+        release(((1, 0), (1, 1), (1, 2), (1, 3)), "g_woven2_after")
 
         out_rows = out_0.rearrange("(p j) c -> p j c", j=LANES)
         pieces = tuple((first, 256) for first in range(0, T, 256))
@@ -298,16 +337,23 @@ def tile_attend_gml_pl_sig_kernel(
         def finish(j):
             nc.sync.dma_start(out=out_rows[:, j, :], in_=windows[j][:])
 
-        def round_on_gpsimd(out, in_):
-            nc.gpsimd.tensor_scalar(out, in_, 1.0, 0.0, MULT, ADD)
+        def late_half(j, tag):
+            dx = tile([P, 2, P], F32, tag)
+            for b in (2, 3):
+                nc.scalar.copy(dx[:, b - 2, :], turned[b, j])
+            return dx[:].rearrange("p b i -> p (b i)")
 
-        release(((3, 2), (3, 0), (3, 3), (3, 1)), "dx3")
-        for j in (2, 0, 3, 1):
+        last = 1
+        late_dx = {j: late_half(j, f"late_dx{j}") for j in (0, 2, 3)}
+        for j in (0, 2, 3):
+            scatter(j, late_dx[j], HALF, HALF)
             finish(j)
-            for k in (2, 3):
+            for k in range(len(pieces)):
                 round_lane(nc.scalar.copy, j, k)
-            for k in (0, 1):
-                round_lane(round_on_gpsimd if j >= 2 else nc.vector.tensor_copy, j, k)
+            if j == 0:
+                late_dx[last] = late_half(last, "late_dx0")
+        scatter(last, late_dx[last], HALF, HALF)
+        finish(last)
 
         out_scale = sb.tile([P, T], U8, name="out_scale", align_bytes=64)
         out_words = out_1[0].rearrange("p c t -> p (c t)").bitcast(I32)
@@ -321,6 +367,9 @@ def tile_attend_gml_pl_sig_kernel(
                 pairs[k][:].rearrange("p h c e -> p h (c e)").bitcast(word).rearrange("p h c -> p c h"),
             )
 
+        for k in (0, 1, 2):
+            round_lane(nc.vector.tensor_copy, last, k)
+        round_lane(nc.scalar.copy, last, 3)
         for k in (0, 1):
             join_pairs(nc.vector.tensor_copy, I32, k)
         for k in (2, 3):

@@ -218,7 +218,7 @@ def tile_attend_gml_pl_sig_kernel(
             weights[b, o] = weight[:]
 
         def on_vector(b, o):
-            return b in (0, 3)
+            return b in (0, 3) or (b, o) == (1, 1)
 
         def squash(b, o, margin):
             if on_vector(b, o):
@@ -237,18 +237,21 @@ def tile_attend_gml_pl_sig_kernel(
             squash(b, o, margin[:])
 
         def late_scores(o, banks):
+            sums = [bank([P, 2, HALF], number) for number in banks]
+            for r in range(LANES):
+                scores(sums[r // 2][:, r % 2, :], o, r, slice(HALF, N))
+            return sums
+
+        def late_margins(o, sums):
             margin = tile([P, LANES, HALF], F32, f"late_margin{o}")
             for pair in range(2):
-                sums = bank([P, 2, HALF], banks[pair])
-                for e in range(2):
-                    scores(sums[:, e, :], o, 2 * pair + e, slice(HALF, N))
                 rows = slice(2 * pair, 2 * pair + 2)
-                nc.vector.tensor_tensor(margin[:, rows, :], sums[:], y_tiles[1, o][:, rows, :], MULT)
+                nc.vector.tensor_tensor(margin[:, rows, :], sums[pair][:], y_tiles[1, o][:, rows, :], MULT)
             return margin
 
         def products(b, tag):
             woven = tile([P, V_PASSES, P, LANES], BF16, tag)
-            for o in (0, 1) if b == 2 else (1, 0):
+            for o in (0, 1) if b == 1 else (1, 0):
                 if on_vector(b, o):
                     nc.vector.tensor_tensor(
                         walk_woven(woven[:, o]), walk_lanes(sigmoids[b, o]), walk_lanes(weights[b, o]), MULT
@@ -307,12 +310,13 @@ def tile_attend_gml_pl_sig_kernel(
         weigh_pass0(2, "weight20")
         for o in (1, 0):
             early_scores(1, o)
-        margins = {1: late_scores(1, (4, 5))}
+        margins = {1: late_margins(1, late_scores(1, (4, 5)))}
+        late_sums = late_scores(0, (6, 0))
         woven = products(0, "g_woven0")
         back(0, woven, 1, (2,))
-        margins[0] = late_scores(0, (6, 0))
+        margins[0] = late_margins(0, late_sums)
         weigh_pass1(HALF, P)
-        for o in (0, 1):
+        for o in (1, 0):
             squash(2, o, margins[o][:, :, block_cols(2)])
         release(((0, 0),), "dx00")
         for o, banks in ((1, (3, 5)), (0, (4, 6))):
@@ -343,15 +347,22 @@ def tile_attend_gml_pl_sig_kernel(
                 nc.scalar.copy(dx[:, b - 2, :], turned[b, j])
             return dx[:].rearrange("p b i -> p (b i)")
 
+        def round_on_gpsimd(out, in_):
+            nc.gpsimd.tensor_scalar(out, in_, 1.0, 0.0, MULT, ADD)
+
         last = 1
-        late_dx = {j: late_half(j, f"late_dx{j}") for j in (0, 2, 3)}
-        for j in (0, 2, 3):
+        release(((3, 0),), "dx30")
+        release(((2, 0),), "late_dx0")
+        late_dx = {j: late_half(j, f"late_dx{j}") for j in (2, 3)}
+        finish(0)
+        for k in range(len(pieces)):
+            round_lane(nc.scalar.copy, 0, k)
+        late_dx[last] = late_half(last, "late_dx0")
+        for j in (2, 3):
             scatter(j, late_dx[j], HALF, HALF)
             finish(j)
             for k in range(len(pieces)):
-                round_lane(nc.scalar.copy, j, k)
-            if j == 0:
-                late_dx[last] = late_half(last, "late_dx0")
+                round_lane(round_on_gpsimd if k < 2 else nc.scalar.copy, j, k)
         scatter(last, late_dx[last], HALF, HALF)
         finish(last)
 
@@ -374,16 +385,20 @@ def tile_attend_gml_pl_sig_kernel(
             join_pairs(nc.vector.tensor_copy, I32, k)
         for k in (2, 3):
             join_pairs(nc.scalar.copy, U32, k)
+        out_codes = sb.tile([P, T], U32, name="out_codes", align_bytes=64)
+        stored = 0
         for k in range(len(pieces)):
             first, width = pieces[k]
             cols = slice(first, first + width)
-            out_codes = sb.tile([P, width], U32, name=f"out_codes{first}", align_bytes=64)
             nc.vector.quantize_mx(
-                out=out_codes[:].bitcast(E4M3),
+                out=out_codes[:, cols].bitcast(E4M3),
                 scales=out_scale[:, cols],
                 in_=woven_out[k][:].rearrange("p c j -> p (c j)"),
             )
-            nc.sync.dma_start(out=out_words[:, cols], in_=out_codes[:].bitcast(I32))
+            if k > 0:
+                cols = slice(stored, first + width)
+                nc.sync.dma_start(out=out_words[:, cols], in_=out_codes[:, cols].bitcast(I32))
+                stored = first + width
         for q in range(4):
             queue = nc.scalar if q % 2 == 0 else nc.sync
             queue.dma_start(

@@ -25,7 +25,6 @@ K_PASS = P * LANES
 V_PASSES = V // K_PASS
 RUN = 4
 HALF = N // 2
-V_CLEARS = 2
 
 
 def deal(nc, out, in_):
@@ -72,15 +71,14 @@ def tile_attend_gml_pl_sig_kernel(
         nc.sync.dma_start(out=wd_raw[:].bitcast(I32), in_=wd_words[0].bitcast(I32))
         offsets = sb.tile([P, N // 16], U16, name="offsets")
         nc.sync.dma_start(offsets[:], offs)
-        rw_cols = tile([P, LANES], F32, "rw_cols")
-        with nc.allow_non_contiguous_dma(reason="one weight a partition"):
-            nc.sync.dma_start(out=rw_cols[:], in_=rw[0].rearrange("(k p) -> p k", p=P))
         x_rows = xT.rearrange("(p t) c -> p t c", t=LANES)
         x_planes = [tile([P, T], F32, f"x_plane{t}") for t in range(LANES)]
-        nc.sync.dma_start(out=x_planes[0][:], in_=x_rows[:, 0, :])
+        rw_cols = tile([P, LANES], F32, "rw_cols")
         cw_sb = tile([P, V_PASSES, LANES], F32, "cw_sb")
-        nc.sync.dma_start(out=cw_sb[:], in_=cw.rearrange("(o p r) one -> p o (r one)", p=P, r=LANES))
-        for t in range(1, LANES):
+        for t in range(LANES):
+            if t == 2:
+                nc.sync.dma_start(out=rw_cols[:], in_=rw[0].rearrange("(p k) -> p k", k=LANES))
+                nc.sync.dma_start(out=cw_sb[:], in_=cw.rearrange("(o p r) one -> p o (r one)", p=P, r=LANES))
             nc.sync.dma_start(out=x_planes[t][:], in_=x_rows[:, t, :])
         warm = tile([P, 8], F32, "warm")
         nc.vector.memset(warm[:], 0.0)
@@ -94,6 +92,9 @@ def tile_attend_gml_pl_sig_kernel(
         for h, o in ((0, 1), (0, 0), (1, 1), (1, 0)):
             y_tiles[h, o] = tile([P, LANES, HALF], F32, f"y{h}{o}")
             nc.sync.dma_start(out=y_tiles[h, o][:], in_=y_rows[o, :, :, HALF * h : HALF * (h + 1)])
+        rw_last = tile([P, 1], F32, "rw_last")
+        with nc.allow_non_contiguous_dma(reason="one weight a partition"):
+            nc.sync.dma_start(out=rw_last[:], in_=rw[0, N - P :].rearrange("(p one) -> p one", one=1))
         wv_sb = tile([P, V_PASSES, D], U16, "wv_sb")
         nc.sync.dma_start(out=wv_sb[:].bitcast(I32), in_=wv_words.bitcast(I32).rearrange("o p w -> p o w"))
         for q in range(4):
@@ -102,24 +103,23 @@ def tile_attend_gml_pl_sig_kernel(
                 in_=wv_scales[:, 4 * q : 4 * q + 4, :].bitcast(I32).rearrange("o f w -> f o w"),
             )
 
-        windows = []
-        for j in range(LANES):
-            window = sb.tile([P, T], F32, name="window", tag=f"window{j}")
-            engine = nc.vector if j < V_CLEARS else nc.gpsimd
-            engine.memset(window[:].bitcast(U32), 0)
-            windows.append(window)
-
         neg_cw = tile([P, V_PASSES * LANES], F32, "neg_cw")
         nc.scalar.activation(neg_cw[:], cw_sb[:].rearrange("p o r -> p (o r)"), ACT.Copy, scale=-1.0)
         rw_bank = bank([P, LANES, P], 7)
         for k in range(LANES):
             nc.tensor.transpose(rw_bank[:, k, :], rw_cols[:, k : k + 1].to_broadcast([P, P]), identity[:])
-        rw_rows = rw_bank[:].rearrange("p k n -> p (k n)")
+
+        def rw_rows(first, count):
+            return rw_bank[:].rearrange("p k n -> p n k")[:, first // LANES : (first + count) // LANES, :]
+
+        def by_four(run):
+            return run.rearrange("p (n k) -> p n k", k=LANES)
+
         outer = {}
         for first, count in ((0, P), (P, HALF)):
             part = tile([P, LANES, count], F32, f"outer{first}")
             for r in range(LANES):
-                nc.scalar.activation(part[:, r, :], rw_rows[:, first : first + count], ACT.Copy, scale=neg_cw[:, r : r + 1])
+                nc.scalar.activation(by_four(part[:, r, :]), rw_rows(first, count), ACT.Copy, scale=neg_cw[:, r : r + 1])
             for b in range(first // P, (first + count) // P):
                 outer[b] = part[:, :, P * b - first : P * (b + 1) - first]
 
@@ -127,6 +127,11 @@ def tile_attend_gml_pl_sig_kernel(
         deal(nc, wd_dealt[:], wd_raw[:])
         wd_scale = tile([P, V], U8, "wd_scale")
         deal(nc, wd_scale[:], wd_scale_raw[:])
+
+        windows = []
+        for engine, tag in ((nc.vector, "window0"), (nc.vector, "window1"), (nc.gpsimd, "wd_raw"), (nc.gpsimd, "wd_scale_raw")):
+            windows.append(tile([P, T], F32, tag))
+            engine.memset(windows[-1][:].bitcast(U32), 0)
 
         def walk_woven(woven):
             return woven.rearrange("p (c i) r -> p c r i", i=RUN)
@@ -190,10 +195,10 @@ def tile_attend_gml_pl_sig_kernel(
             weight = tile([P, LANES, count], F32, f"weight1{h}")
             for r in range(LANES):
                 nc.vector.scalar_tensor_tensor(
-                    weight[:, r, :],
-                    y_tiles[h, 1][:, r, start : start + count],
+                    by_four(weight[:, r, :]),
+                    by_four(y_tiles[h, 1][:, r, start : start + count]),
                     neg_cw[:, LANES + r : LANES + r + 1],
-                    rw_rows[:, first : first + count],
+                    rw_rows(first, count),
                     MULT,
                     MULT,
                 )
@@ -211,7 +216,7 @@ def tile_attend_gml_pl_sig_kernel(
             for r in range(LANES):
                 nc.tensor.transpose(stage[:, r, :], scaled[:, r, :], identity[:])
             rows = tile([P, LANES, P], F32, f"weight_rows{o}")
-            nc.scalar.activation(rows[:], stage[:], ACT.Copy, scale=rw_cols[:, b : b + 1])
+            nc.scalar.activation(rows[:], stage[:], ACT.Copy, scale=rw_last[:])
             weight = bank([P, LANES, P], weight_bank)
             for r in range(LANES):
                 nc.tensor.transpose(weight[:, r, :], rows[:, r, :], identity[:])

@@ -47,8 +47,8 @@ def tile_attend_gml_pl_sig_kernel(
             return offsets[:, first // 16 : (first + count) // 16]
 
         places = {
-            "g_woven3": 0, "g_woven2_after": 1024, "g_woven2": 2048, "g_woven0": 4032, "g_woven1": 4032,
-            "dx0": 6016, "g_codes2": 5056, "g_codes3": 6528,
+            "g_woven2": 2048, "g_woven0": 4032, "g_woven1": 4032,
+            "sigmoid11": 6144, "dx0": 6144, "g_codes2": 6144, "g_codes3": 7168,
         }
 
         def tile(shape, dtype, tag):
@@ -59,6 +59,10 @@ def tile_attend_gml_pl_sig_kernel(
         def bank(shape, number):
             return psum.tile(shape, F32, name="bank", tag=f"bank{number}")
 
+        wd_raw = tile([P, V], U16, "wd_raw")
+        nc.sync.dma_start(out=wd_raw[:].bitcast(I32), in_=wd_words[0].bitcast(I32))
+        offsets = sb.tile([P, N // 16], U16, name="offsets")
+        nc.sync.dma_start(offsets[:], offs)
         wd_scale_raw = tile([P, V], U8, "wd_scale_raw")
         wv_scale = tile([P, V_PASSES, D], U8, "wv_scale")
         nc.gpsimd.memset(wd_scale_raw[:].bitcast(U32), 0)
@@ -67,10 +71,6 @@ def tile_attend_gml_pl_sig_kernel(
                 out=wd_scale_raw[32 * q : 32 * q + 4, :].bitcast(I32),
                 in_=wd_scales[0, 4 * q : 4 * q + 4, :].bitcast(I32),
             )
-        wd_raw = tile([P, V], U16, "wd_raw")
-        nc.sync.dma_start(out=wd_raw[:].bitcast(I32), in_=wd_words[0].bitcast(I32))
-        offsets = sb.tile([P, N // 16], U16, name="offsets")
-        nc.sync.dma_start(offsets[:], offs)
         x_rows = xT.rearrange("(p t) c -> p t c", t=LANES)
         x_planes = [tile([P, T], F32, f"x_plane{t}") for t in range(LANES)]
         rw_cols = tile([P, LANES], F32, "rw_cols")
@@ -267,12 +267,16 @@ def tile_attend_gml_pl_sig_kernel(
 
         turned = {}
 
-        def back(b, woven, sums_bank, turned_banks):
+        def quantise_g(b, woven):
             codes = tile([P, V_PASSES * P], U32, f"g_codes{b}")
             scale = tile([P, V_PASSES * P], U8, f"g_scale{b}")
             nc.vector.quantize_mx(
                 out=codes[:].bitcast(E5M2), scales=scale[:], in_=woven[:].rearrange("p o i r -> p (o i r)")
             )
+            return codes, scale
+
+        def back(b, quantised, sums_bank, turned_banks):
+            codes, scale = quantised
             sums = bank([P, D], sums_bank)
             for o in range(V_PASSES):
                 nc.tensor.matmul_mx(
@@ -317,9 +321,9 @@ def tile_attend_gml_pl_sig_kernel(
             early_scores(1, o)
         margins = {1: late_margins(1, late_scores(1, (4, 5)))}
         late_sums = late_scores(0, (6, 0))
-        woven = products(0, "g_woven0")
-        back(0, woven, 1, (2,))
+        codes = quantise_g(0, products(0, "g_woven0"))
         margins[0] = late_margins(0, late_sums)
+        back(0, codes, 1, (2, 0))
         weigh_pass1(HALF, P)
         for o in (1, 0):
             squash(2, o, margins[o][:, :, block_cols(2)])
@@ -328,12 +332,12 @@ def tile_attend_gml_pl_sig_kernel(
             weigh_through_psum(3, o, *banks)
         for o in (1, 0):
             squash(3, o, margins[o][:, :, block_cols(3)])
-        back(1, products(1, "g_woven1"), 3, (4,))
-        release(((0, 1), (0, 2), (0, 3)), "dx0")
+        back(1, quantise_g(1, products(1, "g_woven1")), 3, (4,))
+        release(((0, 2), (0, 1), (0, 3), ), "dx0")
         woven = products(2, "g_woven2")
-        back(3, products(3, "g_woven3"), 1, (0,))
-        back(2, woven, 3, (2,))
-        release(((1, 0), (1, 1), (1, 2), (1, 3)), "g_woven2_after")
+        back(3, quantise_g(3, products(3, "g_woven3")), 1, (0,))
+        back(2, quantise_g(2, woven), 3, (2,))
+        release(((1, 0), (1, 1), (1, 2), (1, 3)), "sigmoid30")
 
         out_rows = out_0.rearrange("(p j) c -> p j c", j=LANES)
         pieces = tuple((first, 256) for first in range(0, T, 256))
@@ -388,7 +392,7 @@ def tile_attend_gml_pl_sig_kernel(
         round_lane(nc.scalar.copy, last, 3)
         for k in (0, 1):
             join_pairs(nc.vector.tensor_copy, I32, k)
-        for k in (2, 3):
+        for k in (3, 2):
             join_pairs(nc.scalar.copy, U32, k)
         out_codes = sb.tile([P, T], U32, name="out_codes", align_bytes=64)
         stored = 0

@@ -47,8 +47,8 @@ def tile_attend_gml_pl_sig_kernel(
             return offsets[:, first // 16 : (first + count) // 16]
 
         places = {
-            "g_woven2": 2048, "g_woven0": 4032, "g_woven1": 4032,
-            "sigmoid11": 6144, "dx0": 6144, "g_codes2": 6144, "g_codes3": 7168,
+            "g_woven2": 2048, "g_woven0": 4032, "g_woven1": 4032, "weight20": 6016,
+            "sigmoid11": 8192, "dx0": 8192, "g_codes2": 8192, "g_codes3": 9216,
         }
 
         def tile(shape, dtype, tag):
@@ -89,12 +89,13 @@ def tile_attend_gml_pl_sig_kernel(
 
         y_rows = y.rearrange("(o p r) i -> o p r i", p=P, r=LANES)
         y_tiles = {}
-        for h, o in ((0, 1), (0, 0), (1, 1), (1, 0)):
+
+        def load_labels(h, o):
             y_tiles[h, o] = tile([P, LANES, HALF], F32, f"y{h}{o}")
             nc.sync.dma_start(out=y_tiles[h, o][:], in_=y_rows[o, :, :, HALF * h : HALF * (h + 1)])
-        rw_last = tile([P, 1], F32, "rw_last")
-        with nc.allow_non_contiguous_dma(reason="one weight a partition"):
-            nc.sync.dma_start(out=rw_last[:], in_=rw[0, N - P :].rearrange("(p one) -> p one", one=1))
+
+        for h, o in ((0, 1), (0, 0), (1, 1)):
+            load_labels(h, o)
         wv_sb = tile([P, V_PASSES, D], U16, "wv_sb")
         nc.sync.dma_start(out=wv_sb[:].bitcast(I32), in_=wv_words.bitcast(I32).rearrange("o p w -> p o w"))
         for q in range(4):
@@ -102,6 +103,11 @@ def tile_attend_gml_pl_sig_kernel(
                 out=wv_scale[32 * q : 32 * q + 4, :, :].bitcast(I32),
                 in_=wv_scales[:, 4 * q : 4 * q + 4, :].bitcast(I32).rearrange("o f w -> f o w"),
             )
+
+        load_labels(1, 0)
+        rw_last = tile([P, 1], F32, "rw_last")
+        with nc.allow_non_contiguous_dma(reason="one weight a partition"):
+            nc.sync.dma_start(out=rw_last[:], in_=rw[0, N - P :].rearrange("(p one) -> p one", one=1))
 
         neg_cw = tile([P, V_PASSES * LANES], F32, "neg_cw")
         nc.scalar.activation(neg_cw[:], cw_sb[:].rearrange("p o r -> p (o r)"), ACT.Copy, scale=-1.0)
@@ -316,7 +322,6 @@ def tile_attend_gml_pl_sig_kernel(
             early_scores(0, o)
         quantise_x(2, "outer0")
         weigh_pass0(1, "x_woven2")
-        weigh_pass0(2, "weight20")
         for o in (1, 0):
             early_scores(1, o)
         margins = {1: late_margins(1, late_scores(1, (4, 5)))}
@@ -334,6 +339,7 @@ def tile_attend_gml_pl_sig_kernel(
             squash(3, o, margins[o][:, :, block_cols(3)])
         back(1, quantise_g(1, products(1, "g_woven1")), 3, (4,))
         release(((0, 2), (0, 1), (0, 3), ), "dx0")
+        weigh_pass0(2, "weight20")
         woven = products(2, "g_woven2")
         back(3, quantise_g(3, products(3, "g_woven3")), 1, (0,))
         back(2, quantise_g(2, woven), 3, (2,))
@@ -360,9 +366,8 @@ def tile_attend_gml_pl_sig_kernel(
             nc.gpsimd.tensor_scalar(out, in_, 1.0, 0.0, MULT, ADD)
 
         last = 1
-        release(((3, 0),), "dx30")
-        release(((2, 0),), "late_dx0")
-        late_dx = {j: late_half(j, f"late_dx{j}") for j in (2, 3)}
+        late_dx = {j: late_half(j, f"late_dx{j}") for j in (0, 2, 3)}
+        scatter(0, late_dx[0], HALF, HALF)
         finish(0)
         for k in range(len(pieces)):
             round_lane(nc.scalar.copy, 0, k)

@@ -23,15 +23,47 @@ P = 128
 LANES = 4
 K_PASS = P * LANES
 V_PASSES = V // K_PASS
+QUADRANTS = 4
+PER_COLUMN = 16
 RUN = 4
 HALF = N // 2
+PIECE = 256
+
+PLACES = {
+    "g_woven2": 2048, "g_woven0": 4032, "g_woven1": 4032, "weight20": 6016,
+    "sigmoid11": 8192, "dx0": 8192, "g_codes2": 8192, "g_codes3": 9216,
+}
 
 
 def deal(nc, out, in_):
     nc.vector.tensor_copy(
-        out=out.rearrange("p (g t m) -> p g t m", t=LANES, m=P),
-        in_=in_.rearrange("p (g m t) -> p g t m", t=LANES, m=P),
+        out=out.rearrange("p (g r m) -> p g r m", r=LANES, m=P),
+        in_=in_.rearrange("p (g m r) -> p g r m", r=LANES, m=P),
     )
+
+
+def walk_woven(woven):
+    return woven.rearrange("p (c i) r -> p c r i", i=RUN)
+
+
+def walk_lanes(lanes):
+    return lanes.rearrange("p r (c i) -> p c r i", i=RUN)
+
+
+def by_position(lanes):
+    return lanes.rearrange("p r i -> p i r")
+
+
+def by_four(run):
+    return run.rearrange("p (n k) -> p n k", k=LANES)
+
+
+def block_cols(b):
+    return slice(P * (b % 2), P * (b % 2 + 1))
+
+
+def product_on_vector(b, o):
+    return b in (0, 3) or (b, o) == (1, 1)
 
 
 def tile_attend_gml_pl_sig_kernel(
@@ -43,43 +75,43 @@ def tile_attend_gml_pl_sig_kernel(
         laid = ctx.enter_context(tc.tile_pool(name="laid", bufs=1))
         psum = ctx.enter_context(tc.psum_pool(name="psum", bufs=1))
 
-        def listed(first, count):
-            return offsets[:, first // 16 : (first + count) // 16]
-
-        places = {
-            "g_woven2": 2048, "g_woven0": 4032, "g_woven1": 4032, "weight20": 6016,
-            "sigmoid11": 8192, "dx0": 8192, "g_codes2": 8192, "g_codes3": 9216,
-        }
-
         def tile(shape, dtype, tag):
-            if tag in places:
-                return laid.tile(shape, dtype, name="laid", tag=tag, align_bytes=64, offset=places[tag])
+            if tag in PLACES:
+                return laid.tile(shape, dtype, name="laid", tag=tag, align_bytes=64, offset=PLACES[tag])
             return sb.tile(shape, dtype, name="shared", tag=tag, align_bytes=64)
 
         def bank(shape, number):
             return psum.tile(shape, F32, name="bank", tag=f"bank{number}")
 
+        def listed(first, count):
+            return offsets[:, first // PER_COLUMN : (first + count) // PER_COLUMN]
+
         wd_raw = tile([P, V], U16, "wd_raw")
         nc.sync.dma_start(out=wd_raw[:].bitcast(I32), in_=wd_words[0].bitcast(I32))
-        offsets = sb.tile([P, N // 16], U16, name="offsets")
+        offsets = sb.tile([P, N // PER_COLUMN], U16, name="offsets")
         nc.sync.dma_start(offsets[:], offs)
         wd_scale_raw = tile([P, V], U8, "wd_scale_raw")
         wv_scale = tile([P, V_PASSES, D], U8, "wv_scale")
         nc.gpsimd.memset(wd_scale_raw[:].bitcast(U32), 0)
-        for q in range(4):
+        for q in range(QUADRANTS):
             nc.sync.dma_start(
                 out=wd_scale_raw[32 * q : 32 * q + 4, :].bitcast(I32),
                 in_=wd_scales[0, 4 * q : 4 * q + 4, :].bitcast(I32),
             )
         x_rows = xT.rearrange("(p t) c -> p t c", t=LANES)
-        x_planes = [tile([P, T], F32, f"x_plane{t}") for t in range(LANES)]
+        x_lanes = [tile([P, T], F32, f"x_plane{t}") for t in range(LANES)]
         rw_cols = tile([P, LANES], F32, "rw_cols")
         cw_sb = tile([P, V_PASSES, LANES], F32, "cw_sb")
-        for t in range(LANES):
-            if t == 2:
-                nc.sync.dma_start(out=rw_cols[:], in_=rw[0].rearrange("(p k) -> p k", k=LANES))
-                nc.sync.dma_start(out=cw_sb[:], in_=cw.rearrange("(o p r) one -> p o (r one)", p=P, r=LANES))
-            nc.sync.dma_start(out=x_planes[t][:], in_=x_rows[:, t, :])
+
+        def load_x(t):
+            nc.sync.dma_start(out=x_lanes[t][:], in_=x_rows[:, t, :])
+
+        for t in (0, 1):
+            load_x(t)
+        nc.sync.dma_start(out=rw_cols[:], in_=rw[0].rearrange("(p k) -> p k", k=LANES))
+        nc.sync.dma_start(out=cw_sb[:], in_=cw.rearrange("(o p r) one -> p o (r one)", p=P, r=LANES))
+        for t in (2, 3):
+            load_x(t)
         warm = tile([P, 8], F32, "warm")
         nc.vector.memset(warm[:], 0.0)
         nc.scalar.activation(warm[:], warm[:], ACT.Sigmoid)
@@ -88,22 +120,21 @@ def tile_attend_gml_pl_sig_kernel(
         nc.gpsimd.memset(wv_scale[:].bitcast(U32), 0)
 
         y_rows = y.rearrange("(o p r) i -> o p r i", p=P, r=LANES)
-        y_tiles = {}
+        labels = {}
 
         def load_labels(h, o):
-            y_tiles[h, o] = tile([P, LANES, HALF], F32, f"y{h}{o}")
-            nc.sync.dma_start(out=y_tiles[h, o][:], in_=y_rows[o, :, :, HALF * h : HALF * (h + 1)])
+            labels[h, o] = tile([P, LANES, HALF], F32, f"y{h}{o}")
+            nc.sync.dma_start(out=labels[h, o][:], in_=y_rows[o, :, :, HALF * h : HALF * (h + 1)])
 
         for h, o in ((0, 1), (0, 0), (1, 1)):
             load_labels(h, o)
         wv_sb = tile([P, V_PASSES, D], U16, "wv_sb")
         nc.sync.dma_start(out=wv_sb[:].bitcast(I32), in_=wv_words.bitcast(I32).rearrange("o p w -> p o w"))
-        for q in range(4):
+        for q in range(QUADRANTS):
             nc.sync.dma_start(
                 out=wv_scale[32 * q : 32 * q + 4, :, :].bitcast(I32),
                 in_=wv_scales[:, 4 * q : 4 * q + 4, :].bitcast(I32).rearrange("o f w -> f o w"),
             )
-
         load_labels(1, 0)
         rw_last = tile([P, 1], F32, "rw_last")
         with nc.allow_non_contiguous_dma(reason="one weight a partition"):
@@ -117,9 +148,6 @@ def tile_attend_gml_pl_sig_kernel(
 
         def rw_rows(first, count):
             return rw_bank[:].rearrange("p k n -> p n k")[:, first // LANES : (first + count) // LANES, :]
-
-        def by_four(run):
-            return run.rearrange("p (n k) -> p n k", k=LANES)
 
         outer = {}
         for first, count in ((0, P), (P, HALF)):
@@ -139,17 +167,9 @@ def tile_attend_gml_pl_sig_kernel(
             windows.append(tile([P, T], F32, tag))
             engine.memset(windows[-1][:].bitcast(U32), 0)
 
-        def walk_woven(woven):
-            return woven.rearrange("p (c i) r -> p c r i", i=RUN)
-
-        def walk_lanes(lanes):
-            return lanes.rearrange("p r (c i) -> p c r i", i=RUN)
-
         def gather(out, t, first, count):
-            nc.vector.tensor_copy(out, x_planes[t][:].indirect(listed(first, count)))
+            nc.vector.tensor_copy(out, x_lanes[t][:].indirect(listed(first, count)))
 
-        sigmoids = {}
-        weights = {}
         picked = tile([P, LANES, N], BF16, "picked")
         for t in range(LANES - 1):
             gather(picked[:, t, :], t, 0, N)
@@ -160,10 +180,10 @@ def tile_attend_gml_pl_sig_kernel(
         x_codes = {}
         x_scale = tile([P, N], U8, "x_scale")
 
-        def quantise_x(k, tag):
-            first, count = spans[k]
+        def quantise_x(span, tag):
+            first, count = spans[span]
             cols = slice(first, first + count)
-            woven = tile([P, count, LANES], BF16, f"x_woven{k}")
+            woven = tile([P, count, LANES], BF16, f"x_woven{span}")
             nc.scalar.copy(walk_woven(woven[:]), walk_lanes(picked[:, :, cols]))
             x_codes[first] = tile([P, count], U32, tag)[:]
             nc.vector.quantize_mx(
@@ -171,9 +191,6 @@ def tile_attend_gml_pl_sig_kernel(
                 scales=x_scale[:, cols],
                 in_=woven[:].rearrange("p i t -> p (i t)"),
             )
-
-        def block_cols(b):
-            return slice(P * (b % 2), P * (b % 2 + 1))
 
         def scores(out, o, r, cols):
             first = K_PASS * o + P * r
@@ -187,14 +204,11 @@ def tile_attend_gml_pl_sig_kernel(
                 stop=True,
             )
 
-        def by_position(lanes):
-            return lanes.rearrange("p r i -> p i r")
+        weights = {}
 
         def weigh_pass0(b, tag):
             weights[b, 0] = tile([P, LANES, P], F32, tag)[:]
-            nc.gpsimd.tensor_tensor(
-                weights[b, 0], y_tiles[b // 2, 0][:, :, block_cols(b)], outer[b], MULT
-            )
+            nc.gpsimd.tensor_tensor(weights[b, 0], labels[b // 2, 0][:, :, block_cols(b)], outer[b], MULT)
 
         def weigh_pass1(first, count):
             h, start = divmod(first, HALF)
@@ -202,7 +216,7 @@ def tile_attend_gml_pl_sig_kernel(
             for r in range(LANES):
                 nc.vector.scalar_tensor_tensor(
                     by_four(weight[:, r, :]),
-                    by_four(y_tiles[h, 1][:, r, start : start + count]),
+                    by_four(labels[h, 1][:, r, start : start + count]),
                     neg_cw[:, LANES + r : LANES + r + 1],
                     rw_rows(first, count),
                     MULT,
@@ -211,12 +225,12 @@ def tile_attend_gml_pl_sig_kernel(
             for k in range(count // P):
                 weights[first // P + k, 1] = weight[:, :, P * k : P * (k + 1)]
 
-        def weigh_through_psum(b, o, stage_bank, weight_bank):
+        def weigh_last_block(o, stage_bank, weight_bank):
             scaled = tile([P, LANES, P], F32, f"scaled_labels{o}")
             for r in range(LANES):
                 k = LANES * o + r
                 nc.scalar.activation(
-                    scaled[:, r, :], y_tiles[b // 2, o][:, r, block_cols(b)], ACT.Copy, scale=neg_cw[:, k : k + 1]
+                    scaled[:, r, :], labels[1, o][:, r, block_cols(3)], ACT.Copy, scale=neg_cw[:, k : k + 1]
                 )
             stage = bank([P, LANES, P], stage_bank)
             for r in range(LANES):
@@ -226,13 +240,12 @@ def tile_attend_gml_pl_sig_kernel(
             weight = bank([P, LANES, P], weight_bank)
             for r in range(LANES):
                 nc.tensor.transpose(weight[:, r, :], rows[:, r, :], identity[:])
-            weights[b, o] = weight[:]
+            weights[3, o] = weight[:]
 
-        def on_vector(b, o):
-            return b in (0, 3) or (b, o) == (1, 1)
+        sigmoids = {}
 
         def squash(b, o, margin):
-            if on_vector(b, o):
+            if product_on_vector(b, o):
                 sigmoids[b, o] = tile([P, LANES, P], F32, f"sigmoid{b}{o}")[:]
             else:
                 sigmoids[b, o] = tile([P, P, LANES], F32, f"sigmoid{b}{o}")[:]
@@ -244,7 +257,7 @@ def tile_attend_gml_pl_sig_kernel(
             for r in range(LANES):
                 scores(sums[:, r, :], o, r, slice(P * b, P * (b + 1)))
             margin = tile([P, LANES, P], F32, f"margin{b}{o}")
-            nc.vector.tensor_tensor(margin[:], sums[:], y_tiles[0, o][:, :, block_cols(b)], MULT)
+            nc.vector.tensor_tensor(margin[:], sums[:], labels[0, o][:, :, block_cols(b)], MULT)
             squash(b, o, margin[:])
 
         def late_scores(o, banks):
@@ -257,21 +270,19 @@ def tile_attend_gml_pl_sig_kernel(
             margin = tile([P, LANES, HALF], F32, f"late_margin{o}")
             for pair in range(2):
                 rows = slice(2 * pair, 2 * pair + 2)
-                nc.vector.tensor_tensor(margin[:, rows, :], sums[pair][:], y_tiles[1, o][:, rows, :], MULT)
+                nc.vector.tensor_tensor(margin[:, rows, :], sums[pair][:], labels[1, o][:, rows, :], MULT)
             return margin
 
-        def products(b, tag):
-            woven = tile([P, V_PASSES, P, LANES], BF16, tag)
+        def products(b):
+            woven = tile([P, V_PASSES, P, LANES], BF16, f"g_woven{b}")
             for o in (0, 1) if b == 1 else (1, 0):
-                if on_vector(b, o):
+                if product_on_vector(b, o):
                     nc.vector.tensor_tensor(
                         walk_woven(woven[:, o]), walk_lanes(sigmoids[b, o]), walk_lanes(weights[b, o]), MULT
                     )
                 else:
                     nc.gpsimd.tensor_tensor(woven[:, o], sigmoids[b, o], by_position(weights[b, o]), MULT)
             return woven
-
-        turned = {}
 
         def quantise_g(b, woven):
             codes = tile([P, V_PASSES * P], U32, f"g_codes{b}")
@@ -280,6 +291,8 @@ def tile_attend_gml_pl_sig_kernel(
                 out=codes[:].bitcast(E5M2), scales=scale[:], in_=woven[:].rearrange("p o i r -> p (o i r)")
             )
             return codes, scale
+
+        turned = {}
 
         def back(b, quantised, sums_bank, turned_banks):
             codes, scale = quantised
@@ -307,11 +320,11 @@ def tile_attend_gml_pl_sig_kernel(
         def scatter(j, dx, first, count):
             nc.vector.tensor_copy(windows[j][:].indirect(listed(first, count)), dx)
 
-        def release(parts, tag):
-            dx = tile([P, len(parts), P], F32, tag)
-            for k, (b, j) in enumerate(parts):
+        def release(b, lanes, tag):
+            dx = tile([P, len(lanes), P], F32, tag)
+            for k, j in enumerate(lanes):
                 nc.scalar.copy(dx[:, k, :], turned[b, j])
-            for k, (b, j) in enumerate(parts):
+            for k, j in enumerate(lanes):
                 scatter(j, dx[:, k, :], P * b, P)
 
         quantise_x(0, "x_codes0")
@@ -326,34 +339,36 @@ def tile_attend_gml_pl_sig_kernel(
             early_scores(1, o)
         margins = {1: late_margins(1, late_scores(1, (4, 5)))}
         late_sums = late_scores(0, (6, 0))
-        codes = quantise_g(0, products(0, "g_woven0"))
+        quantised = quantise_g(0, products(0))
         margins[0] = late_margins(0, late_sums)
-        back(0, codes, 1, (2, 0))
+        back(0, quantised, 1, (2, 0))
         weigh_pass1(HALF, P)
         for o in (1, 0):
             squash(2, o, margins[o][:, :, block_cols(2)])
-        release(((0, 0),), "dx00")
+        release(0, (0,), "dx00")
         for o, banks in ((1, (3, 5)), (0, (4, 6))):
-            weigh_through_psum(3, o, *banks)
+            weigh_last_block(o, *banks)
         for o in (1, 0):
             squash(3, o, margins[o][:, :, block_cols(3)])
-        back(1, quantise_g(1, products(1, "g_woven1")), 3, (4,))
-        release(((0, 2), (0, 1), (0, 3), ), "dx0")
+        back(1, quantise_g(1, products(1)), 3, (4,))
+        release(0, (2, 1, 3), "dx0")
         weigh_pass0(2, "weight20")
-        woven = products(2, "g_woven2")
-        back(3, quantise_g(3, products(3, "g_woven3")), 1, (0,))
-        back(2, quantise_g(2, woven), 3, (2,))
-        release(((1, 0), (1, 1), (1, 2), (1, 3)), "sigmoid30")
+        g_block2 = products(2)
+        back(3, quantise_g(3, products(3)), 1, (0,))
+        back(2, quantise_g(2, g_block2), 3, (2,))
+        release(1, range(LANES), "sigmoid30")
 
         out_rows = out_0.rearrange("(p j) c -> p j c", j=LANES)
-        pieces = tuple((first, 256) for first in range(0, T, 256))
-        pairs = [sb.tile([P, 2, width, 2], BF16, name=f"pairs{first}") for first, width in pieces]
+        firsts = range(0, T, PIECE)
+        pairs = [sb.tile([P, 2, PIECE, 2], BF16, name=f"pairs{first}") for first in firsts]
 
         def round_lane(engine_copy, j, k):
-            first, width = pieces[k]
-            engine_copy(pairs[k][:, j // 2, :, j % 2], windows[j][:, first : first + width])
+            engine_copy(pairs[k][:, j // 2, :, j % 2], windows[j][:, firsts[k] : firsts[k] + PIECE])
 
-        def finish(j):
+        def round_on_gpsimd(out, in_):
+            nc.gpsimd.tensor_scalar(out, in_, 1.0, -0.0, MULT, ADD)
+
+        def store_window(j):
             nc.sync.dma_start(out=out_rows[:, j, :], in_=windows[j][:])
 
         def late_half(j, tag):
@@ -362,31 +377,27 @@ def tile_attend_gml_pl_sig_kernel(
                 nc.scalar.copy(dx[:, b - 2, :], turned[b, j])
             return dx[:].rearrange("p b i -> p (b i)")
 
-        def round_on_gpsimd(out, in_):
-            nc.gpsimd.tensor_scalar(out, in_, 1.0, 0.0, MULT, ADD)
-
         last = 1
         late_dx = {j: late_half(j, f"late_dx{j}") for j in (0, 2, 3)}
         scatter(0, late_dx[0], HALF, HALF)
-        finish(0)
-        for k in range(len(pieces)):
+        store_window(0)
+        for k in range(len(firsts)):
             round_lane(nc.scalar.copy, 0, k)
         late_dx[last] = late_half(last, "late_dx0")
         for j in (2, 3):
             scatter(j, late_dx[j], HALF, HALF)
-            finish(j)
-            for k in range(len(pieces)):
-                round_lane(round_on_gpsimd if k < 2 else nc.scalar.copy, j, k)
+            store_window(j)
+            for k in range(len(firsts)):
+                round_lane(round_on_gpsimd if k < len(firsts) // 2 else nc.scalar.copy, j, k)
         scatter(last, late_dx[last], HALF, HALF)
-        finish(last)
+        store_window(last)
 
         out_scale = sb.tile([P, T], U8, name="out_scale", align_bytes=64)
         out_words = out_1[0].rearrange("p c t -> p (c t)").bitcast(I32)
         woven_out = {}
 
         def join_pairs(engine_copy, word, k):
-            first, width = pieces[k]
-            woven_out[k] = sb.tile([P, width, LANES], BF16, name=f"out_woven{first}", align_bytes=64)
+            woven_out[k] = sb.tile([P, PIECE, LANES], BF16, name=f"out_woven{firsts[k]}", align_bytes=64)
             engine_copy(
                 woven_out[k][:].bitcast(word),
                 pairs[k][:].rearrange("p h c e -> p h (c e)").bitcast(word).rearrange("p h c -> p c h"),
@@ -401,19 +412,18 @@ def tile_attend_gml_pl_sig_kernel(
             join_pairs(nc.scalar.copy, U32, k)
         out_codes = sb.tile([P, T], U32, name="out_codes", align_bytes=64)
         stored = 0
-        for k in range(len(pieces)):
-            first, width = pieces[k]
-            cols = slice(first, first + width)
+        for k, first in enumerate(firsts):
+            cols = slice(first, first + PIECE)
             nc.vector.quantize_mx(
                 out=out_codes[:, cols].bitcast(E4M3),
                 scales=out_scale[:, cols],
                 in_=woven_out[k][:].rearrange("p c j -> p (c j)"),
             )
             if k > 0:
-                cols = slice(stored, first + width)
-                nc.sync.dma_start(out=out_words[:, cols], in_=out_codes[:, cols].bitcast(I32))
-                stored = first + width
-        for q in range(4):
+                unstored = slice(stored, first + PIECE)
+                nc.sync.dma_start(out=out_words[:, unstored], in_=out_codes[:, unstored].bitcast(I32))
+                stored = first + PIECE
+        for q in range(QUADRANTS):
             queue = nc.scalar if q % 2 == 0 else nc.sync
             queue.dma_start(
                 out=out_2[0, 4 * q : 4 * q + 4, :].bitcast(I32),

@@ -23,22 +23,20 @@ P = 128
 LANES = 4
 K_PASS = P * LANES
 V_PASSES = V // K_PASS
+GROUPS = N // P
+LAST = GROUPS - 1
 QUADRANTS = 4
 PER_COLUMN = 16
 RUN = 4
 HALF = N // 2
 PIECE = 256
-
-PLACES = {
-    "g_woven2": 2048, "g_woven0": 4032, "g_woven1": 4032, "weight20": 6016,
-    "sigmoid11": 8192, "dx0": 8192, "g_codes2": 8192, "g_codes3": 9216,
-}
+PIECES = T // PIECE
 
 
-def deal(nc, out, in_):
-    nc.vector.tensor_copy(
-        out=out.rearrange("p (g r m) -> p g r m", r=LANES, m=P),
-        in_=in_.rearrange("p (g m r) -> p g r m", r=LANES, m=P),
+def deal(engine_copy, out, in_):
+    engine_copy(
+        out.rearrange("p (g r m) -> p g r m", r=LANES, m=P),
+        in_.rearrange("p (g m r) -> p g r m", r=LANES, m=P),
     )
 
 
@@ -58,12 +56,8 @@ def by_four(run):
     return run.rearrange("p (n k) -> p n k", k=LANES)
 
 
-def block_cols(b):
-    return slice(P * (b % 2), P * (b % 2 + 1))
-
-
-def product_on_vector(b, o):
-    return b in (0, 3) or (b, o) == (1, 1)
+def group_cols(b):
+    return slice(P * b, P * (b + 1))
 
 
 def tile_attend_gml_pl_sig_kernel(
@@ -72,12 +66,9 @@ def tile_attend_gml_pl_sig_kernel(
     nc = tc.nc
     with ExitStack() as ctx:
         sb = ctx.enter_context(tc.tile_pool(name="sb", bufs=1))
-        laid = ctx.enter_context(tc.tile_pool(name="laid", bufs=1))
         psum = ctx.enter_context(tc.psum_pool(name="psum", bufs=1))
 
         def tile(shape, dtype, tag):
-            if tag in PLACES:
-                return laid.tile(shape, dtype, name="laid", tag=tag, align_bytes=64, offset=PLACES[tag])
             return sb.tile(shape, dtype, name="shared", tag=tag, align_bytes=64)
 
         def bank(shape, number):
@@ -91,7 +82,7 @@ def tile_attend_gml_pl_sig_kernel(
         offsets = sb.tile([P, N // PER_COLUMN], U16, name="offsets")
         nc.sync.dma_start(offsets[:], offs)
         wd_scale_raw = tile([P, V], U8, "wd_scale_raw")
-        wv_scale = tile([P, V_PASSES, D], U8, "wv_scale")
+        wv_scale_raw = tile([P, V_PASSES * D], U8, "wv_scale_raw")
         nc.gpsimd.memset(wd_scale_raw[:].bitcast(U32), 0)
         for q in range(QUADRANTS):
             nc.sync.dma_start(
@@ -99,7 +90,7 @@ def tile_attend_gml_pl_sig_kernel(
                 in_=wd_scales[0, 4 * q : 4 * q + 4, :].bitcast(I32),
             )
         x_rows = xT.rearrange("(p t) c -> p t c", t=LANES)
-        x_lanes = [tile([P, T], F32, f"x_plane{t}") for t in range(LANES)]
+        x_lanes = [tile([P, T], F32, f"x_lane{t}") for t in range(LANES)]
         rw_cols = tile([P, LANES], F32, "rw_cols")
         cw_sb = tile([P, V_PASSES, LANES], F32, "cw_sb")
 
@@ -117,7 +108,7 @@ def tile_attend_gml_pl_sig_kernel(
         nc.scalar.activation(warm[:], warm[:], ACT.Sigmoid)
         identity = tile([P, P], F32, "identity")
         make_identity(nc, identity[:])
-        nc.gpsimd.memset(wv_scale[:].bitcast(U32), 0)
+        nc.gpsimd.memset(wv_scale_raw[:].bitcast(U32), 0)
 
         y_rows = y.rearrange("(o p r) i -> o p r i", p=P, r=LANES)
         labels = {}
@@ -126,16 +117,23 @@ def tile_attend_gml_pl_sig_kernel(
             labels[h, o] = tile([P, LANES, HALF], F32, f"y{h}{o}")
             nc.sync.dma_start(out=labels[h, o][:], in_=y_rows[o, :, :, HALF * h : HALF * (h + 1)])
 
-        for h, o in ((0, 1), (0, 0), (1, 1)):
-            load_labels(h, o)
-        wv_sb = tile([P, V_PASSES, D], U16, "wv_sb")
-        nc.sync.dma_start(out=wv_sb[:].bitcast(I32), in_=wv_words.bitcast(I32).rearrange("o p w -> p o w"))
+        def group_labels(b, o):
+            return labels[b // 2, o][:, :, group_cols(b % 2)]
+
         for q in range(QUADRANTS):
             nc.sync.dma_start(
-                out=wv_scale[32 * q : 32 * q + 4, :, :].bitcast(I32),
+                out=wv_scale_raw[32 * q : 32 * q + 4, :].bitcast(I32).rearrange("f (o w) -> f o w", o=V_PASSES),
                 in_=wv_scales[:, 4 * q : 4 * q + 4, :].bitcast(I32).rearrange("o f w -> f o w"),
             )
-        load_labels(1, 0)
+        for o in (1, 0):
+            load_labels(0, o)
+        wv_raw = tile([P, V_PASSES * D], U16, "wv_raw")
+        nc.sync.dma_start(
+            out=wv_raw[:].bitcast(I32).rearrange("p (o w) -> p o w", o=V_PASSES),
+            in_=wv_words.bitcast(I32).rearrange("o p w -> p o w"),
+        )
+        for o in (1, 0):
+            load_labels(1, o)
         rw_last = tile([P, 1], F32, "rw_last")
         with nc.allow_non_contiguous_dma(reason="one weight a partition"):
             nc.sync.dma_start(out=rw_last[:], in_=rw[0, N - P :].rearrange("(p one) -> p one", one=1))
@@ -149,18 +147,22 @@ def tile_attend_gml_pl_sig_kernel(
         def rw_rows(first, count):
             return rw_bank[:].rearrange("p k n -> p n k")[:, first // LANES : (first + count) // LANES, :]
 
-        outer = {}
-        for first, count in ((0, P), (P, HALF)):
-            part = tile([P, LANES, count], F32, f"outer{first}")
+        outer = tile([P, LANES, P], F32, "outer")
+        for r in range(LANES):
+            k = LANES + r
+            nc.scalar.activation(by_four(outer[:, r, :]), rw_rows(0, P), ACT.Copy, scale=neg_cw[:, k : k + 1])
+        cw_rows = tile([P, V_PASSES, LANES, P], F32, "cw_rows")
+        for o in range(V_PASSES):
+            spread = bank([P, LANES, P], o)
             for r in range(LANES):
-                nc.scalar.activation(by_four(part[:, r, :]), rw_rows(first, count), ACT.Copy, scale=neg_cw[:, r : r + 1])
-            for b in range(first // P, (first + count) // P):
-                outer[b] = part[:, :, P * b - first : P * (b + 1) - first]
+                k = LANES * o + r
+                nc.tensor.transpose(spread[:, r, :], neg_cw[:, k : k + 1].to_broadcast([P, P]), identity[:])
+            nc.scalar.copy(cw_rows[:, o], spread[:])
 
         wd_dealt = tile([P, V], U16, "wd_dealt")
-        deal(nc, wd_dealt[:], wd_raw[:])
+        deal(nc.vector.tensor_copy, wd_dealt[:], wd_raw[:])
         wd_scale = tile([P, V], U8, "wd_scale")
-        deal(nc, wd_scale[:], wd_scale_raw[:])
+        deal(nc.vector.tensor_copy, wd_scale[:], wd_scale_raw[:])
 
         windows = []
         for engine, tag in ((nc.vector, "window0"), (nc.vector, "window1"), (nc.gpsimd, "wd_raw"), (nc.gpsimd, "wd_scale_raw")):
@@ -173,256 +175,259 @@ def tile_attend_gml_pl_sig_kernel(
         picked = tile([P, LANES, N], BF16, "picked")
         for t in range(LANES - 1):
             gather(picked[:, t, :], t, 0, N)
-        spans = ((0, P), (P, P), (HALF, HALF))
+        spans = ((0, P), (P, N - P))
         for first, count in spans:
             gather(picked[:, LANES - 1, first : first + count], LANES - 1, first, count)
 
         x_codes = {}
         x_scale = tile([P, N], U8, "x_scale")
 
-        def quantise_x(span, tag):
+        def quantise_x(span, woven_tag, codes_tag):
             first, count = spans[span]
             cols = slice(first, first + count)
-            woven = tile([P, count, LANES], BF16, f"x_woven{span}")
+            woven = tile([P, count, LANES], BF16, woven_tag)
             nc.scalar.copy(walk_woven(woven[:]), walk_lanes(picked[:, :, cols]))
-            x_codes[first] = tile([P, count], U32, tag)[:]
+            codes = tile([P, count], U32, codes_tag)
             nc.vector.quantize_mx(
-                out=x_codes[first].bitcast(E4M3),
-                scales=x_scale[:, cols],
-                in_=woven[:].rearrange("p i t -> p (i t)"),
+                out=codes[:].bitcast(E4M3), scales=x_scale[:, cols], in_=woven[:].rearrange("p i t -> p (i t)")
             )
+            for b in range(first // P, (first + count) // P):
+                x_codes[b] = codes[:, P * b - first : P * (b + 1) - first]
 
-        def scores(out, o, r, cols):
-            first = K_PASS * o + P * r
-            nc.tensor.matmul_mx(
-                out=out,
-                lhsT=wd_dealt[:, first : first + P].bitcast(E2M1),
-                lhsT_scale=wd_scale[:, first : first + P],
-                rhs=x_codes[cols.start].bitcast(E4M3),
-                rhs_scale=x_scale[:, cols],
-                start=True,
-                stop=True,
-            )
+        sigmoids = {}
 
-        weights = {}
-
-        def weigh_pass0(b, tag):
-            weights[b, 0] = tile([P, LANES, P], F32, tag)[:]
-            nc.gpsimd.tensor_tensor(weights[b, 0], labels[b // 2, 0][:, :, block_cols(b)], outer[b], MULT)
-
-        def weigh_pass1(first, count):
-            h, start = divmod(first, HALF)
-            weight = tile([P, LANES, count], F32, f"weight1{h}")
+        def score(b, o, number):
+            sums = bank([P, LANES, P], number)
             for r in range(LANES):
+                cols = slice(K_PASS * o + P * r, K_PASS * o + P * (r + 1))
+                nc.tensor.matmul_mx(
+                    out=sums[:, r, :],
+                    lhsT=wd_dealt[:, cols].bitcast(E2M1),
+                    lhsT_scale=wd_scale[:, cols],
+                    rhs=x_codes[b].bitcast(E4M3),
+                    rhs_scale=x_scale[:, group_cols(b)],
+                    start=True,
+                    stop=True,
+                )
+            margin = tile([P, LANES, P], F32, f"margin{b}{o}")
+            nc.vector.tensor_tensor(margin[:], sums[:], group_labels(b, o), MULT)
+            if b not in sigmoids:
+                sigmoids[b] = tile([P, V_PASSES, K_PASS], F32, f"sigmoid{b}")
+            if b == LAST:
+                source, out = margin[:], sigmoids[b][:, o].rearrange("p (r i) -> p r i", r=LANES)
+            else:
+                source, out = by_position(margin[:]), sigmoids[b][:, o].rearrange("p (i r) -> p i r", r=LANES)
+            nc.scalar.activation(out, source, ACT.Sigmoid, scale=-1.0)
+
+        def weigh(out, o, first, count):
+            h, start = divmod(first, HALF)
+            for r in range(LANES):
+                k = LANES * o + r
                 nc.vector.scalar_tensor_tensor(
-                    by_four(weight[:, r, :]),
-                    by_four(labels[h, 1][:, r, start : start + count]),
-                    neg_cw[:, LANES + r : LANES + r + 1],
+                    by_four(out[:, r, :]),
+                    by_four(labels[h, o][:, r, start : start + count]),
+                    neg_cw[:, k : k + 1],
                     rw_rows(first, count),
                     MULT,
                     MULT,
                 )
-            for k in range(count // P):
-                weights[first // P + k, 1] = weight[:, :, P * k : P * (k + 1)]
 
-        def weigh_last_block(o, stage_bank, weight_bank):
-            scaled = tile([P, LANES, P], F32, f"scaled_labels{o}")
-            for r in range(LANES):
-                k = LANES * o + r
-                nc.scalar.activation(
-                    scaled[:, r, :], labels[1, o][:, r, block_cols(3)], ACT.Copy, scale=neg_cw[:, k : k + 1]
-                )
+        def weigh_last(o, stage_bank, weight_bank):
             stage = bank([P, LANES, P], stage_bank)
             for r in range(LANES):
-                nc.tensor.transpose(stage[:, r, :], scaled[:, r, :], identity[:])
+                nc.tensor.transpose(stage[:, r, :], group_labels(LAST, o)[:, r, :], identity[:])
             rows = tile([P, LANES, P], F32, f"weight_rows{o}")
-            nc.scalar.activation(rows[:], stage[:], ACT.Copy, scale=rw_last[:])
+            nc.vector.scalar_tensor_tensor(
+                rows[:].rearrange("p r m -> p (r m)"),
+                stage[:].rearrange("p r m -> p (r m)"),
+                rw_last[:],
+                cw_rows[:, o].rearrange("p r m -> p (r m)"),
+                MULT,
+                MULT,
+            )
             weight = bank([P, LANES, P], weight_bank)
             for r in range(LANES):
                 nc.tensor.transpose(weight[:, r, :], rows[:, r, :], identity[:])
-            weights[3, o] = weight[:]
+            return weight
 
-        sigmoids = {}
+        g_codes = [tile([P, N], U32, f"g_codes{o}") for o in range(V_PASSES)]
+        g_scales = [tile([P, N], U8, f"g_scale{o}") for o in range(V_PASSES)]
 
-        def squash(b, o, margin):
-            if product_on_vector(b, o):
-                sigmoids[b, o] = tile([P, LANES, P], F32, f"sigmoid{b}{o}")[:]
-            else:
-                sigmoids[b, o] = tile([P, P, LANES], F32, f"sigmoid{b}{o}")[:]
-                margin = by_position(margin)
-            nc.scalar.activation(sigmoids[b, o], margin, ACT.Sigmoid, scale=-1.0)
+        def product_on_gpsimd(woven, b, weight, passes):
+            nc.gpsimd.tensor_tensor(
+                woven[:, passes, :P, :],
+                sigmoids[b][:, passes].rearrange("p o (i r) -> p o i r", r=LANES),
+                weight[:, passes].rearrange("p o r i -> p o i r"),
+                MULT,
+            )
 
-        def early_scores(b, o):
-            sums = bank([P, LANES, P], 2 * b + o)
-            for r in range(LANES):
-                scores(sums[:, r, :], o, r, slice(P * b, P * (b + 1)))
-            margin = tile([P, LANES, P], F32, f"margin{b}{o}")
-            nc.vector.tensor_tensor(margin[:], sums[:], labels[0, o][:, :, block_cols(b)], MULT)
-            squash(b, o, margin[:])
+        def quantise_g(woven, cols):
+            for o in (1, 0):
+                nc.vector.quantize_mx(
+                    out=g_codes[o][:, cols].bitcast(E5M2),
+                    scales=g_scales[o][:, cols],
+                    in_=woven[:, o].rearrange("p i r -> p (i r)"),
+                )
 
-        def late_scores(o, banks):
-            sums = [bank([P, 2, HALF], number) for number in banks]
-            for r in range(LANES):
-                scores(sums[r // 2][:, r % 2, :], o, r, slice(HALF, N))
+        def back(out, j, cols):
+            for o in (1, 0):
+                dealt = slice(D * o + P * j, D * o + P * (j + 1))
+                nc.tensor.matmul_mx(
+                    out=out,
+                    lhsT=wv_dealt[:, dealt].bitcast(E2M1),
+                    lhsT_scale=wv_scale[:, dealt],
+                    rhs=g_codes[o][:, cols].bitcast(E5M2),
+                    rhs_scale=g_scales[o][:, cols],
+                    start=(o == 1),
+                    stop=(o == 0),
+                )
+
+        def back_group(b, lanes, number):
+            sums = bank([P, len(lanes), P], number)
+            for k, j in enumerate(lanes):
+                back(sums[:, k, :], j, group_cols(b))
             return sums
 
-        def late_margins(o, sums):
-            margin = tile([P, LANES, HALF], F32, f"late_margin{o}")
-            for pair in range(2):
-                rows = slice(2 * pair, 2 * pair + 2)
-                nc.vector.tensor_tensor(margin[:, rows, :], sums[pair][:], labels[1, o][:, rows, :], MULT)
-            return margin
+        def scalar_scatter(j, dx, first, count):
+            nc.scalar.activation(windows[j][:].indirect(listed(first, count)), dx, ACT.Copy)
 
-        def products(b):
-            woven = tile([P, V_PASSES, P, LANES], BF16, f"g_woven{b}")
-            for o in (0, 1) if b == 1 else (1, 0):
-                if product_on_vector(b, o):
-                    nc.vector.tensor_tensor(
-                        walk_woven(woven[:, o]), walk_lanes(sigmoids[b, o]), walk_lanes(weights[b, o]), MULT
-                    )
-                else:
-                    nc.gpsimd.tensor_tensor(woven[:, o], sigmoids[b, o], by_position(weights[b, o]), MULT)
-            return woven
-
-        def quantise_g(b, woven):
-            codes = tile([P, V_PASSES * P], U32, f"g_codes{b}")
-            scale = tile([P, V_PASSES * P], U8, f"g_scale{b}")
-            nc.vector.quantize_mx(
-                out=codes[:].bitcast(E5M2), scales=scale[:], in_=woven[:].rearrange("p o i r -> p (o i r)")
-            )
-            return codes, scale
-
-        turned = {}
-
-        def back(b, quantised, sums_bank, turned_banks):
-            codes, scale = quantised
-            sums = bank([P, D], sums_bank)
-            for o in range(V_PASSES):
-                nc.tensor.matmul_mx(
-                    out=sums[:],
-                    lhsT=codes[:, P * o : P * (o + 1)].bitcast(E5M2),
-                    lhsT_scale=scale[:, P * o : P * (o + 1)],
-                    rhs=wv_sb[:, o, :].bitcast(E2M1),
-                    rhs_scale=wv_scale[:, o, :],
-                    start=(o == 0),
-                    stop=(o == V_PASSES - 1),
-                )
-            by_lane = tile([P, 2, 2, P], F32, f"by_lane{b}")
-            for odd in range(2):
-                nc.scalar.copy(by_lane[:, odd], sums[:].rearrange("p (m k e) -> p e k m", k=2, e=2)[:, odd])
-            banks = [bank([P, LANES, P], number) for number in turned_banks]
-            for odd in range(2):
-                for k in range(2):
-                    j = 2 * k + odd
-                    turned[b, j] = banks[odd % len(banks)][:, j, :]
-                    nc.tensor.transpose(turned[b, j], by_lane[:, odd, k, :], identity[:])
-
-        def scatter(j, dx, first, count):
+        def vector_scatter(j, dx, first, count):
             nc.vector.tensor_copy(windows[j][:].indirect(listed(first, count)), dx)
 
-        def release(b, lanes, tag):
-            dx = tile([P, len(lanes), P], F32, tag)
-            for k, j in enumerate(lanes):
-                nc.scalar.copy(dx[:, k, :], turned[b, j])
-            for k, j in enumerate(lanes):
-                scatter(j, dx[:, k, :], P * b, P)
+        def on_scalar(sums, tag):
+            dx = tile(list(sums.shape), F32, tag)
+            nc.scalar.copy(dx[:], sums)
+            return dx
 
-        quantise_x(0, "x_codes0")
-        quantise_x(1, "x_codes1")
-        weigh_pass0(0, "x_woven1")
-        weigh_pass1(0, HALF)
+        def on_vector(sums, tag):
+            dx = tile(list(sums.shape), F32, tag)
+            nc.vector.tensor_copy(dx[:], sums)
+            return dx
+
+        both = slice(0, V_PASSES)
+        quantise_x(0, "x_woven0", "x_codes0")
+        wv_scale = tile([P, V_PASSES * D], U8, "x_woven0")
+        deal(nc.vector.tensor_copy, wv_scale[:], wv_scale_raw[:])
+        early_weight = tile([P, V_PASSES, LANES, HALF], F32, "wv_scale_raw")
+        nc.gpsimd.tensor_tensor(early_weight[:, 1, :, :P], group_labels(0, 1), outer[:], MULT)
+        score(0, 1, 0)
+        score(0, 0, 1)
+        quantise_x(1, "woven", "outer")
+        weigh(early_weight[:, 0], 0, 0, HALF)
+        wv_dealt = tile([P, V_PASSES * D], U16, "wv_dealt")
+        deal(nc.scalar.copy, wv_dealt[:], wv_raw[:])
+        score(1, 1, 2)
+        weigh(early_weight[:, 1, :, P:], 1, P, P)
+        score(1, 0, 3)
+        woven = tile([P, V_PASSES, P, LANES], BF16, "woven")
         for o in (1, 0):
-            early_scores(0, o)
-        quantise_x(2, "outer0")
-        weigh_pass0(1, "x_woven2")
+            product_on_gpsimd(woven, 0, early_weight[:, :, :, :P], slice(o, o + 1))
+        weight2 = tile([P, V_PASSES, LANES, P], F32, "weight2")
+        score(2, 1, 4)
+        weigh(weight2[:, 1], 1, HALF, P)
+        quantise_g(woven, group_cols(0))
+        sums0 = back_group(0, range(LANES), 6)
+        scalar_scatter(0, on_scalar(sums0[:, 0, :], "dx00")[:], 0, P)
+        woven = tile([P, V_PASSES, P, LANES], BF16, "woven")
+        product_on_gpsimd(woven, 1, early_weight[:, :, :, P:], both)
+        score(2, 0, 5)
+        weigh(weight2[:, 0], 0, HALF, P)
+        dx = on_scalar(sums0[:, 1:3, :], "margin20")
+        for j in (1, 2):
+            scalar_scatter(j, dx[:, j - 1, :], 0, P)
+        last_weights = {1: weigh_last(1, 2, 3)}
+        score(3, 1, 0)
+        quantise_g(woven, group_cols(1))
+        sums1 = back_group(1, (0, 1, 3), 5)
+        woven = tile([P, V_PASSES, HALF, LANES], BF16, "woven")
+        product_on_gpsimd(woven, 2, weight2, both)
+        last_weights[0] = weigh_last(0, 2, 4)
+        score(3, 0, 1)
         for o in (1, 0):
-            early_scores(1, o)
-        margins = {1: late_margins(1, late_scores(1, (4, 5)))}
-        late_sums = late_scores(0, (6, 0))
-        quantised = quantise_g(0, products(0))
-        margins[0] = late_margins(0, late_sums)
-        back(0, quantised, 1, (2, 0))
-        weigh_pass1(HALF, P)
-        for o in (1, 0):
-            squash(2, o, margins[o][:, :, block_cols(2)])
-        release(0, (0,), "dx00")
-        for o, banks in ((1, (3, 5)), (0, (4, 6))):
-            weigh_last_block(o, *banks)
-        for o in (1, 0):
-            squash(3, o, margins[o][:, :, block_cols(3)])
-        back(1, quantise_g(1, products(1)), 3, (4,))
-        release(0, (2, 1, 3), "dx0")
-        weigh_pass0(2, "weight20")
-        g_block2 = products(2)
-        back(3, quantise_g(3, products(3)), 1, (0,))
-        back(2, quantise_g(2, g_block2), 3, (2,))
-        release(1, range(LANES), "sigmoid30")
+            nc.vector.tensor_tensor(
+                walk_woven(woven[:, o, P:, :]),
+                walk_lanes(sigmoids[LAST][:, o].rearrange("p (r i) -> p r i", r=LANES)),
+                walk_lanes(last_weights[o][:]),
+                MULT,
+            )
+        dx = tile([P, 3, P], F32, "margin30")
+        nc.scalar.copy(dx[:, 2, :], sums0[:, 3, :])
+        nc.scalar.copy(dx[:, :2, :], sums1[:, :2, :])
+        scalar_scatter(3, dx[:, 2, :], 0, P)
+        for j in (1, 0):
+            scalar_scatter(j, dx[:, j, :], P, P)
+        quantise_g(woven, slice(HALF, N))
+        vector_scatter(3, on_vector(sums1[:, 2, :], "woven")[:], P, P)
+        late = {}
+        for j, number in ((1, 0), (0, 1), (3, 2)):
+            late[j] = bank([P, HALF], number)
+            back(late[j][:], j, slice(HALF, N))
+        late[2] = bank([P, N - P], 7)
+        back(late[2][:, :P], 2, group_cols(1))
+        back(late[2][:, P:], 2, slice(HALF, N))
+        vector_scatter(1, on_vector(late[1][:], "dx1")[:], HALF, HALF)
+        scalar_scatter(0, on_scalar(late[0][:], "dx0")[:], HALF, HALF)
 
         out_rows = out_0.rearrange("(p j) c -> p j c", j=LANES)
-        firsts = range(0, T, PIECE)
-        pairs = [sb.tile([P, 2, PIECE, 2], BF16, name=f"pairs{first}") for first in firsts]
-
-        def round_lane(engine_copy, j, k):
-            engine_copy(pairs[k][:, j // 2, :, j % 2], windows[j][:, firsts[k] : firsts[k] + PIECE])
-
-        def round_on_gpsimd(out, in_):
-            nc.gpsimd.tensor_scalar(out, in_, 1.0, -0.0, MULT, ADD)
 
         def store_window(j):
             nc.sync.dma_start(out=out_rows[:, j, :], in_=windows[j][:])
 
-        def late_half(j, tag):
-            dx = tile([P, 2, P], F32, tag)
-            for b in (2, 3):
-                nc.scalar.copy(dx[:, b - 2, :], turned[b, j])
-            return dx[:].rearrange("p b i -> p (b i)")
-
-        last = 1
-        late_dx = {j: late_half(j, f"late_dx{j}") for j in (0, 2, 3)}
-        scatter(0, late_dx[0], HALF, HALF)
-        store_window(0)
-        for k in range(len(firsts)):
-            round_lane(nc.scalar.copy, 0, k)
-        late_dx[last] = late_half(last, "late_dx0")
-        for j in (2, 3):
-            scatter(j, late_dx[j], HALF, HALF)
+        pairs_tile = sb.tile([P, LANES * T], BF16, name="pairs")
+        pairs = pairs_tile[:].rearrange("p (k h c e) -> p k h c e", h=2, c=PIECE, e=2)
+        for j in (1, 0):
             store_window(j)
-            for k in range(len(firsts)):
-                round_lane(round_on_gpsimd if k < len(firsts) // 2 else nc.scalar.copy, j, k)
-        scatter(last, late_dx[last], HALF, HALF)
-        store_window(last)
+            nc.gpsimd.tensor_scalar(
+                pairs[:, : PIECES - 1, 0, :, j],
+                windows[j][:, : T - PIECE].rearrange("p (k c) -> p k c", c=PIECE),
+                1.0,
+                -0.0,
+                MULT,
+                ADD,
+            )
+
+        vector_scatter(3, on_vector(late[3][:], "dx3")[:], HALF, HALF)
+        store_window(3)
+        scalar_scatter(2, on_scalar(late[2][:], "dx2")[:], P, N - P)
+        store_window(2)
+
+        def round_lane(engine_copy, j, k):
+            engine_copy(pairs[:, k, j // 2, :, j % 2], windows[j][:, PIECE * k : PIECE * (k + 1)])
 
         out_scale = sb.tile([P, T], U8, name="out_scale", align_bytes=64)
         out_words = out_1[0].rearrange("p c t -> p (c t)").bitcast(I32)
         woven_out = {}
 
         def join_pairs(engine_copy, word, k):
-            woven_out[k] = sb.tile([P, PIECE, LANES], BF16, name=f"out_woven{firsts[k]}", align_bytes=64)
+            woven_out[k] = sb.tile([P, PIECE, LANES], BF16, name=f"out_woven{k}", align_bytes=64)
             engine_copy(
                 woven_out[k][:].bitcast(word),
-                pairs[k][:].rearrange("p h c e -> p h (c e)").bitcast(word).rearrange("p h c -> p c h"),
+                pairs_tile[:, LANES * PIECE * k : LANES * PIECE * (k + 1)].bitcast(word).rearrange("p (h c) -> p c h", h=2),
             )
 
-        for k in (0, 1, 2):
-            round_lane(nc.vector.tensor_copy, last, k)
-        round_lane(nc.scalar.copy, last, 3)
+        for k in range(PIECES - 1):
+            round_lane(nc.vector.tensor_copy, 3, k)
+        for j in (1, 0):
+            round_lane(nc.vector.tensor_copy, j, PIECES - 1)
+        for k in range(PIECES - 1):
+            round_lane(nc.vector.tensor_copy, 2, k)
+        for j in (3, 2):
+            round_lane(nc.scalar.copy, j, PIECES - 1)
         for k in (0, 1):
             join_pairs(nc.vector.tensor_copy, I32, k)
         for k in (3, 2):
             join_pairs(nc.scalar.copy, U32, k)
         out_codes = sb.tile([P, T], U32, name="out_codes", align_bytes=64)
-        stored = 0
-        for k, first in enumerate(firsts):
-            cols = slice(first, first + PIECE)
+        for k in range(PIECES):
+            cols = slice(PIECE * k, PIECE * (k + 1))
             nc.vector.quantize_mx(
                 out=out_codes[:, cols].bitcast(E4M3),
                 scales=out_scale[:, cols],
                 in_=woven_out[k][:].rearrange("p c j -> p (c j)"),
             )
-            if k > 0:
-                unstored = slice(stored, first + PIECE)
-                nc.sync.dma_start(out=out_words[:, unstored], in_=out_codes[:, unstored].bitcast(I32))
-                stored = first + PIECE
+            if k % 2 == 1:
+                two = slice(PIECE * (k - 1), PIECE * (k + 1))
+                nc.sync.dma_start(out=out_words[:, two], in_=out_codes[:, two].bitcast(I32))
         for q in range(QUADRANTS):
             queue = nc.scalar if q % 2 == 0 else nc.sync
             queue.dma_start(

@@ -23,8 +23,6 @@ P = 128
 LANES = 4
 K_PASS = P * LANES
 V_PASSES = V // K_PASS
-GROUPS = N // P
-LAST = GROUPS - 1
 QUADRANTS = 4
 PER_COLUMN = 16
 RUN = 4
@@ -46,10 +44,6 @@ def walk_woven(woven):
 
 def walk_lanes(lanes):
     return lanes.rearrange("p r (c i) -> p c r i", i=RUN)
-
-
-def by_position(lanes):
-    return lanes.rearrange("p r i -> p i r")
 
 
 def by_four(run):
@@ -120,13 +114,13 @@ def tile_attend_gml_pl_sig_kernel(
         def group_labels(b, o):
             return labels[b // 2, o][:, :, group_cols(b % 2)]
 
+        load_labels(0, 1)
         for q in range(QUADRANTS):
             nc.sync.dma_start(
                 out=wv_scale_raw[32 * q : 32 * q + 4, :].bitcast(I32).rearrange("f (o w) -> f o w", o=V_PASSES),
                 in_=wv_scales[:, 4 * q : 4 * q + 4, :].bitcast(I32).rearrange("o f w -> f o w"),
             )
-        for o in (1, 0):
-            load_labels(0, o)
+        load_labels(0, 0)
         wv_raw = tile([P, V_PASSES * D], U16, "wv_raw")
         nc.sync.dma_start(
             out=wv_raw[:].bitcast(I32).rearrange("p (o w) -> p o w", o=V_PASSES),
@@ -134,9 +128,6 @@ def tile_attend_gml_pl_sig_kernel(
         )
         for o in (1, 0):
             load_labels(1, o)
-        rw_last = tile([P, 1], F32, "rw_last")
-        with nc.allow_non_contiguous_dma(reason="one weight a partition"):
-            nc.sync.dma_start(out=rw_last[:], in_=rw[0, N - P :].rearrange("(p one) -> p one", one=1))
 
         neg_cw = tile([P, V_PASSES * LANES], F32, "neg_cw")
         nc.scalar.activation(neg_cw[:], cw_sb[:].rearrange("p o r -> p (o r)"), ACT.Copy, scale=-1.0)
@@ -146,18 +137,6 @@ def tile_attend_gml_pl_sig_kernel(
 
         def rw_rows(first, count):
             return rw_bank[:].rearrange("p k n -> p n k")[:, first // LANES : (first + count) // LANES, :]
-
-        outer = tile([P, LANES, P], F32, "outer")
-        for r in range(LANES):
-            k = LANES + r
-            nc.scalar.activation(by_four(outer[:, r, :]), rw_rows(0, P), ACT.Copy, scale=neg_cw[:, k : k + 1])
-        cw_rows = tile([P, V_PASSES, LANES, P], F32, "cw_rows")
-        for o in range(V_PASSES):
-            spread = bank([P, LANES, P], o)
-            for r in range(LANES):
-                k = LANES * o + r
-                nc.tensor.transpose(spread[:, r, :], neg_cw[:, k : k + 1].to_broadcast([P, P]), identity[:])
-            nc.scalar.copy(cw_rows[:, o], spread[:])
 
         wd_dealt = tile([P, V], U16, "wd_dealt")
         deal(nc.vector.tensor_copy, wd_dealt[:], wd_raw[:])
@@ -195,8 +174,9 @@ def tile_attend_gml_pl_sig_kernel(
                 x_codes[b] = codes[:, P * b - first : P * (b + 1) - first]
 
         sigmoids = {}
+        weights = {}
 
-        def score(b, o, number):
+        def score(b, o, number, margin_tag):
             sums = bank([P, LANES, P], number)
             for r in range(LANES):
                 cols = slice(K_PASS * o + P * r, K_PASS * o + P * (r + 1))
@@ -209,83 +189,61 @@ def tile_attend_gml_pl_sig_kernel(
                     start=True,
                     stop=True,
                 )
-            margin = tile([P, LANES, P], F32, f"margin{b}{o}")
+            margin = tile([P, LANES, P], F32, margin_tag)
             nc.vector.tensor_tensor(margin[:], sums[:], group_labels(b, o), MULT)
-            if b not in sigmoids:
-                sigmoids[b] = tile([P, V_PASSES, K_PASS], F32, f"sigmoid{b}")
-            if b == LAST:
-                source, out = margin[:], sigmoids[b][:, o].rearrange("p (r i) -> p r i", r=LANES)
-            else:
-                source, out = by_position(margin[:]), sigmoids[b][:, o].rearrange("p (i r) -> p i r", r=LANES)
-            nc.scalar.activation(out, source, ACT.Sigmoid, scale=-1.0)
+            return margin
 
-        def weigh(out, o, first, count):
+        def squash(b, o, margin):
+            sigmoids[b, o] = tile([P, LANES, P], F32, f"sigmoid{b}{o}")
+            nc.scalar.activation(sigmoids[b, o][:], margin[:], ACT.Sigmoid, scale=-1.0)
+
+        def weigh(o, first, count):
             h, start = divmod(first, HALF)
+            weight = tile([P, LANES, count], F32, f"weight{first}_{o}")
             for r in range(LANES):
                 k = LANES * o + r
                 nc.vector.scalar_tensor_tensor(
-                    by_four(out[:, r, :]),
+                    by_four(weight[:, r, :]),
                     by_four(labels[h, o][:, r, start : start + count]),
                     neg_cw[:, k : k + 1],
                     rw_rows(first, count),
                     MULT,
                     MULT,
                 )
+            for k in range(count // P):
+                weights[first // P + k, o] = weight[:, :, group_cols(k)]
 
-        def weigh_last(o, stage_bank, weight_bank):
-            stage = bank([P, LANES, P], stage_bank)
-            for r in range(LANES):
-                nc.tensor.transpose(stage[:, r, :], group_labels(LAST, o)[:, r, :], identity[:])
-            rows = tile([P, LANES, P], F32, f"weight_rows{o}")
-            nc.vector.scalar_tensor_tensor(
-                rows[:].rearrange("p r m -> p (r m)"),
-                stage[:].rearrange("p r m -> p (r m)"),
-                rw_last[:],
-                cw_rows[:, o].rearrange("p r m -> p (r m)"),
-                MULT,
-                MULT,
-            )
-            weight = bank([P, LANES, P], weight_bank)
-            for r in range(LANES):
-                nc.tensor.transpose(weight[:, r, :], rows[:, r, :], identity[:])
-            return weight
+        g_codes = {}
+        g_scales = {}
 
-        g_codes = [tile([P, N], U32, f"g_codes{o}") for o in range(V_PASSES)]
-        g_scales = [tile([P, N], U8, f"g_scale{o}") for o in range(V_PASSES)]
-
-        def product_on_gpsimd(woven, b, weight, passes):
-            nc.gpsimd.tensor_tensor(
-                woven[:, passes, :P, :],
-                sigmoids[b][:, passes].rearrange("p o (i r) -> p o i r", r=LANES),
-                weight[:, passes].rearrange("p o r i -> p o i r"),
-                MULT,
+        def form_g(b):
+            woven = tile([P, V_PASSES, P, LANES], BF16, f"g_woven{b}")
+            for o in (1, 0):
+                nc.vector.tensor_tensor(
+                    walk_woven(woven[:, o]), walk_lanes(sigmoids[b, o][:]), walk_lanes(weights[b, o]), MULT
+                )
+            g_codes[b] = tile([P, V_PASSES * P], U32, f"g_codes{b}")
+            g_scales[b] = tile([P, V_PASSES * P], U8, f"g_scale{b}")
+            nc.vector.quantize_mx(
+                out=g_codes[b][:].bitcast(E5M2),
+                scales=g_scales[b][:],
+                in_=woven[:].rearrange("p o i r -> p (o i r)"),
             )
 
-        def quantise_g(woven, cols):
-            for o in (1, 0):
-                nc.vector.quantize_mx(
-                    out=g_codes[o][:, cols].bitcast(E5M2),
-                    scales=g_scales[o][:, cols],
-                    in_=woven[:, o].rearrange("p i r -> p (i r)"),
-                )
-
-        def back(out, j, cols):
-            for o in (1, 0):
-                dealt = slice(D * o + P * j, D * o + P * (j + 1))
-                nc.tensor.matmul_mx(
-                    out=out,
-                    lhsT=wv_dealt[:, dealt].bitcast(E2M1),
-                    lhsT_scale=wv_scale[:, dealt],
-                    rhs=g_codes[o][:, cols].bitcast(E5M2),
-                    rhs_scale=g_scales[o][:, cols],
-                    start=(o == 1),
-                    stop=(o == 0),
-                )
-
-        def back_group(b, lanes, number):
+        def back(b, lanes, number):
             sums = bank([P, len(lanes), P], number)
             for k, j in enumerate(lanes):
-                back(sums[:, k, :], j, group_cols(b))
+                for o in range(V_PASSES):
+                    dealt = slice(D * o + P * j, D * o + P * (j + 1))
+                    nc.tensor.matmul_mx(
+                        out=sums[:, k, :],
+                        lhsT=wv_dealt[:, dealt].bitcast(E2M1),
+                        lhsT_scale=wv_scale[:, dealt],
+                        rhs=g_codes[b][:, group_cols(o)].bitcast(E5M2),
+                        rhs_scale=g_scales[b][:, group_cols(o)],
+                        start=(o == 0),
+                        stop=(o == V_PASSES - 1),
+                    )
             return sums
 
         def scalar_scatter(j, dx, first, count):
@@ -294,79 +252,54 @@ def tile_attend_gml_pl_sig_kernel(
         def vector_scatter(j, dx, first, count):
             nc.vector.tensor_copy(windows[j][:].indirect(listed(first, count)), dx)
 
-        def on_scalar(sums, tag):
-            dx = tile(list(sums.shape), F32, tag)
-            nc.scalar.copy(dx[:], sums)
-            return dx
+        def release_on_scalar(b, sums, lanes, tag):
+            dx = tile([P, len(lanes), P], F32, tag)
+            nc.scalar.copy(dx[:], sums[:, lanes[0] : lanes[-1] + 1, :])
+            for k, j in enumerate(lanes):
+                scalar_scatter(j, dx[:, k, :], P * b, P)
 
-        def on_vector(sums, tag):
-            dx = tile(list(sums.shape), F32, tag)
-            nc.vector.tensor_copy(dx[:], sums)
-            return dx
-
-        both = slice(0, V_PASSES)
         quantise_x(0, "x_woven0", "x_codes0")
+        weigh(1, 0, P)
+        squash(0, 1, score(0, 1, 0, "margin01"))
         wv_scale = tile([P, V_PASSES * D], U8, "x_woven0")
         deal(nc.vector.tensor_copy, wv_scale[:], wv_scale_raw[:])
-        early_weight = tile([P, V_PASSES, LANES, HALF], F32, "wv_scale_raw")
-        nc.gpsimd.tensor_tensor(early_weight[:, 1, :, :P], group_labels(0, 1), outer[:], MULT)
-        score(0, 1, 0)
-        score(0, 0, 1)
-        quantise_x(1, "woven", "outer")
-        weigh(early_weight[:, 0], 0, 0, HALF)
+        squash(0, 0, score(0, 0, 1, "margin00"))
+        weigh(0, 0, P)
+        quantise_x(1, "x_woven1", "x_codes1")
         wv_dealt = tile([P, V_PASSES * D], U16, "wv_dealt")
         deal(nc.scalar.copy, wv_dealt[:], wv_raw[:])
-        score(1, 1, 2)
-        weigh(early_weight[:, 1, :, P:], 1, P, P)
-        score(1, 0, 3)
-        woven = tile([P, V_PASSES, P, LANES], BF16, "woven")
+        form_g(0)
+        margins = {}
         for o in (1, 0):
-            product_on_gpsimd(woven, 0, early_weight[:, :, :, :P], slice(o, o + 1))
-        weight2 = tile([P, V_PASSES, LANES, P], F32, "weight2")
-        score(2, 1, 4)
-        weigh(weight2[:, 1], 1, HALF, P)
-        quantise_g(woven, group_cols(0))
-        sums0 = back_group(0, range(LANES), 6)
-        scalar_scatter(0, on_scalar(sums0[:, 0, :], "dx00")[:], 0, P)
-        woven = tile([P, V_PASSES, P, LANES], BF16, "woven")
-        product_on_gpsimd(woven, 1, early_weight[:, :, :, P:], both)
-        score(2, 0, 5)
-        weigh(weight2[:, 0], 0, HALF, P)
-        dx = on_scalar(sums0[:, 1:3, :], "margin20")
-        for j in (1, 2):
-            scalar_scatter(j, dx[:, j - 1, :], 0, P)
-        last_weights = {1: weigh_last(1, 2, 3)}
-        score(3, 1, 0)
-        quantise_g(woven, group_cols(1))
-        sums1 = back_group(1, (0, 1, 3), 5)
-        woven = tile([P, V_PASSES, HALF, LANES], BF16, "woven")
-        product_on_gpsimd(woven, 2, weight2, both)
-        last_weights[0] = weigh_last(0, 2, 4)
-        score(3, 0, 1)
+            margins[1, o] = score(1, o, 2 + o, f"margin1{o}")
+        sums0 = back(0, range(LANES), 6)
+        release_on_scalar(0, sums0, (0, 1), "dx0")
         for o in (1, 0):
-            nc.vector.tensor_tensor(
-                walk_woven(woven[:, o, P:, :]),
-                walk_lanes(sigmoids[LAST][:, o].rearrange("p (r i) -> p r i", r=LANES)),
-                walk_lanes(last_weights[o][:]),
-                MULT,
-            )
-        dx = tile([P, 3, P], F32, "margin30")
-        nc.scalar.copy(dx[:, 2, :], sums0[:, 3, :])
-        nc.scalar.copy(dx[:, :2, :], sums1[:, :2, :])
-        scalar_scatter(3, dx[:, 2, :], 0, P)
-        for j in (1, 0):
-            scalar_scatter(j, dx[:, j, :], P, P)
-        quantise_g(woven, slice(HALF, N))
-        vector_scatter(3, on_vector(sums1[:, 2, :], "woven")[:], P, P)
-        late = {}
-        for j, number in ((1, 0), (0, 1), (3, 2)):
-            late[j] = bank([P, HALF], number)
-            back(late[j][:], j, slice(HALF, N))
-        late[2] = bank([P, N - P], 7)
-        back(late[2][:, :P], 2, group_cols(1))
-        back(late[2][:, P:], 2, slice(HALF, N))
-        vector_scatter(1, on_vector(late[1][:], "dx1")[:], HALF, HALF)
-        scalar_scatter(0, on_scalar(late[0][:], "dx0")[:], HALF, HALF)
+            squash(1, o, margins[1, o])
+        for o in (1, 0):
+            margins[2, o] = score(2, o, 4 + o, f"margin2{o}")
+        for o in (1, 0):
+            margins[3, o] = score(3, o, o, f"margin3{o}")
+        release_on_scalar(0, sums0, (2, 3), "margin10")
+        for b in (2, 3):
+            for o in (1, 0):
+                squash(b, o, margins[b, o])
+        for o in (1, 0):
+            weigh(o, P, P)
+        form_g(1)
+        release_on_scalar(1, back(1, range(LANES), 2), range(LANES), "margin30")
+        for o in (1, 0):
+            weigh(o, HALF, HALF)
+        form_g(2)
+        late = {(2, odd): back(2, (odd, odd + 2), 3 + odd) for odd in (1, 0)}
+        form_g(3)
+        late.update({(3, odd): back(3, (odd, odd + 2), 5 + odd) for odd in (1, 0)})
+        for odd, engine_copy, scatter in ((1, nc.vector.tensor_copy, vector_scatter), (0, nc.scalar.copy, scalar_scatter)):
+            dx = tile([P, 2, HALF], F32, f"late_dx{odd}")
+            for b in (2, 3):
+                engine_copy(dx[:, :, group_cols(b - 2)], late[b, odd][:])
+                scatter(odd, dx[:, 0, group_cols(b - 2)], P * b, P)
+            scatter(odd + 2, dx[:, 1, :], HALF, HALF)
 
         out_rows = out_0.rearrange("(p j) c -> p j c", j=LANES)
 
@@ -386,10 +319,8 @@ def tile_attend_gml_pl_sig_kernel(
                 ADD,
             )
 
-        vector_scatter(3, on_vector(late[3][:], "dx3")[:], HALF, HALF)
-        store_window(3)
-        scalar_scatter(2, on_scalar(late[2][:], "dx2")[:], P, N - P)
-        store_window(2)
+        for j in (3, 2):
+            store_window(j)
 
         def round_lane(engine_copy, j, k):
             engine_copy(pairs[:, k, j // 2, :, j % 2], windows[j][:, PIECE * k : PIECE * (k + 1)])

@@ -16,13 +16,13 @@ E4M3 = mybir.dt.float8_e4m3fn_x4
 E5M2 = mybir.dt.float8_e5m2_x4
 E2M1 = mybir.dt.float4_e2m1fn_x4
 MULT = mybir.AluOpType.mult
-ADD = mybir.AluOpType.add
 ACT = mybir.ActivationFunctionType
 
 P = 128
 LANES = 4
 K_PASS = P * LANES
 V_PASSES = V // K_PASS
+GROUPS = N // P
 QUADRANTS = 4
 PER_COLUMN = 16
 RUN = 4
@@ -91,10 +91,16 @@ def tile_attend_gml_pl_sig_kernel(
         def load_x(t):
             nc.sync.dma_start(out=x_lanes[t][:], in_=x_rows[:, t, :])
 
+        nc.gpsimd.memset(wv_scale_raw[:].bitcast(U32), 0)
         for t in (0, 1):
             load_x(t)
         nc.sync.dma_start(out=rw_cols[:], in_=rw[0].rearrange("(p k) -> p k", k=LANES))
         nc.sync.dma_start(out=cw_sb[:], in_=cw.rearrange("(o p r) one -> p o (r one)", p=P, r=LANES))
+        for q in range(QUADRANTS):
+            nc.sync.dma_start(
+                out=wv_scale_raw[32 * q : 32 * q + 4, :].bitcast(I32).rearrange("f (o w) -> f o w", o=V_PASSES),
+                in_=wv_scales[:, 4 * q : 4 * q + 4, :].bitcast(I32).rearrange("o f w -> f o w"),
+            )
         for t in (2, 3):
             load_x(t)
         warm = tile([P, 8], F32, "warm")
@@ -102,7 +108,6 @@ def tile_attend_gml_pl_sig_kernel(
         nc.scalar.activation(warm[:], warm[:], ACT.Sigmoid)
         identity = tile([P, P], F32, "identity")
         make_identity(nc, identity[:])
-        nc.gpsimd.memset(wv_scale_raw[:].bitcast(U32), 0)
 
         y_rows = y.rearrange("(o p r) i -> o p r i", p=P, r=LANES)
         labels = {}
@@ -114,13 +119,8 @@ def tile_attend_gml_pl_sig_kernel(
         def group_labels(b, o):
             return labels[b // 2, o][:, :, group_cols(b % 2)]
 
-        load_labels(0, 1)
-        for q in range(QUADRANTS):
-            nc.sync.dma_start(
-                out=wv_scale_raw[32 * q : 32 * q + 4, :].bitcast(I32).rearrange("f (o w) -> f o w", o=V_PASSES),
-                in_=wv_scales[:, 4 * q : 4 * q + 4, :].bitcast(I32).rearrange("o f w -> f o w"),
-            )
-        load_labels(0, 0)
+        for o in (1, 0):
+            load_labels(0, o)
         wv_raw = tile([P, V_PASSES * D], U16, "wv_raw")
         nc.sync.dma_start(
             out=wv_raw[:].bitcast(I32).rearrange("p (o w) -> p o w", o=V_PASSES),
@@ -139,7 +139,7 @@ def tile_attend_gml_pl_sig_kernel(
             return rw_bank[:].rearrange("p k n -> p n k")[:, first // LANES : (first + count) // LANES, :]
 
         wd_dealt = tile([P, V], U16, "wd_dealt")
-        deal(nc.vector.tensor_copy, wd_dealt[:], wd_raw[:])
+        deal(nc.scalar.copy, wd_dealt[:], wd_raw[:])
         wd_scale = tile([P, V], U8, "wd_scale")
         deal(nc.vector.tensor_copy, wd_scale[:], wd_scale_raw[:])
 
@@ -152,8 +152,11 @@ def tile_attend_gml_pl_sig_kernel(
             nc.vector.tensor_copy(out, x_lanes[t][:].indirect(listed(first, count)))
 
         picked = tile([P, LANES, N], BF16, "picked")
-        for t in range(LANES - 1):
-            gather(picked[:, t, :], t, 0, N)
+        gather(picked[:, 0, :], 0, 0, N)
+        nc.scalar.activation(picked[:, 1, :], x_lanes[1][:].indirect(offsets[:]), ACT.Copy)
+        wv_scale = tile([P, V_PASSES * D], U8, "wv_scale")
+        deal(nc.vector.tensor_copy, wv_scale[:], wv_scale_raw[:])
+        gather(picked[:, 2, :], 2, 0, N)
         spans = ((0, P), (P, N - P))
         for first, count in spans:
             gather(picked[:, LANES - 1, first : first + count], LANES - 1, first, count)
@@ -173,10 +176,11 @@ def tile_attend_gml_pl_sig_kernel(
             for b in range(first // P, (first + count) // P):
                 x_codes[b] = codes[:, P * b - first : P * (b + 1) - first]
 
-        sigmoids = {}
-        weights = {}
+        margins = [tile([P, LANES, V_PASSES, P], F32, f"margin{b}") for b in range(GROUPS)]
+        sigmoids = [tile([P, LANES, V_PASSES, P], F32, f"sigmoid{b}") for b in range(GROUPS)]
+        weights = [tile([P, LANES, V_PASSES, HALF], F32, f"weight{h}") for h in range(2)]
 
-        def score(b, o, number, margin_tag):
+        def score(b, o, number):
             sums = bank([P, LANES, P], number)
             for r in range(LANES):
                 cols = slice(K_PASS * o + P * r, K_PASS * o + P * (r + 1))
@@ -189,29 +193,23 @@ def tile_attend_gml_pl_sig_kernel(
                     start=True,
                     stop=True,
                 )
-            margin = tile([P, LANES, P], F32, margin_tag)
-            nc.vector.tensor_tensor(margin[:], sums[:], group_labels(b, o), MULT)
-            return margin
+            nc.vector.tensor_tensor(margins[b][:, :, o, :], sums[:], group_labels(b, o), MULT)
 
-        def squash(b, o, margin):
-            sigmoids[b, o] = tile([P, LANES, P], F32, f"sigmoid{b}{o}")
-            nc.scalar.activation(sigmoids[b, o][:], margin[:], ACT.Sigmoid, scale=-1.0)
+        def squash(b, passes):
+            nc.scalar.activation(sigmoids[b][:, :, passes, :], margins[b][:, :, passes, :], ACT.Sigmoid, scale=-1.0)
 
         def weigh(o, first, count):
             h, start = divmod(first, HALF)
-            weight = tile([P, LANES, count], F32, f"weight{first}_{o}")
             for r in range(LANES):
                 k = LANES * o + r
                 nc.vector.scalar_tensor_tensor(
-                    by_four(weight[:, r, :]),
+                    by_four(weights[h][:, r, o, start : start + count]),
                     by_four(labels[h, o][:, r, start : start + count]),
                     neg_cw[:, k : k + 1],
                     rw_rows(first, count),
                     MULT,
                     MULT,
                 )
-            for k in range(count // P):
-                weights[first // P + k, o] = weight[:, :, group_cols(k)]
 
         g_codes = {}
         g_scales = {}
@@ -220,7 +218,10 @@ def tile_attend_gml_pl_sig_kernel(
             woven = tile([P, V_PASSES, P, LANES], BF16, f"g_woven{b}")
             for o in (1, 0):
                 nc.vector.tensor_tensor(
-                    walk_woven(woven[:, o]), walk_lanes(sigmoids[b, o][:]), walk_lanes(weights[b, o]), MULT
+                    walk_woven(woven[:, o]),
+                    walk_lanes(sigmoids[b][:, :, o, :]),
+                    walk_lanes(weights[b // 2][:, :, o, group_cols(b % 2)]),
+                    MULT,
                 )
             g_codes[b] = tile([P, V_PASSES * P], U32, f"g_codes{b}")
             g_scales[b] = tile([P, V_PASSES * P], U8, f"g_scale{b}")
@@ -258,48 +259,55 @@ def tile_attend_gml_pl_sig_kernel(
             for k, j in enumerate(lanes):
                 scalar_scatter(j, dx[:, k, :], P * b, P)
 
+        both = slice(0, V_PASSES)
         quantise_x(0, "x_woven0", "x_codes0")
         weigh(1, 0, P)
-        squash(0, 1, score(0, 1, 0, "margin01"))
-        wv_scale = tile([P, V_PASSES * D], U8, "x_woven0")
-        deal(nc.vector.tensor_copy, wv_scale[:], wv_scale_raw[:])
-        squash(0, 0, score(0, 0, 1, "margin00"))
+        score(0, 1, 0)
+        squash(0, slice(1, 2))
+        score(0, 0, 1)
+        squash(0, slice(0, 1))
         weigh(0, 0, P)
         quantise_x(1, "x_woven1", "x_codes1")
         wv_dealt = tile([P, V_PASSES * D], U16, "wv_dealt")
         deal(nc.scalar.copy, wv_dealt[:], wv_raw[:])
         form_g(0)
-        margins = {}
         for o in (1, 0):
-            margins[1, o] = score(1, o, 2 + o, f"margin1{o}")
+            score(1, o, 2 + o)
         sums0 = back(0, range(LANES), 6)
         release_on_scalar(0, sums0, (0, 1), "dx0")
+        squash(1, both)
         for o in (1, 0):
-            squash(1, o, margins[1, o])
+            score(2, o, 4 + o)
         for o in (1, 0):
-            margins[2, o] = score(2, o, 4 + o, f"margin2{o}")
-        for o in (1, 0):
-            margins[3, o] = score(3, o, o, f"margin3{o}")
-        release_on_scalar(0, sums0, (2, 3), "margin10")
+            score(3, o, o)
+        release_on_scalar(0, sums0, (2, 3), "margin1")
         for b in (2, 3):
-            for o in (1, 0):
-                squash(b, o, margins[b, o])
+            squash(b, both)
         for o in (1, 0):
             weigh(o, P, P)
         form_g(1)
-        release_on_scalar(1, back(1, range(LANES), 2), range(LANES), "margin30")
+        release_on_scalar(1, back(1, range(LANES), 2), range(LANES), "margin3")
         for o in (1, 0):
             weigh(o, HALF, HALF)
         form_g(2)
-        late = {(2, odd): back(2, (odd, odd + 2), 3 + odd) for odd in (1, 0)}
+        vector_sums = {2: back(2, (1, 3), 3)}
+        scalar_sums = {2: back(2, (0, 2), 4)}
         form_g(3)
-        late.update({(3, odd): back(3, (odd, odd + 2), 5 + odd) for odd in (1, 0)})
-        for odd, engine_copy, scatter in ((1, nc.vector.tensor_copy, vector_scatter), (0, nc.scalar.copy, scalar_scatter)):
-            dx = tile([P, 2, HALF], F32, f"late_dx{odd}")
-            for b in (2, 3):
-                engine_copy(dx[:, :, group_cols(b - 2)], late[b, odd][:])
-                scatter(odd, dx[:, 0, group_cols(b - 2)], P * b, P)
-            scatter(odd + 2, dx[:, 1, :], HALF, HALF)
+        vector_sums[3] = back(3, (1,), 5)
+        scalar_sums[3] = back(3, (0, 2, 3), 6)
+        dx = tile([P, 3, P], F32, "vector_dx")
+        nc.vector.tensor_copy(dx[:, :2, :], vector_sums[2][:])
+        for k, j in enumerate((1, 3)):
+            vector_scatter(j, dx[:, k, :], HALF, P)
+        nc.vector.tensor_copy(dx[:, 2:, :], vector_sums[3][:])
+        vector_scatter(1, dx[:, 2, :], HALF + P, P)
+        dx = tile([P, 3, HALF], F32, "scalar_dx")
+        nc.scalar.copy(dx[:, :2, :P], scalar_sums[2][:])
+        scalar_scatter(0, dx[:, 0, :P], HALF, P)
+        nc.scalar.copy(dx[:, :, P:], scalar_sums[3][:])
+        scalar_scatter(0, dx[:, 0, P:], HALF + P, P)
+        scalar_scatter(2, dx[:, 1, :], HALF, HALF)
+        scalar_scatter(3, dx[:, 2, P:], HALF + P, P)
 
         out_rows = out_0.rearrange("(p j) c -> p j c", j=LANES)
 
@@ -308,22 +316,13 @@ def tile_attend_gml_pl_sig_kernel(
 
         pairs_tile = sb.tile([P, LANES * T], BF16, name="pairs")
         pairs = pairs_tile[:].rearrange("p (k h c e) -> p k h c e", h=2, c=PIECE, e=2)
-        for j in (1, 0):
+        for j in (1, 0, 2, 3):
             store_window(j)
-            nc.gpsimd.tensor_scalar(
-                pairs[:, : PIECES - 1, 0, :, j],
-                windows[j][:, : T - PIECE].rearrange("p (k c) -> p k c", c=PIECE),
-                1.0,
-                -0.0,
-                MULT,
-                ADD,
+
+        def round_lane(engine_copy, j, pieces):
+            engine_copy(
+                pairs[:, pieces, j // 2, :, j % 2], windows[j][:].rearrange("p (k c) -> p k c", c=PIECE)[:, pieces, :]
             )
-
-        for j in (3, 2):
-            store_window(j)
-
-        def round_lane(engine_copy, j, k):
-            engine_copy(pairs[:, k, j // 2, :, j % 2], windows[j][:, PIECE * k : PIECE * (k + 1)])
 
         out_scale = sb.tile([P, T], U8, name="out_scale", align_bytes=64)
         out_words = out_1[0].rearrange("p c t -> p (c t)").bitcast(I32)
@@ -336,14 +335,13 @@ def tile_attend_gml_pl_sig_kernel(
                 pairs_tile[:, LANES * PIECE * k : LANES * PIECE * (k + 1)].bitcast(word).rearrange("p (h c) -> p c h", h=2),
             )
 
-        for k in range(PIECES - 1):
-            round_lane(nc.vector.tensor_copy, 3, k)
         for j in (1, 0):
-            round_lane(nc.vector.tensor_copy, j, PIECES - 1)
-        for k in range(PIECES - 1):
-            round_lane(nc.vector.tensor_copy, 2, k)
-        for j in (3, 2):
-            round_lane(nc.scalar.copy, j, PIECES - 1)
+            round_lane(nc.vector.tensor_copy, j, slice(0, PIECES))
+        for j in (2, 3):
+            for k in range(PIECES - 1):
+                round_lane(nc.vector.tensor_copy, j, slice(k, k + 1))
+        for j in (2, 3):
+            round_lane(nc.scalar.copy, j, slice(PIECES - 1, PIECES))
         for k in (0, 1):
             join_pairs(nc.vector.tensor_copy, I32, k)
         for k in (3, 2):

@@ -143,10 +143,25 @@ def tile_attend_gml_pl_sig_kernel(
         wd_scale = tile([P, V], U8, "wd_scale")
         deal(nc.vector.tensor_copy, wd_scale[:], wd_scale_raw[:])
 
-        windows = []
-        for engine, tag in ((nc.vector, "window0"), (nc.vector, "window1"), (nc.gpsimd, "wd_raw"), (nc.gpsimd, "wd_scale_raw")):
-            windows.append(tile([P, T], F32, tag))
-            engine.memset(windows[-1][:].bitcast(U32), 0)
+        late_rw = tile([P, HALF], F32, "late_rw")
+        nc.scalar.copy(by_four(late_rw[:]), rw_rows(HALF, HALF))
+        outer = {}
+
+        def make_outer(o, tag):
+            outer[o] = tile([P, LANES, HALF], F32, tag)
+            nc.gpsimd.tensor_tensor(
+                outer[o][:],
+                late_rw[:].unsqueeze(1).to_broadcast([P, LANES, HALF]),
+                neg_cw[:, LANES * o : LANES * (o + 1)].unsqueeze(2).to_broadcast([P, LANES, HALF]),
+                MULT,
+            )
+
+        make_outer(1, "outer1")
+
+        windows = [tile([P, T], F32, f"window{j}") for j in range(LANES)]
+        for j in range(LANES):
+            engine = nc.vector if j < 2 else nc.gpsimd
+            engine.memset(windows[j][:].bitcast(U32), 0)
 
         def gather(out, t, first, count):
             nc.vector.tensor_copy(out, x_lanes[t][:].indirect(listed(first, count)))
@@ -158,17 +173,17 @@ def tile_attend_gml_pl_sig_kernel(
         deal(nc.vector.tensor_copy, wv_scale[:], wv_scale_raw[:])
         gather(picked[:, 2, :], 2, 0, N)
         spans = ((0, P), (P, N - P))
-        for first, count in spans:
-            gather(picked[:, LANES - 1, first : first + count], LANES - 1, first, count)
+        gather(picked[:, LANES - 1, :P], LANES - 1, 0, P)
+        nc.scalar.activation(picked[:, LANES - 1, P:], x_lanes[LANES - 1][:].indirect(listed(P, N - P)), ACT.Copy)
 
         x_codes = {}
         x_scale = tile([P, N], U8, "x_scale")
 
-        def quantise_x(span, woven_tag, codes_tag):
+        def quantise_x(span, engine_copy, woven_tag, codes_tag):
             first, count = spans[span]
             cols = slice(first, first + count)
             woven = tile([P, count, LANES], BF16, woven_tag)
-            nc.scalar.copy(walk_woven(woven[:]), walk_lanes(picked[:, :, cols]))
+            engine_copy(walk_woven(woven[:]), walk_lanes(picked[:, :, cols]))
             codes = tile([P, count], U32, codes_tag)
             nc.vector.quantize_mx(
                 out=codes[:].bitcast(E4M3), scales=x_scale[:, cols], in_=woven[:].rearrange("p i t -> p (i t)")
@@ -178,7 +193,7 @@ def tile_attend_gml_pl_sig_kernel(
 
         margins = [tile([P, LANES, V_PASSES, P], F32, f"margin{b}") for b in range(GROUPS)]
         sigmoids = [tile([P, LANES, V_PASSES, P], F32, f"sigmoid{b}") for b in range(GROUPS)]
-        weights = [tile([P, LANES, V_PASSES, HALF], F32, f"weight{h}") for h in range(2)]
+        weights = {}
 
         def score(b, o, number):
             sums = bank([P, LANES, P], number)
@@ -198,15 +213,14 @@ def tile_attend_gml_pl_sig_kernel(
         def squash(b, passes):
             nc.scalar.activation(sigmoids[b][:, :, passes, :], margins[b][:, :, passes, :], ACT.Sigmoid, scale=-1.0)
 
-        def weigh(o, first, count):
-            h, start = divmod(first, HALF)
+        def weigh(b, o):
             for r in range(LANES):
                 k = LANES * o + r
                 nc.vector.scalar_tensor_tensor(
-                    by_four(weights[h][:, r, o, start : start + count]),
-                    by_four(labels[h, o][:, r, start : start + count]),
+                    by_four(weights[b][:, r, o, :]),
+                    by_four(group_labels(b, o)[:, r, :]),
                     neg_cw[:, k : k + 1],
-                    rw_rows(first, count),
+                    rw_rows(P * b, P),
                     MULT,
                     MULT,
                 )
@@ -220,7 +234,7 @@ def tile_attend_gml_pl_sig_kernel(
                 nc.vector.tensor_tensor(
                     walk_woven(woven[:, o]),
                     walk_lanes(sigmoids[b][:, :, o, :]),
-                    walk_lanes(weights[b // 2][:, :, o, group_cols(b % 2)]),
+                    walk_lanes(weights[b][:, :, o, :]),
                     MULT,
                 )
             g_codes[b] = tile([P, V_PASSES * P], U32, f"g_codes{b}")
@@ -255,59 +269,72 @@ def tile_attend_gml_pl_sig_kernel(
 
         def release_on_scalar(b, sums, lanes, tag):
             dx = tile([P, len(lanes), P], F32, tag)
-            nc.scalar.copy(dx[:], sums[:, lanes[0] : lanes[-1] + 1, :])
-            for k, j in enumerate(lanes):
+            nc.scalar.copy(dx[:], sums[:, min(lanes) : max(lanes) + 1, :])
+            for k, j in enumerate(lanes.values()):
                 scalar_scatter(j, dx[:, k, :], P * b, P)
 
         both = slice(0, V_PASSES)
-        quantise_x(0, "x_woven0", "x_codes0")
-        weigh(1, 0, P)
+        quantise_x(0, nc.vector.tensor_copy, "x_woven0", "x_codes0")
+        make_outer(0, "x_woven0")
+        weights[0] = tile([P, LANES, V_PASSES, P], F32, "weight0")[:]
+        weigh(0, 1)
         score(0, 1, 0)
         squash(0, slice(1, 2))
         score(0, 0, 1)
         squash(0, slice(0, 1))
-        weigh(0, 0, P)
-        quantise_x(1, "x_woven1", "x_codes1")
+        weigh(0, 0)
+        quantise_x(1, nc.scalar.copy, "x_woven1", "x_codes1")
         wv_dealt = tile([P, V_PASSES * D], U16, "wv_dealt")
         deal(nc.scalar.copy, wv_dealt[:], wv_raw[:])
         form_g(0)
+        late_weights = tile([P, LANES, V_PASSES, HALF], F32, "g_woven0")
+        for o in (1, 0):
+            nc.gpsimd.tensor_tensor(late_weights[:, :, o, :], labels[1, o][:], outer[o][:], MULT)
+        for b in (2, 3):
+            weights[b] = late_weights[:, :, :, group_cols(b - 2)]
         for o in (1, 0):
             score(1, o, 2 + o)
-        sums0 = back(0, range(LANES), 6)
-        release_on_scalar(0, sums0, (0, 1), "dx0")
+        sums0 = back(0, (0, 2, 3), 6)
+        release_on_scalar(0, sums0, {0: 0, 1: 2}, "dx0")
         squash(1, both)
         for o in (1, 0):
             score(2, o, 4 + o)
         for o in (1, 0):
             score(3, o, o)
-        release_on_scalar(0, sums0, (2, 3), "margin1")
-        for b in (2, 3):
-            squash(b, both)
+        squash(2, both)
+        release_on_scalar(0, sums0, {2: 3}, "margin2")
+        squash(3, both)
+        weights[1] = tile([P, LANES, V_PASSES, P], F32, "x_woven1")[:]
         for o in (1, 0):
-            weigh(o, P, P)
+            weigh(1, o)
+        dx = tile([P, 1, P], F32, "first_dx")
+        nc.vector.tensor_copy(dx[:], back(0, (1,), 2)[:])
+        vector_scatter(1, dx[:, 0, :], 0, P)
         form_g(1)
-        release_on_scalar(1, back(1, range(LANES), 2), range(LANES), "margin3")
-        for o in (1, 0):
-            weigh(o, HALF, HALF)
+        vector_sums = {1: back(1, (1,), 2)}
+        scalar_sums = {1: back(1, (0, 2, 3), 3)}
+        scalar_dx = tile([P, 3, N - P], F32, "margin3")
+        nc.scalar.copy(scalar_dx[:, :, :P], scalar_sums[1][:])
+        for k, j in ((2, 3), (1, 2), (0, 0)):
+            scalar_scatter(j, scalar_dx[:, k, :P], P, P)
         form_g(2)
-        vector_sums = {2: back(2, (1, 3), 3)}
-        scalar_sums = {2: back(2, (0, 2), 4)}
+        vector_sums[2] = back(2, (1, 3), 4)
+        scalar_sums[2] = back(2, (0, 2), 5)
         form_g(3)
-        vector_sums[3] = back(3, (1,), 5)
-        scalar_sums[3] = back(3, (0, 2, 3), 6)
-        dx = tile([P, 3, P], F32, "vector_dx")
-        nc.vector.tensor_copy(dx[:, :2, :], vector_sums[2][:])
-        for k, j in enumerate((1, 3)):
-            vector_scatter(j, dx[:, k, :], HALF, P)
-        nc.vector.tensor_copy(dx[:, 2:, :], vector_sums[3][:])
-        vector_scatter(1, dx[:, 2, :], HALF + P, P)
-        dx = tile([P, 3, HALF], F32, "scalar_dx")
-        nc.scalar.copy(dx[:, :2, :P], scalar_sums[2][:])
-        scalar_scatter(0, dx[:, 0, :P], HALF, P)
-        nc.scalar.copy(dx[:, :, P:], scalar_sums[3][:])
-        scalar_scatter(0, dx[:, 0, P:], HALF + P, P)
-        scalar_scatter(2, dx[:, 1, :], HALF, HALF)
-        scalar_scatter(3, dx[:, 2, P:], HALF + P, P)
+        vector_sums[3] = back(3, (1,), 6)
+        scalar_sums[3] = back(3, (0, 2, 3), 0)
+        vector_dx = tile([P, 2, N - P], F32, "g_woven3")
+        nc.vector.tensor_copy(vector_dx[:, :1, :P], vector_sums[1][:])
+        nc.vector.tensor_copy(vector_dx[:, :, P:HALF], vector_sums[2][:])
+        vector_scatter(1, vector_dx[:, 0, :HALF], P, HALF)
+        nc.vector.tensor_copy(vector_dx[:, :1, HALF:], vector_sums[3][:])
+        vector_scatter(1, vector_dx[:, 0, HALF:], HALF + P, P)
+        vector_scatter(3, vector_dx[:, 1, P:HALF], HALF, P)
+        nc.scalar.copy(scalar_dx[:, :2, P:HALF], scalar_sums[2][:])
+        nc.scalar.copy(scalar_dx[:, :, HALF:], scalar_sums[3][:])
+        for k, j in enumerate((0, 2)):
+            scalar_scatter(j, scalar_dx[:, k, P:], HALF, HALF)
+        scalar_scatter(3, scalar_dx[:, 2, HALF:], HALF + P, P)
 
         out_rows = out_0.rearrange("(p j) c -> p j c", j=LANES)
 
@@ -354,9 +381,9 @@ def tile_attend_gml_pl_sig_kernel(
                 scales=out_scale[:, cols],
                 in_=woven_out[k][:].rearrange("p c j -> p (c j)"),
             )
-            if k % 2 == 1:
-                two = slice(PIECE * (k - 1), PIECE * (k + 1))
-                nc.sync.dma_start(out=out_words[:, two], in_=out_codes[:, two].bitcast(I32))
+            if k > 0:
+                done = slice(PIECE * k if k > 1 else 0, PIECE * (k + 1))
+                nc.sync.dma_start(out=out_words[:, done], in_=out_codes[:, done].bitcast(I32))
         for q in range(QUADRANTS):
             queue = nc.scalar if q % 2 == 0 else nc.sync
             queue.dma_start(

@@ -71,13 +71,14 @@ def tile_attend_gml_pl_sig_kernel(
         def listed(first, count):
             return offsets[:, first // PER_COLUMN : (first + count) // PER_COLUMN]
 
-        wd_raw = tile([P, V], U16, "wd_raw")
-        nc.sync.dma_start(out=wd_raw[:].bitcast(I32), in_=wd_words[0].bitcast(I32))
         offsets = sb.tile([P, N // PER_COLUMN], U16, name="offsets")
         nc.sync.dma_start(offsets[:], offs)
+        wd_raw = tile([P, V], U16, "wd_raw")
+        nc.sync.dma_start(out=wd_raw[:].bitcast(I32), in_=wd_words[0].bitcast(I32))
         wd_scale_raw = tile([P, V], U8, "wd_scale_raw")
         wv_scale_raw = tile([P, V_PASSES * D], U8, "wv_scale_raw")
-        nc.gpsimd.memset(wd_scale_raw[:].bitcast(U32), 0)
+        for raw in (wd_scale_raw, wv_scale_raw):
+            nc.gpsimd.memset(raw[:].bitcast(U32), 0)
         for q in range(QUADRANTS):
             nc.sync.dma_start(
                 out=wd_scale_raw[32 * q : 32 * q + 4, :].bitcast(I32),
@@ -85,17 +86,12 @@ def tile_attend_gml_pl_sig_kernel(
             )
         x_rows = xT.rearrange("(p t) c -> p t c", t=LANES)
         x_lanes = [tile([P, T], F32, f"x_lane{t}") for t in range(LANES)]
-        rw_cols = tile([P, LANES], F32, "rw_cols")
-        cw_sb = tile([P, V_PASSES, LANES], F32, "cw_sb")
 
         def load_x(t):
             nc.sync.dma_start(out=x_lanes[t][:], in_=x_rows[:, t, :])
 
-        nc.gpsimd.memset(wv_scale_raw[:].bitcast(U32), 0)
         for t in (0, 1):
             load_x(t)
-        nc.sync.dma_start(out=rw_cols[:], in_=rw[0].rearrange("(p k) -> p k", k=LANES))
-        nc.sync.dma_start(out=cw_sb[:], in_=cw.rearrange("(o p r) one -> p o (r one)", p=P, r=LANES))
         for q in range(QUADRANTS):
             nc.sync.dma_start(
                 out=wv_scale_raw[32 * q : 32 * q + 4, :].bitcast(I32).rearrange("f (o w) -> f o w", o=V_PASSES),
@@ -103,6 +99,10 @@ def tile_attend_gml_pl_sig_kernel(
             )
         for t in (2, 3):
             load_x(t)
+        rw_cols = tile([P, LANES], F32, "rw_cols")
+        cw_sb = tile([P, V_PASSES, LANES], F32, "cw_sb")
+        nc.sync.dma_start(out=rw_cols[:], in_=rw[0].rearrange("(p k) -> p k", k=LANES))
+        nc.sync.dma_start(out=cw_sb[:], in_=cw.rearrange("(o p r) one -> p o (r one)", p=P, r=LANES))
         warm = tile([P, 8], F32, "warm")
         nc.vector.memset(warm[:], 0.0)
         nc.scalar.activation(warm[:], warm[:], ACT.Sigmoid)
@@ -112,25 +112,25 @@ def tile_attend_gml_pl_sig_kernel(
         y_rows = y.rearrange("(o p r) i -> o p r i", p=P, r=LANES)
         labels = {}
 
-        def load_labels(h, o):
-            labels[h, o] = tile([P, LANES, HALF], F32, f"y{h}{o}")
-            nc.sync.dma_start(out=labels[h, o][:], in_=y_rows[o, :, :, HALF * h : HALF * (h + 1)])
+        def load_labels(first, count):
+            for o in (1, 0):
+                labels[first, o] = tile([P, LANES, count], F32, f"labels{first}_{o}")
+                nc.sync.dma_start(out=labels[first, o][:], in_=y_rows[o, :, :, first : first + count])
 
-        def group_labels(b, o):
-            return labels[b // 2, o][:, :, group_cols(b % 2)]
+        def span_labels(first, count, o):
+            base = min(first, P)
+            return labels[base, o][:, :, first - base : first - base + count]
 
-        for o in (1, 0):
-            load_labels(0, o)
+        load_labels(0, P)
         wv_raw = tile([P, V_PASSES * D], U16, "wv_raw")
         nc.sync.dma_start(
             out=wv_raw[:].bitcast(I32).rearrange("p (o w) -> p o w", o=V_PASSES),
             in_=wv_words.bitcast(I32).rearrange("o p w -> p o w"),
         )
-        for o in (1, 0):
-            load_labels(1, o)
+        load_labels(P, N - P)
 
         neg_cw = tile([P, V_PASSES * LANES], F32, "neg_cw")
-        nc.scalar.activation(neg_cw[:], cw_sb[:].rearrange("p o r -> p (o r)"), ACT.Copy, scale=-1.0)
+        nc.gpsimd.tensor_scalar_mul(neg_cw[:], cw_sb[:].rearrange("p o r -> p (o r)"), -1.0)
         rw_bank = bank([P, LANES, P], 7)
         for k in range(LANES):
             nc.tensor.transpose(rw_bank[:, k, :], rw_cols[:, k : k + 1].to_broadcast([P, P]), identity[:])
@@ -143,25 +143,10 @@ def tile_attend_gml_pl_sig_kernel(
         wd_scale = tile([P, V], U8, "wd_scale")
         deal(nc.vector.tensor_copy, wd_scale[:], wd_scale_raw[:])
 
-        late_rw = tile([P, HALF], F32, "late_rw")
-        nc.scalar.copy(by_four(late_rw[:]), rw_rows(HALF, HALF))
-        outer = {}
-
-        def make_outer(o, tag):
-            outer[o] = tile([P, LANES, HALF], F32, tag)
-            nc.gpsimd.tensor_tensor(
-                outer[o][:],
-                late_rw[:].unsqueeze(1).to_broadcast([P, LANES, HALF]),
-                neg_cw[:, LANES * o : LANES * (o + 1)].unsqueeze(2).to_broadcast([P, LANES, HALF]),
-                MULT,
-            )
-
-        make_outer(1, "outer1")
-
-        windows = [tile([P, T], F32, f"window{j}") for j in range(LANES)]
-        for j in range(LANES):
-            engine = nc.vector if j < 2 else nc.gpsimd
-            engine.memset(windows[j][:].bitcast(U32), 0)
+        windows = []
+        for engine, tag in ((nc.vector, "window0"), (nc.vector, "window1"), (nc.gpsimd, "wd_raw"), (nc.gpsimd, "wd_scale_raw")):
+            windows.append(tile([P, T], F32, tag))
+            engine.memset(windows[-1][:].bitcast(U32), 0)
 
         def gather(out, t, first, count):
             nc.vector.tensor_copy(out, x_lanes[t][:].indirect(listed(first, count)))
@@ -208,22 +193,29 @@ def tile_attend_gml_pl_sig_kernel(
                     start=True,
                     stop=True,
                 )
-            nc.vector.tensor_tensor(margins[b][:, :, o, :], sums[:], group_labels(b, o), MULT)
+            nc.vector.tensor_tensor(margins[b][:, :, o, :], sums[:], span_labels(P * b, P, o), MULT)
 
         def squash(b, passes):
             nc.scalar.activation(sigmoids[b][:, :, passes, :], margins[b][:, :, passes, :], ACT.Sigmoid, scale=-1.0)
 
-        def weigh(b, o):
-            for r in range(LANES):
-                k = LANES * o + r
-                nc.vector.scalar_tensor_tensor(
-                    by_four(weights[b][:, r, o, :]),
-                    by_four(group_labels(b, o)[:, r, :]),
-                    neg_cw[:, k : k + 1],
-                    rw_rows(P * b, P),
-                    MULT,
-                    MULT,
-                )
+        def weigh(first, count, tag):
+            weight = tile([P, LANES, V_PASSES, count], F32, tag)
+
+            def one_pass(o):
+                for r in range(LANES):
+                    k = LANES * o + r
+                    nc.vector.scalar_tensor_tensor(
+                        by_four(weight[:, r, o, :]),
+                        by_four(span_labels(first, count, o)[:, r, :]),
+                        neg_cw[:, k : k + 1],
+                        rw_rows(first, count),
+                        MULT,
+                        MULT,
+                    )
+
+            for k in range(count // P):
+                weights[first // P + k] = weight[:, :, :, group_cols(k)]
+            return one_pass
 
         g_codes = {}
         g_scales = {}
@@ -275,66 +267,46 @@ def tile_attend_gml_pl_sig_kernel(
 
         both = slice(0, V_PASSES)
         quantise_x(0, nc.vector.tensor_copy, "x_woven0", "x_codes0")
-        make_outer(0, "x_woven0")
-        weights[0] = tile([P, LANES, V_PASSES, P], F32, "weight0")[:]
-        weigh(0, 1)
-        score(0, 1, 0)
-        squash(0, slice(1, 2))
-        score(0, 0, 1)
-        squash(0, slice(0, 1))
-        weigh(0, 0)
+        weigh_first = weigh(0, P, "weight0")
+        for o in (1, 0):
+            weigh_first(o)
+        for o in (1, 0):
+            score(0, o, 1 - o)
+            squash(0, slice(o, o + 1))
         quantise_x(1, nc.scalar.copy, "x_woven1", "x_codes1")
         wv_dealt = tile([P, V_PASSES * D], U16, "wv_dealt")
         deal(nc.scalar.copy, wv_dealt[:], wv_raw[:])
         form_g(0)
-        late_weights = tile([P, LANES, V_PASSES, HALF], F32, "g_woven0")
-        for o in (1, 0):
-            nc.gpsimd.tensor_tensor(late_weights[:, :, o, :], labels[1, o][:], outer[o][:], MULT)
-        for b in (2, 3):
-            weights[b] = late_weights[:, :, :, group_cols(b - 2)]
         for o in (1, 0):
             score(1, o, 2 + o)
-        sums0 = back(0, (0, 2, 3), 6)
-        release_on_scalar(0, sums0, {0: 0, 1: 2}, "dx0")
+        sums0 = back(0, range(LANES), 6)
+        release_on_scalar(0, sums0, {0: 0, 1: 1}, "dx0")
         squash(1, both)
+        release_on_scalar(0, sums0, {2: 2, 3: 3}, "margin1")
         for o in (1, 0):
             score(2, o, 4 + o)
         for o in (1, 0):
             score(3, o, o)
-        squash(2, both)
-        release_on_scalar(0, sums0, {2: 3}, "margin2")
-        squash(3, both)
-        weights[1] = tile([P, LANES, V_PASSES, P], F32, "x_woven1")[:]
+        for b in (2, 3):
+            squash(b, both)
+        weigh_second = weigh(P, P, "x_woven1")
         for o in (1, 0):
-            weigh(1, o)
-        dx = tile([P, 1, P], F32, "first_dx")
-        nc.vector.tensor_copy(dx[:], back(0, (1,), 2)[:])
-        vector_scatter(1, dx[:, 0, :], 0, P)
+            weigh_second(o)
         form_g(1)
-        vector_sums = {1: back(1, (1,), 2)}
-        scalar_sums = {1: back(1, (0, 2, 3), 3)}
-        scalar_dx = tile([P, 3, N - P], F32, "margin3")
-        nc.scalar.copy(scalar_dx[:, :, :P], scalar_sums[1][:])
-        for k, j in ((2, 3), (1, 2), (0, 0)):
-            scalar_scatter(j, scalar_dx[:, k, :P], P, P)
+        weigh_late = weigh(HALF, HALF, "g_woven0")
+        release_on_scalar(1, back(1, range(LANES), 2), {j: j for j in range(LANES)}, "margin3")
+        for o in (1, 0):
+            weigh_late(o)
         form_g(2)
-        vector_sums[2] = back(2, (1, 3), 4)
-        scalar_sums[2] = back(2, (0, 2), 5)
+        late = {(2, odd): back(2, (odd, odd + 2), 3 + odd) for odd in (1, 0)}
         form_g(3)
-        vector_sums[3] = back(3, (1,), 6)
-        scalar_sums[3] = back(3, (0, 2, 3), 0)
-        vector_dx = tile([P, 2, N - P], F32, "g_woven3")
-        nc.vector.tensor_copy(vector_dx[:, :1, :P], vector_sums[1][:])
-        nc.vector.tensor_copy(vector_dx[:, :, P:HALF], vector_sums[2][:])
-        vector_scatter(1, vector_dx[:, 0, :HALF], P, HALF)
-        nc.vector.tensor_copy(vector_dx[:, :1, HALF:], vector_sums[3][:])
-        vector_scatter(1, vector_dx[:, 0, HALF:], HALF + P, P)
-        vector_scatter(3, vector_dx[:, 1, P:HALF], HALF, P)
-        nc.scalar.copy(scalar_dx[:, :2, P:HALF], scalar_sums[2][:])
-        nc.scalar.copy(scalar_dx[:, :, HALF:], scalar_sums[3][:])
-        for k, j in enumerate((0, 2)):
-            scalar_scatter(j, scalar_dx[:, k, P:], HALF, HALF)
-        scalar_scatter(3, scalar_dx[:, 2, HALF:], HALF + P, P)
+        late.update({(3, odd): back(3, (odd, odd + 2), 5 + odd) for odd in (1, 0)})
+        for odd, engine_copy, scatter in ((1, nc.vector.tensor_copy, vector_scatter), (0, nc.scalar.copy, scalar_scatter)):
+            dx = tile([P, 2, HALF], F32, f"late_dx{odd}")
+            for b in (2, 3):
+                engine_copy(dx[:, :, group_cols(b - 2)], late[b, odd][:])
+                scatter(odd, dx[:, 0, group_cols(b - 2)], P * b, P)
+            scatter(odd + 2, dx[:, 1, :], HALF, HALF)
 
         out_rows = out_0.rearrange("(p j) c -> p j c", j=LANES)
 
@@ -343,7 +315,7 @@ def tile_attend_gml_pl_sig_kernel(
 
         pairs_tile = sb.tile([P, LANES * T], BF16, name="pairs")
         pairs = pairs_tile[:].rearrange("p (k h c e) -> p k h c e", h=2, c=PIECE, e=2)
-        for j in (1, 0, 2, 3):
+        for j in (1, 0, 3, 2):
             store_window(j)
 
         def round_lane(engine_copy, j, pieces):
@@ -364,10 +336,10 @@ def tile_attend_gml_pl_sig_kernel(
 
         for j in (1, 0):
             round_lane(nc.vector.tensor_copy, j, slice(0, PIECES))
-        for j in (2, 3):
+        for j in (3, 2):
             for k in range(PIECES - 1):
                 round_lane(nc.vector.tensor_copy, j, slice(k, k + 1))
-        for j in (2, 3):
+        for j in (3, 2):
             round_lane(nc.scalar.copy, j, slice(PIECES - 1, PIECES))
         for k in (0, 1):
             join_pairs(nc.vector.tensor_copy, I32, k)

@@ -157,7 +157,7 @@ def tile_attend_gml_pl_sig_kernel(
         wv_scale = tile([P, V_PASSES * D], U8, "wv_scale")
         deal(nc.vector.tensor_copy, wv_scale[:], wv_scale_raw[:])
         gather(picked[:, 2, :], 2, 0, N)
-        spans = ((0, P), (P, N - P))
+        spans = ((0, P), (P, P), (HALF, HALF))
         gather(picked[:, LANES - 1, :P], LANES - 1, 0, P)
         nc.scalar.activation(picked[:, LANES - 1, P:], x_lanes[LANES - 1][:].indirect(listed(P, N - P)), ACT.Copy)
 
@@ -179,6 +179,7 @@ def tile_attend_gml_pl_sig_kernel(
         margins = [tile([P, LANES, V_PASSES, P], F32, f"margin{b}") for b in range(GROUPS)]
         sigmoids = [tile([P, LANES, V_PASSES, P], F32, f"sigmoid{b}") for b in range(GROUPS)]
         weights = {}
+        late_weight = {}
 
         def score(b, o, number):
             sums = bank([P, LANES, P], number)
@@ -200,6 +201,7 @@ def tile_attend_gml_pl_sig_kernel(
 
         def weigh(first, count, tag):
             weight = tile([P, LANES, V_PASSES, count], F32, tag)
+            late_weight[0] = weight
 
             def one_pass(o):
                 for r in range(LANES):
@@ -220,36 +222,37 @@ def tile_attend_gml_pl_sig_kernel(
         g_codes = {}
         g_scales = {}
 
-        def form_g(b):
+        def form_g(b, steps):
             woven = tile([P, V_PASSES, P, LANES], BF16, f"g_woven{b}")
-            for o in (1, 0):
-                nc.vector.tensor_tensor(
-                    walk_woven(woven[:, o]),
-                    walk_lanes(sigmoids[b][:, :, o, :]),
-                    walk_lanes(weights[b][:, :, o, :]),
-                    MULT,
+            g_codes[b] = tile([P, V_PASSES, P], U32, f"g_codes{b}")
+            g_scales[b] = tile([P, V_PASSES, P], U8, f"g_scale{b}")
+            for passes in steps:
+                for o in range(passes.start, passes.stop):
+                    nc.vector.tensor_tensor(
+                        walk_woven(woven[:, o]),
+                        walk_lanes(sigmoids[b][:, :, o, :]),
+                        walk_lanes(weights[b][:, :, o, :]),
+                        MULT,
+                    )
+                nc.vector.quantize_mx(
+                    out=g_codes[b][:, passes].rearrange("p o i -> p (o i)").bitcast(E5M2),
+                    scales=g_scales[b][:, passes].rearrange("p o i -> p (o i)"),
+                    in_=woven[:, passes].rearrange("p o i r -> p (o i r)"),
                 )
-            g_codes[b] = tile([P, V_PASSES * P], U32, f"g_codes{b}")
-            g_scales[b] = tile([P, V_PASSES * P], U8, f"g_scale{b}")
-            nc.vector.quantize_mx(
-                out=g_codes[b][:].bitcast(E5M2),
-                scales=g_scales[b][:],
-                in_=woven[:].rearrange("p o i r -> p (o i r)"),
-            )
 
         def back(b, lanes, number):
             sums = bank([P, len(lanes), P], number)
-            for k, j in enumerate(lanes):
-                for o in range(V_PASSES):
+            for o in (1, 0):
+                for k, j in enumerate(lanes):
                     dealt = slice(D * o + P * j, D * o + P * (j + 1))
                     nc.tensor.matmul_mx(
                         out=sums[:, k, :],
                         lhsT=wv_dealt[:, dealt].bitcast(E2M1),
                         lhsT_scale=wv_scale[:, dealt],
-                        rhs=g_codes[b][:, group_cols(o)].bitcast(E5M2),
-                        rhs_scale=g_scales[b][:, group_cols(o)],
-                        start=(o == 0),
-                        stop=(o == V_PASSES - 1),
+                        rhs=g_codes[b][:, o, :].bitcast(E5M2),
+                        rhs_scale=g_scales[b][:, o, :],
+                        start=(o == 1 and k == 0),
+                        stop=(o == 0 and k == len(lanes) - 1),
                     )
             return sums
 
@@ -276,7 +279,14 @@ def tile_attend_gml_pl_sig_kernel(
         quantise_x(1, nc.scalar.copy, "x_woven1", "x_codes1")
         wv_dealt = tile([P, V_PASSES * D], U16, "wv_dealt")
         deal(nc.scalar.copy, wv_dealt[:], wv_raw[:])
-        form_g(0)
+        outer = tile([P, LANES, HALF], F32, "margin0")
+        for r in range(LANES):
+            k = LANES + r
+            nc.scalar.activation(by_four(outer[:, r, :]), rw_rows(HALF, HALF), ACT.Copy, scale=neg_cw[:, k : k + 1])
+        form_g(0, (slice(1, 2), slice(0, 1)))
+        quantise_x(2, nc.scalar.copy, "x_woven2", "g_woven0")
+        weigh_late = weigh(HALF, HALF, "x_woven2")
+        nc.gpsimd.tensor_tensor(late_weight[0][:, :, 1, :], span_labels(HALF, HALF, 1), outer[:], MULT)
         for o in (1, 0):
             score(1, o, 2 + o)
         sums0 = back(0, range(LANES), 6)
@@ -289,17 +299,15 @@ def tile_attend_gml_pl_sig_kernel(
             score(3, o, o)
         for b in (2, 3):
             squash(b, both)
-        weigh_second = weigh(P, P, "x_woven1")
+        weigh_second = weigh(P, P, "weight0")
         for o in (1, 0):
             weigh_second(o)
-        form_g(1)
-        weigh_late = weigh(HALF, HALF, "g_woven0")
+        form_g(1, (both,))
         release_on_scalar(1, back(1, range(LANES), 2), {j: j for j in range(LANES)}, "margin3")
-        for o in (1, 0):
-            weigh_late(o)
-        form_g(2)
+        weigh_late(0)
+        form_g(2, (both,))
         late = {(2, odd): back(2, (odd, odd + 2), 3 + odd) for odd in (1, 0)}
-        form_g(3)
+        form_g(3, (both,))
         late.update({(3, odd): back(3, (odd, odd + 2), 5 + odd) for odd in (1, 0)})
         for odd, engine_copy, scatter in ((1, nc.vector.tensor_copy, vector_scatter), (0, nc.scalar.copy, scalar_scatter)):
             dx = tile([P, 2, HALF], F32, f"late_dx{odd}")

@@ -16,6 +16,7 @@ E4M3 = mybir.dt.float8_e4m3fn_x4
 E5M2 = mybir.dt.float8_e5m2_x4
 E2M1 = mybir.dt.float4_e2m1fn_x4
 MULT = mybir.AluOpType.mult
+ADD = mybir.AluOpType.add
 ACT = mybir.ActivationFunctionType
 
 P = 128
@@ -27,6 +28,7 @@ QUADRANTS = 4
 PER_COLUMN = 16
 RUN = 4
 HALF = N // 2
+SPLIT = 192
 PIECE = 256
 PIECES = T // PIECE
 
@@ -292,7 +294,10 @@ def tile_attend_gml_pl_sig_kernel(
         sums0 = back(0, range(LANES), 6)
         release_on_scalar(0, sums0, {0: 0, 1: 1}, "dx0")
         squash(1, both)
-        release_on_scalar(0, sums0, {2: 2, 3: 3}, "margin1")
+        release_on_scalar(0, sums0, {2: 2}, "margin1")
+        odd_dx = tile([P, 2, N], F32, "odd_dx")
+        last_dx = odd_dx[:, 1, :]
+        nc.scalar.copy(last_dx[:, group_cols(0)], sums0[:, 3, :])
         for o in (1, 0):
             score(2, o, 4 + o)
         for o in (1, 0):
@@ -303,18 +308,28 @@ def tile_attend_gml_pl_sig_kernel(
         for o in (1, 0):
             weigh_second(o)
         form_g(1, (both,))
-        release_on_scalar(1, back(1, range(LANES), 2), {j: j for j in range(LANES)}, "margin3")
+        sums1 = back(1, range(LANES), 2)
+        release_on_scalar(1, sums1, {1: 1}, "margin3")
+        nc.scalar.copy(last_dx[:, group_cols(1)], sums1[:, 3, :])
+        scalar_scatter(3, last_dx[:, :SPLIT], 0, SPLIT)
+        even_dx = tile([P, 2, P], F32, "margin2")
+        nc.scalar.copy(even_dx[:], sums1[:, 0:3:2, :])
+        for k in range(2):
+            scalar_scatter(2 * k, even_dx[:, k, :], P, P)
         weigh_late(0)
         form_g(2, (both,))
         late = {(2, odd): back(2, (odd, odd + 2), 3 + odd) for odd in (1, 0)}
         form_g(3, (both,))
         late.update({(3, odd): back(3, (odd, odd + 2), 5 + odd) for odd in (1, 0)})
-        for odd, engine_copy, scatter in ((1, nc.vector.tensor_copy, vector_scatter), (0, nc.scalar.copy, scalar_scatter)):
-            dx = tile([P, 2, HALF], F32, f"late_dx{odd}")
-            for b in (2, 3):
-                engine_copy(dx[:, :, group_cols(b - 2)], late[b, odd][:])
-                scatter(odd, dx[:, 0, group_cols(b - 2)], P * b, P)
-            scatter(odd + 2, dx[:, 1, :], HALF, HALF)
+        for b in (2, 3):
+            nc.vector.tensor_copy(odd_dx[:, :, group_cols(b)], late[b, 1][:])
+            vector_scatter(1, odd_dx[:, 0, group_cols(b)], P * b, P)
+        vector_scatter(3, last_dx[:, SPLIT:], SPLIT, N - SPLIT)
+        dx = tile([P, 2, HALF], F32, "late_dx0")
+        for b in (2, 3):
+            nc.scalar.copy(dx[:, :, group_cols(b - 2)], late[b, 0][:])
+            scalar_scatter(0, dx[:, 0, group_cols(b - 2)], P * b, P)
+        scalar_scatter(2, dx[:, 1, :], HALF, HALF)
 
         out_rows = out_0.rearrange("(p j) c -> p j c", j=LANES)
 
@@ -331,6 +346,9 @@ def tile_attend_gml_pl_sig_kernel(
                 pairs[:, pieces, j // 2, :, j % 2], windows[j][:].rearrange("p (k c) -> p k c", c=PIECE)[:, pieces, :]
             )
 
+        def round_on_gpsimd(out, in_):
+            nc.gpsimd.tensor_scalar(out, in_, 1.0, -0.0, MULT, ADD)
+
         out_scale = sb.tile([P, T], U8, name="out_scale", align_bytes=64)
         out_words = out_1[0].rearrange("p c t -> p (c t)").bitcast(I32)
         woven_out = {}
@@ -343,7 +361,9 @@ def tile_attend_gml_pl_sig_kernel(
             )
 
         for j in (1, 0):
-            round_lane(nc.vector.tensor_copy, j, slice(0, PIECES))
+            round_lane(round_on_gpsimd, j, slice(0, 1))
+            for pieces in (slice(1, 2), slice(2, PIECES)):
+                round_lane(nc.vector.tensor_copy, j, pieces)
         for j in (3, 2):
             for k in range(PIECES - 1):
                 round_lane(nc.vector.tensor_copy, j, slice(k, k + 1))

@@ -16,7 +16,6 @@ E4M3 = mybir.dt.float8_e4m3fn_x4
 E5M2 = mybir.dt.float8_e5m2_x4
 E2M1 = mybir.dt.float4_e2m1fn_x4
 MULT = mybir.AluOpType.mult
-ADD = mybir.AluOpType.add
 ACT = mybir.ActivationFunctionType
 
 P = 128
@@ -346,9 +345,6 @@ def tile_attend_gml_pl_sig_kernel(
                 pairs[:, pieces, j // 2, :, j % 2], windows[j][:].rearrange("p (k c) -> p k c", c=PIECE)[:, pieces, :]
             )
 
-        def round_on_gpsimd(out, in_):
-            nc.gpsimd.tensor_scalar(out, in_, 1.0, -0.0, MULT, ADD)
-
         out_scale = sb.tile([P, T], U8, name="out_scale", align_bytes=64)
         out_words = out_1[0].rearrange("p c t -> p (c t)").bitcast(I32)
         woven_out = {}
@@ -361,9 +357,7 @@ def tile_attend_gml_pl_sig_kernel(
             )
 
         for j in (1, 0):
-            round_lane(round_on_gpsimd, j, slice(0, 1))
-            for pieces in (slice(1, 2), slice(2, PIECES)):
-                round_lane(nc.vector.tensor_copy, j, pieces)
+            round_lane(nc.vector.tensor_copy, j, slice(0, PIECES))
         for j in (3, 2):
             for k in range(PIECES - 1):
                 round_lane(nc.vector.tensor_copy, j, slice(k, k + 1))

@@ -32,6 +32,9 @@ PIECE = 256
 PIECES = T // PIECE
 
 
+PLACES = {"outer": 0, "margin0": 2048, "x_woven2": 4096, "late_weight": 4096}
+
+
 def deal(engine_copy, out, in_):
     engine_copy(
         out.rearrange("p (g r m) -> p g r m", r=LANES, m=P),
@@ -61,9 +64,12 @@ def tile_attend_gml_pl_sig_kernel(
     nc = tc.nc
     with ExitStack() as ctx:
         sb = ctx.enter_context(tc.tile_pool(name="sb", bufs=1))
+        laid = ctx.enter_context(tc.tile_pool(name="laid", bufs=1))
         psum = ctx.enter_context(tc.psum_pool(name="psum", bufs=1))
 
         def tile(shape, dtype, tag):
+            if tag in PLACES:
+                return laid.tile(shape, dtype, name="laid", tag=tag, align_bytes=64, offset=PLACES[tag])
             return sb.tile(shape, dtype, name="shared", tag=tag, align_bytes=64)
 
         def bank(shape, number):
@@ -98,11 +104,11 @@ def tile_attend_gml_pl_sig_kernel(
                 out=wv_scale_raw[32 * q : 32 * q + 4, :].bitcast(I32).rearrange("f (o w) -> f o w", o=V_PASSES),
                 in_=wv_scales[:, 4 * q : 4 * q + 4, :].bitcast(I32).rearrange("o f w -> f o w"),
             )
-        for t in (2, 3):
-            load_x(t)
+        load_x(2)
         rw_cols = tile([P, LANES], F32, "rw_cols")
-        cw_sb = tile([P, V_PASSES, LANES], F32, "cw_sb")
         nc.sync.dma_start(out=rw_cols[:], in_=rw[0].rearrange("(p k) -> p k", k=LANES))
+        load_x(3)
+        cw_sb = tile([P, V_PASSES, LANES], F32, "cw_sb")
         nc.sync.dma_start(out=cw_sb[:], in_=cw.rearrange("(o p r) one -> p o (r one)", p=P, r=LANES))
         warm = tile([P, 8], F32, "warm")
         nc.vector.memset(warm[:], 0.0)
@@ -157,19 +163,27 @@ def tile_attend_gml_pl_sig_kernel(
         nc.scalar.activation(picked[:, 1, :], x_lanes[1][:].indirect(offsets[:]), ACT.Copy)
         wv_scale = tile([P, V_PASSES * D], U8, "wv_scale")
         deal(nc.vector.tensor_copy, wv_scale[:], wv_scale_raw[:])
-        gather(picked[:, 2, :], 2, 0, N)
+        early_woven = [tile([P, P, LANES], BF16, f"x_woven{b}") for b in range(2)]
+        for b in range(2):
+            nc.scalar.copy(early_woven[b][:, :, :2], picked[:, :2, group_cols(b)].rearrange("p t i -> p i t"))
+            gather(early_woven[b][:, :, 2], 2, P * b, P)
+        gather(picked[:, 2, HALF:], 2, HALF, HALF)
+        gather(early_woven[0][:, :, 3], 3, 0, P)
         spans = ((0, P), (P, P), (HALF, HALF))
-        gather(picked[:, LANES - 1, :P], LANES - 1, 0, P)
-        nc.scalar.activation(picked[:, LANES - 1, P:], x_lanes[LANES - 1][:].indirect(listed(P, N - P)), ACT.Copy)
+        nc.scalar.activation(picked[:, 3, HALF:], x_lanes[3][:].indirect(listed(HALF, HALF)), ACT.Copy)
 
         x_codes = {}
         x_scale = tile([P, N], U8, "x_scale")
 
-        def quantise_x(span, engine_copy, woven_tag, codes_tag):
+        def weave(span):
+            first, count = spans[span]
+            woven = tile([P, count, LANES], BF16, f"x_woven{span}")
+            nc.scalar.copy(walk_woven(woven[:]), walk_lanes(picked[:, :, first : first + count]))
+            return woven
+
+        def quantise_x(span, woven, codes_tag):
             first, count = spans[span]
             cols = slice(first, first + count)
-            woven = tile([P, count, LANES], BF16, woven_tag)
-            engine_copy(walk_woven(woven[:]), walk_lanes(picked[:, :, cols]))
             codes = tile([P, count], U32, codes_tag)
             nc.vector.quantize_mx(
                 out=codes[:].bitcast(E4M3), scales=x_scale[:, cols], in_=woven[:].rearrange("p i t -> p (i t)")
@@ -270,23 +284,25 @@ def tile_attend_gml_pl_sig_kernel(
                 scalar_scatter(j, dx[:, k, :], P * b, P)
 
         both = slice(0, V_PASSES)
-        quantise_x(0, nc.vector.tensor_copy, "x_woven0", "x_codes0")
+        quantise_x(0, early_woven[0], "x_codes0")
+        gather(early_woven[1][:, :, 3], 3, P, P)
         weigh_first = weigh(0, P, "weight0")
         for o in (1, 0):
             weigh_first(o)
         for o in (1, 0):
             score(0, o, 1 - o)
             squash(0, slice(o, o + 1))
-        quantise_x(1, nc.scalar.copy, "x_woven1", "x_codes1")
+        quantise_x(1, early_woven[1], "x_codes1")
         wv_dealt = tile([P, V_PASSES * D], U16, "wv_dealt")
         deal(nc.scalar.copy, wv_dealt[:], wv_raw[:])
-        outer = tile([P, LANES, HALF], F32, "margin0")
+        late_woven = weave(2)
+        outer = tile([P, LANES, HALF], F32, "outer")
         for r in range(LANES):
             k = LANES + r
             nc.scalar.activation(by_four(outer[:, r, :]), rw_rows(HALF, HALF), ACT.Copy, scale=neg_cw[:, k : k + 1])
         form_g(0, (slice(1, 2), slice(0, 1)))
-        quantise_x(2, nc.scalar.copy, "x_woven2", "g_woven0")
-        weigh_late = weigh(HALF, HALF, "x_woven2")
+        quantise_x(2, late_woven, "g_woven0")
+        weigh_late = weigh(HALF, HALF, "late_weight")
         nc.gpsimd.tensor_tensor(late_weight[0][:, :, 1, :], span_labels(HALF, HALF, 1), outer[:], MULT)
         for o in (1, 0):
             score(1, o, 2 + o)

from contextlib import ExitStack

import concourse.mybir as mybir
from concourse.masks import make_identity

N, T, D, V = 512, 1024, 512, 1024
FLOPS = 2 * D * V * N * 2

F32 = mybir.dt.float32
BF16 = mybir.dt.bfloat16
I32 = mybir.dt.int32
U32 = mybir.dt.uint32
U16 = mybir.dt.uint16
U8 = mybir.dt.uint8
E4M3 = mybir.dt.float8_e4m3fn_x4
E5M2 = mybir.dt.float8_e5m2_x4
E2M1 = mybir.dt.float4_e2m1fn_x4
MULT = mybir.AluOpType.mult
ACT = mybir.ActivationFunctionType

P = 128
LANES = 4
K_PASS = P * LANES
V_PASSES = V // K_PASS
GROUPS = N // P
QUADRANTS = 4
PER_COLUMN = 16
RUN = 4
HALF = N // 2
SPLIT = 192
PIECE = 256
PIECES = T // PIECE


PLACES = {"outer": 0, "margin0": 2048, "x_woven2": 4096, "late_weight": 4096}


def deal(engine_copy, out, in_):
    engine_copy(
        out.rearrange("p (g r m) -> p g r m", r=LANES, m=P),
        in_.rearrange("p (g m r) -> p g r m", r=LANES, m=P),
    )


def walk_woven(woven):
    return woven.rearrange("p (c i) r -> p c r i", i=RUN)


def walk_lanes(lanes):
    return lanes.rearrange("p r (c i) -> p c r i", i=RUN)


def by_four(run):
    return run.rearrange("p (n k) -> p n k", k=LANES)


def group_cols(b):
    return slice(P * b, P * (b + 1))


def tile_attend_gml_pl_sig_kernel(
    tc, xT, wd_words, wd_scales, wv_words, wv_scales, y, cw, rw, offs, out_0, out_1, out_2
):
    nc = tc.nc
    with ExitStack() as ctx:
        sb = ctx.enter_context(tc.tile_pool(name="sb", bufs=1))
        laid = ctx.enter_context(tc.tile_pool(name="laid", bufs=1))
        psum = ctx.enter_context(tc.psum_pool(name="psum", bufs=1))

        def tile(shape, dtype, tag):
            if tag in PLACES:
                return laid.tile(shape, dtype, name="laid", tag=tag, align_bytes=64, offset=PLACES[tag])
            return sb.tile(shape, dtype, name="shared", tag=tag, align_bytes=64)

        def bank(shape, number):
            return psum.tile(shape, F32, name="bank", tag=f"bank{number}")

        def listed(first, count):
            return offsets[:, first // PER_COLUMN : (first + count) // PER_COLUMN]

        offsets = sb.tile([P, N // PER_COLUMN], U16, name="offsets")
        nc.sync.dma_start(offsets[:], offs)
        wd_raw = tile([P, V], U16, "wd_raw")
        nc.sync.dma_start(out=wd_raw[:].bitcast(I32), in_=wd_words[0].bitcast(I32))
        wd_scale_raw = tile([P, V], U8, "wd_scale_raw")
        wv_scale_raw = tile([P, V_PASSES * D], U8, "wv_scale_raw")
        for raw in (wd_scale_raw, wv_scale_raw):
            nc.gpsimd.memset(raw[:].bitcast(U32), 0)
        for q in range(QUADRANTS):
            nc.sync.dma_start(
                out=wd_scale_raw[32 * q : 32 * q + 4, :].bitcast(I32),
                in_=wd_scales[0, 4 * q : 4 * q + 4, :].bitcast(I32),
            )
        x_rows = xT.rearrange("(p t) c -> p t c", t=LANES)
        x_lanes = [tile([P, T], F32, f"x_lane{t}") for t in range(LANES)]

        def load_x(t):
            nc.sync.dma_start(out=x_lanes[t][:], in_=x_rows[:, t, :])

        for t in (0, 1):
            load_x(t)
        for q in range(QUADRANTS):
            nc.sync.dma_start(
                out=wv_scale_raw[32 * q : 32 * q + 4, :].bitcast(I32).rearrange("f (o w) -> f o w", o=V_PASSES),
                in_=wv_scales[:, 4 * q : 4 * q + 4, :].bitcast(I32).rearrange("o f w -> f o w"),
            )
        load_x(2)
        rw_cols = tile([P, LANES], F32, "rw_cols")
        nc.sync.dma_start(out=rw_cols[:], in_=rw[0].rearrange("(p k) -> p k", k=LANES))
        load_x(3)
        cw_sb = tile([P, V_PASSES, LANES], F32, "cw_sb")
        nc.sync.dma_start(out=cw_sb[:], in_=cw.rearrange("(o p r) one -> p o (r one)", p=P, r=LANES))
        warm = tile([P, 8], F32, "warm")
        nc.vector.memset(warm[:], 0.0)
        nc.scalar.activation(warm[:], warm[:], ACT.Sigmoid)
        identity = tile([P, P], F32, "identity")
        make_identity(nc, identity[:])

        y_rows = y.rearrange("(o p r) i -> o p r i", p=P, r=LANES)
        labels = {}

        def load_labels(first, count):
            for o in (1, 0):
                labels[first, o] = tile([P, LANES, count], F32, f"labels{first}_{o}")
                nc.sync.dma_start(out=labels[first, o][:], in_=y_rows[o, :, :, first : first + count])

        def span_labels(first, count, o):
            base = min(first, P)
            return labels[base, o][:, :, first - base : first - base + count]

        load_labels(0, P)
        wv_raw = tile([P, V_PASSES * D], U16, "wv_raw")
        nc.sync.dma_start(
            out=wv_raw[:].bitcast(I32).rearrange("p (o w) -> p o w", o=V_PASSES),
            in_=wv_words.bitcast(I32).rearrange("o p w -> p o w"),
        )
        load_labels(P, N - P)

        neg_cw = tile([P, V_PASSES * LANES], F32, "neg_cw")
        nc.gpsimd.tensor_scalar_mul(neg_cw[:], cw_sb[:].rearrange("p o r -> p (o r)"), -1.0)
        rw_bank = bank([P, LANES, P], 7)
        for k in range(LANES):
            nc.tensor.transpose(rw_bank[:, k, :], rw_cols[:, k : k + 1].to_broadcast([P, P]), identity[:])

        def rw_rows(first, count):
            return rw_bank[:].rearrange("p k n -> p n k")[:, first // LANES : (first + count) // LANES, :]

        wd_dealt = tile([P, V], U16, "wd_dealt")
        deal(nc.scalar.copy, wd_dealt[:], wd_raw[:])
        wd_scale = tile([P, V], U8, "wd_scale")
        deal(nc.vector.tensor_copy, wd_scale[:], wd_scale_raw[:])

        windows = []
        for engine, tag in ((nc.vector, "window0"), (nc.vector, "window1"), (nc.gpsimd, "wd_raw"), (nc.gpsimd, "wd_scale_raw")):
            windows.append(tile([P, T], F32, tag))
            engine.memset(windows[-1][:].bitcast(U32), 0)

        def gather(out, t, first, count):
            nc.vector.tensor_copy(out, x_lanes[t][:].indirect(listed(first, count)))

        picked = tile([P, LANES, N], BF16, "picked")
        gather(picked[:, 0, :], 0, 0, N)
        nc.scalar.activation(picked[:, 1, :], x_lanes[1][:].indirect(offsets[:]), ACT.Copy)
        wv_scale = tile([P, V_PASSES * D], U8, "wv_scale")
        deal(nc.vector.tensor_copy, wv_scale[:], wv_scale_raw[:])
        early_woven = [tile([P, P, LANES], BF16, f"x_woven{b}") for b in range(2)]
        for b in range(2):
            nc.scalar.copy(early_woven[b][:, :, :2], picked[:, :2, group_cols(b)].rearrange("p t i -> p i t"))
            gather(early_woven[b][:, :, 2], 2, P * b, P)
        gather(picked[:, 2, HALF:], 2, HALF, HALF)
        gather(early_woven[0][:, :, 3], 3, 0, P)
        spans = ((0, P), (P, P), (HALF, HALF))
        nc.scalar.activation(picked[:, 3, HALF:], x_lanes[3][:].indirect(listed(HALF, HALF)), ACT.Copy)

        x_codes = {}
        x_scale = tile([P, N], U8, "x_scale")

        def weave(span):
            first, count = spans[span]
            woven = tile([P, count, LANES], BF16, f"x_woven{span}")
            nc.scalar.copy(walk_woven(woven[:]), walk_lanes(picked[:, :, first : first + count]))
            return woven

        def quantise_x(span, woven, codes_tag):
            first, count = spans[span]
            cols = slice(first, first + count)
            codes = tile([P, count], U32, codes_tag)
            nc.vector.quantize_mx(
                out=codes[:].bitcast(E4M3), scales=x_scale[:, cols], in_=woven[:].rearrange("p i t -> p (i t)")
            )
            for b in range(first // P, (first + count) // P):
                x_codes[b] = codes[:, P * b - first : P * (b + 1) - first]

        margins = [tile([P, LANES, V_PASSES, P], F32, f"margin{b}") for b in range(GROUPS)]
        sigmoids = [tile([P, LANES, V_PASSES, P], F32, f"sigmoid{b}") for b in range(GROUPS)]
        weights = {}
        late_weight = {}

        def score(b, o, number):
            sums = bank([P, LANES, P], number)
            for r in range(LANES):
                cols = slice(K_PASS * o + P * r, K_PASS * o + P * (r + 1))
                nc.tensor.matmul_mx(
                    out=sums[:, r, :],
                    lhsT=wd_dealt[:, cols].bitcast(E2M1),
                    lhsT_scale=wd_scale[:, cols],
                    rhs=x_codes[b].bitcast(E4M3),
                    rhs_scale=x_scale[:, group_cols(b)],
                    start=True,
                    stop=True,
                )
            nc.vector.tensor_tensor(margins[b][:, :, o, :], sums[:], span_labels(P * b, P, o), MULT)

        def squash(b, passes):
            nc.scalar.activation(sigmoids[b][:, :, passes, :], margins[b][:, :, passes, :], ACT.Sigmoid, scale=-1.0)

        def weigh(first, count, tag):
            weight = tile([P, LANES, V_PASSES, count], F32, tag)
            late_weight[0] = weight

            def one_pass(o):
                for r in range(LANES):
                    k = LANES * o + r
                    nc.vector.scalar_tensor_tensor(
                        by_four(weight[:, r, o, :]),
                        by_four(span_labels(first, count, o)[:, r, :]),
                        neg_cw[:, k : k + 1],
                        rw_rows(first, count),
                        MULT,
                        MULT,
                    )

            for k in range(count // P):
                weights[first // P + k] = weight[:, :, :, group_cols(k)]
            return one_pass

        g_codes = {}
        g_scales = {}

        def form_g(b, steps):
            woven = tile([P, V_PASSES, P, LANES], BF16, f"g_woven{b}")
            g_codes[b] = tile([P, V_PASSES, P], U32, f"g_codes{b}")
            g_scales[b] = tile([P, V_PASSES, P], U8, f"g_scale{b}")
            for passes in steps:
                for o in range(passes.start, passes.stop):
                    nc.vector.tensor_tensor(
                        walk_woven(woven[:, o]),
                        walk_lanes(sigmoids[b][:, :, o, :]),
                        walk_lanes(weights[b][:, :, o, :]),
                        MULT,
                    )
                nc.vector.quantize_mx(
                    out=g_codes[b][:, passes].rearrange("p o i -> p (o i)").bitcast(E5M2),
                    scales=g_scales[b][:, passes].rearrange("p o i -> p (o i)"),
                    in_=woven[:, passes].rearrange("p o i r -> p (o i r)"),
                )

        def back(b, lanes, number):
            sums = bank([P, len(lanes), P], number)
            for o in (1, 0):
                for k, j in enumerate(lanes):
                    dealt = slice(D * o + P * j, D * o + P * (j + 1))
                    nc.tensor.matmul_mx(
                        out=sums[:, k, :],
                        lhsT=wv_dealt[:, dealt].bitcast(E2M1),
                        lhsT_scale=wv_scale[:, dealt],
                        rhs=g_codes[b][:, o, :].bitcast(E5M2),
                        rhs_scale=g_scales[b][:, o, :],
                        start=(o == 1 and k == 0),
                        stop=(o == 0 and k == len(lanes) - 1),
                    )
            return sums

        def scalar_scatter(j, dx, first, count):
            nc.scalar.activation(windows[j][:].indirect(listed(first, count)), dx, ACT.Copy)

        def vector_scatter(j, dx, first, count):
            nc.vector.tensor_copy(windows[j][:].indirect(listed(first, count)), dx)

        def release_on_scalar(b, sums, lanes, tag):
            dx = tile([P, len(lanes), P], F32, tag)
            nc.scalar.copy(dx[:], sums[:, min(lanes) : max(lanes) + 1, :])
            for k, j in enumerate(lanes.values()):
                scalar_scatter(j, dx[:, k, :], P * b, P)

        both = slice(0, V_PASSES)
        quantise_x(0, early_woven[0], "x_codes0")
        gather(early_woven[1][:, :, 3], 3, P, P)
        weigh_first = weigh(0, P, "weight0")
        for o in (1, 0):
            weigh_first(o)
        for o in (1, 0):
            score(0, o, 1 - o)
            squash(0, slice(o, o + 1))
        quantise_x(1, early_woven[1], "x_codes1")
        wv_dealt = tile([P, V_PASSES * D], U16, "wv_dealt")
        deal(nc.scalar.copy, wv_dealt[:], wv_raw[:])
        late_woven = weave(2)
        outer = tile([P, LANES, HALF], F32, "outer")
        for r in range(LANES):
            k = LANES + r
            nc.scalar.activation(by_four(outer[:, r, :]), rw_rows(HALF, HALF), ACT.Copy, scale=neg_cw[:, k : k + 1])
        form_g(0, (slice(1, 2), slice(0, 1)))
        quantise_x(2, late_woven, "g_woven0")
        weigh_late = weigh(HALF, HALF, "late_weight")
        nc.gpsimd.tensor_tensor(late_weight[0][:, :, 1, :], span_labels(HALF, HALF, 1), outer[:], MULT)
        for o in (1, 0):
            score(1, o, 2 + o)
        sums0 = back(0, range(LANES), 6)
        release_on_scalar(0, sums0, {0: 0, 1: 1}, "dx0")
        squash(1, both)
        release_on_scalar(0, sums0, {2: 2}, "margin1")
        odd_dx = tile([P, 2, N], F32, "odd_dx")
        last_dx = odd_dx[:, 1, :]
        nc.scalar.copy(last_dx[:, group_cols(0)], sums0[:, 3, :])
        for o in (1, 0):
            score(2, o, 4 + o)
        for o in (1, 0):
            score(3, o, o)
        for b in (2, 3):
            squash(b, both)
        weigh_second = weigh(P, P, "weight0")
        for o in (1, 0):
            weigh_second(o)
        form_g(1, (both,))
        sums1 = back(1, range(LANES), 2)
        release_on_scalar(1, sums1, {1: 1}, "margin3")
        nc.scalar.copy(last_dx[:, group_cols(1)], sums1[:, 3, :])
        scalar_scatter(3, last_dx[:, :SPLIT], 0, SPLIT)
        even_dx = tile([P, 2, P], F32, "margin2")
        nc.scalar.copy(even_dx[:], sums1[:, 0:3:2, :])
        for k in range(2):
            scalar_scatter(2 * k, even_dx[:, k, :], P, P)
        weigh_late(0)
        form_g(2, (both,))
        late = {(2, odd): back(2, (odd, odd + 2), 3 + odd) for odd in (1, 0)}
        form_g(3, (both,))
        late.update({(3, odd): back(3, (odd, odd + 2), 5 + odd) for odd in (1, 0)})
        for b in (2, 3):
            nc.vector.tensor_copy(odd_dx[:, :, group_cols(b)], late[b, 1][:])
            vector_scatter(1, odd_dx[:, 0, group_cols(b)], P * b, P)
        vector_scatter(3, last_dx[:, SPLIT:], SPLIT, N - SPLIT)
        dx = tile([P, 2, HALF], F32, "late_dx0")
        for b in (2, 3):
            nc.scalar.copy(dx[:, :, group_cols(b - 2)], late[b, 0][:])
            scalar_scatter(0, dx[:, 0, group_cols(b - 2)], P * b, P)
        scalar_scatter(2, dx[:, 1, :], HALF, HALF)

        out_rows = out_0.rearrange("(p j) c -> p j c", j=LANES)

        def store_window(j):
            nc.sync.dma_start(out=out_rows[:, j, :], in_=windows[j][:])

        pairs_tile = sb.tile([P, LANES * T], BF16, name="pairs")
        pairs = pairs_tile[:].rearrange("p (k h c e) -> p k h c e", h=2, c=PIECE, e=2)
        for j in (1, 0, 3, 2):
            store_window(j)

        def round_lane(engine_copy, j, pieces):
            engine_copy(
                pairs[:, pieces, j // 2, :, j % 2], windows[j][:].rearrange("p (k c) -> p k c", c=PIECE)[:, pieces, :]
            )

        out_scale = sb.tile([P, T], U8, name="out_scale", align_bytes=64)
        out_words = out_1[0].rearrange("p c t -> p (c t)").bitcast(I32)
        woven_out = {}

        def join_pairs(engine_copy, word, k):
            woven_out[k] = sb.tile([P, PIECE, LANES], BF16, name=f"out_woven{k}", align_bytes=64)
            engine_copy(
                woven_out[k][:].bitcast(word),
                pairs_tile[:, LANES * PIECE * k : LANES * PIECE * (k + 1)].bitcast(word).rearrange("p (h c) -> p c h", h=2),
            )

        for j in (1, 0):
            round_lane(nc.vector.tensor_copy, j, slice(0, PIECES))
        for j in (3, 2):
            for k in range(PIECES - 1):
                round_lane(nc.vector.tensor_copy, j, slice(k, k + 1))
        for j in (3, 2):
            round_lane(nc.scalar.copy, j, slice(PIECES - 1, PIECES))
        for k in (0, 1):
            join_pairs(nc.vector.tensor_copy, I32, k)
        for k in (3, 2):
            join_pairs(nc.scalar.copy, U32, k)
        out_codes = sb.tile([P, T], U32, name="out_codes", align_bytes=64)
        for k in range(PIECES):
            cols = slice(PIECE * k, PIECE * (k + 1))
            nc.vector.quantize_mx(
                out=out_codes[:, cols].bitcast(E4M3),
                scales=out_scale[:, cols],
                in_=woven_out[k][:].rearrange("p c j -> p (c j)"),
            )
            if k > 0:
                done = slice(PIECE * k if k > 1 else 0, PIECE * (k + 1))
                nc.sync.dma_start(out=out_words[:, done], in_=out_codes[:, done].bitcast(I32))
        for q in range(QUADRANTS):
            queue = nc.scalar if q % 2 == 0 else nc.sync
            queue.dma_start(
                out=out_2[0, 4 * q : 4 * q + 4, :].bitcast(I32),
                in_=out_scale[32 * q : 32 * q + 4, :].bitcast(I32),
            )
